import numpy as np, ml_dtypes
CORES = [2,3,42,43,82,83,122,123]
N = 8
import mx_ref
BF = ml_dtypes.bfloat16
def entries(a):
    return np.ascontiguousarray(a.T).reshape(-1)
def table(e):
    return np.ascontiguousarray(np.reshape(e, (-1, 16)).T).astype(np.int32)
def cols(t, e):
    v = np.concatenate([t.reshape(128, -1, 4), np.zeros((128, 1, 4), BF)], axis=1)
    return np.ascontiguousarray(v[:, e]).reshape(128, -1)
def f(rng, *shape):
    return mx_ref.flush((rng.standard_normal(shape, dtype=np.float32) * np.exp2(rng.integers(-2, 3, shape[:-1] + (1,)))).astype(BF))
def wide(rng, *shape, cols=0):
    v = rng.standard_normal(shape, dtype=np.float32) * np.exp2(rng.integers(-12, 13, shape)).astype(np.float32)
    if cols: v *= np.repeat(np.exp2(rng.integers(-cols, cols + 1, shape[:-2] + (1, shape[-1] // 4))) * (rng.random(shape[:-2] + (1, shape[-1] // 4)) > 0.0625), 4, axis=-1).astype(np.float32)
    return mx_ref.flush(v.astype(BF))
T, O = 256, 4
CAP, ROOM = 288, 320
PAIR, MOVE, BOTH = 48, 16, 60
def turn(v, e):
    v = np.sort(v); return v[np.argsort((v // T - e) % N, kind="stable")]
def play(c1, c2):
    a, b = c1.reshape(-1), c2.reshape(-1)
    first = [turn(np.flatnonzero(a == e), e)[:CAP] for e in range(N)]
    refused = np.setdiff1d(np.arange(N * T), np.concatenate(first))
    second = [turn(refused[b[refused] == e], e)[:ROOM - len(first[e])] for e in range(N)]
    return first, second, refused
def broken(c1, c2):
    b = []
    if c1.min() < 0 or c1.max() >= N: return ["c1"]
    if c2.min() < 0 or c2.max() >= N: return ["c2"]
    if (c1 == c2).any(): b.append("a token with two equal choices")
    if max(np.bincount(v, minlength=N).max() for v in c1) > PAIR: b.append("first choices of a pair of ranks")
    first, second, refused = play(c1, c2)
    if np.bincount(c1.reshape(-1)[refused] * N + c2.reshape(-1)[refused], minlength=N * N).max() > MOVE: b.append("refused tokens of a pair of ranks")
    for e in range(N):
        if np.bincount(np.concatenate([first[e], second[e]]) // T, minlength=N).max() > BOTH: b.append("admitted tokens of a pair of ranks")
    return b
def fill(rng, low, high, total):
    n, p = np.array(low), rng.dirichlet(np.full(len(low), 16.0))
    while n.sum() < total: n = np.minimum(n + rng.multinomial(total - n.sum(), p), high)
    return n
def deal(rng, tot):
    n = np.stack([np.bincount(v, minlength=N) for v in rng.permutation(np.repeat(np.arange(N), tot)).reshape(N, T)])
    while n.max() > PAIR:
        s, e = np.argwhere(n > PAIR)[0]
        q = rng.choice(np.flatnonzero(n[:, e] < PAIR))
        g = rng.choice(np.flatnonzero(n[q] > n[s]))
        n[s, e] -= 1; n[q, e] += 1; n[q, g] -= 1; n[s, g] += 1
    return n
def bounds():
    return np.full(N, T >> 3), np.full(N, N * PAIR), np.zeros((N, N), int), MOVE * (1 - np.eye(N, dtype=int))
def lists(rng, low, high, mlow, mhigh, pair=None, skew=False, force=None):
    for _ in range(50):
        n = deal(rng, fill(rng, low, high, N * T))
        if pair or force:
            s, g, e = pair or (*force, force[1])
            for to in (g, e):
                while n[s, to] < PAIR:
                    h, q = [(h, q) for h in range(N) for q in range(N) if h not in (g, e) and n[s, h] > 0 and q != s and n[q, to] > 0 and n[q, h] < PAIR][0]
                    n[s, to] += 1; n[s, h] -= 1; n[q, to] -= 1; n[q, h] += 1
        c1 = np.concatenate([rng.permutation(np.repeat(np.arange(N), v)) for v in n])
        c2 = (c1 + rng.integers(1, N, N * T)) % N
        for e in range(N):
            at = turn(np.flatnonzero(c1 == e), e)[CAP:]
            c2[at] = rng.permutation(np.repeat(np.arange(N), fill(rng, mlow[e], mhigh[e], len(at))))
            if pair and e == pair[1]:
                mine = at[at // T == pair[0]]; named = c2[at]
                named = np.concatenate([named[named == pair[2]], named[named != pair[2]]]); k = int((named == pair[2]).sum())
                to = rng.permutation(mine)[:k]; c2[np.setdiff1d(at, to)] = named[k:]; c2[to] = pair[2]
        if skew:
            out = np.zeros(N * T, bool)
            for e in range(N): out[turn(np.flatnonzero(c1 == e), e)[CAP:]] = True
            for s in range(N):
                e = (s + rng.integers(3, N)) % N; k = np.arange(s * T, s * T + T)
                k = k[~out[k] & ((c1[k] - s - 1) % N < 2)]; c2[k] = e
        c1, c2 = c1.reshape(N, T), c2.reshape(N, T)
        if not broken(c1, c2): return {"c1": np.stack([table(v) for v in c1]), "c2": np.stack([table(v) for v in c2])}
    raise RuntimeError("no lists found")
def tiles(rng):
    return {"x": f(rng, N, 128, 4 * T), "w": f(rng, N, 128, 512 * O)}
def setup_inputs(rng):
    return {**tiles(rng), **lists(rng, *bounds())}
def setup_inputs_pair(rng):
    low, high, mlow, mhigh = bounds()
    p = rng.permutation(N); g, e, z = p[0], p[1], p[2]; s = (g - 1) % N
    if s in (e, z): e, z = [k for k in p if k not in (g, s)][:2]
    few = N - 2 - (N > 4)
    high[:] = CAP + (few - 1 + (N == 4)) * MOVE
    low[g] = high[g] = CAP + min(PAIR, BOTH - PAIR + few * MOVE); low[e] = N * PAIR >> 2; high[e] = CAP
    mhigh[:, e] = 0; mlow[g, e] = mhigh[g, e] = BOTH - PAIR
    if N > 4: low[z] = high[z] = 0; mhigh[:, z] = 0
    return {**tiles(rng), **lists(rng, low, high, mlow, mhigh, (int(s), int(g), int(e)))}
def setup_inputs_exact(rng):
    low, high, mlow, mhigh = bounds()
    p = rng.permutation(N); src = p[2:2 + (ROOM - CAP) // MOVE]
    high[:] = CAP
    low[p[0]] = CAP
    low[p[1]] = high[p[1]] = CAP + 1
    low[p[-1]] = N * PAIR >> 2
    mhigh[:, p[-1]] = np.minimum(mhigh[:, p[-1]], MOVE >> 1)
    low[src] = high[src] = N * PAIR
    mhigh[:, p[0]] = 0
    mlow[src, p[0]] = mhigh[src, p[0]] = MOVE
    return {**tiles(rng), **lists(rng, low, high, mlow, mhigh, skew=True, force=(int(p[-1] - 1) % N, int(p[-1])))}
def setup_inputs_full(rng):
    low, high, mlow, mhigh = bounds()
    p = rng.permutation(N); src = p[1:1 + 2 * ((ROOM - CAP) // MOVE)]
    low[p[0]] = CAP + 3 * MOVE // 2
    low[src] = CAP + MOVE
    mlow[src, p[0]] = MOVE
    return {**tiles(rng), **lists(rng, low, high, mlow, mhigh)}
def setup_inputs_room(rng):
    low, high, mlow, mhigh = bounds()
    p = rng.permutation(N); src = p[1:2 + (ROOM - CAP) // MOVE]
    low[p[0]] = high[p[0]] = CAP - 1
    low[src] = CAP + MOVE
    mlow[src, p[0]] = MOVE
    return {**tiles(rng), **lists(rng, low, high, mlow, mhigh)}
def setup_inputs_spread(rng):
    d = setup_inputs(rng); d["x"] = wide(rng, N, 128, 4 * T, cols=6); return d
def check_inputs(d):
    return broken(np.stack([entries(v) for v in d["c1"]]), np.stack([entries(v) for v in d["c2"]]))
def reference(x, w, c1, c2):
    first, second, _ = play(np.stack([entries(v) for v in c1]), np.stack([entries(v) for v in c2]))
    tokens = np.concatenate([x[r] for r in range(N)], axis=1)
    y = np.zeros((N, 128, O * ROOM), np.float32)
    for e in range(N):
        held = np.concatenate([first[e], second[e]])
        t = mx_ref.quantize(cols(tokens, np.concatenate([held, np.full(ROOM - len(held), -1)])))
        for o in range(O): y[e][:, ROOM * o:ROOM * o + ROOM] = mx_ref.matmul(mx_ref.quantize(w[e][:, 512 * o:512 * o + 512]), t)
    return {"y": y}

@@ -1,0 +1,402 @@
+from concourse.bass import DstId, RemoteDMATransfer
+from concourse.mybir import dt, AluOpType, AxisListType, ActivationFunctionType
+
+N, TOK, O, CAP, ROOM = 8, 256, 4, 288, 320
+SLOT = 64
+ZERO = N * SLOT
+NZ = 128
+WIN = 1344
+LATE = 400
+
+
+def _sb(n, d):
+    return ("sbuf", [128, n], d)
+
+
+F32, I32, U16, B16, MX, U8 = "float32", "int32", "uint16", "bfloat16", "float8_e4m3fn_x4", "uint8"
+SCRATCH = {
+    "lists": ("dram", [N, 128, 2], I32), "marks": ("dram", [N, 128, 2], F32),
+    "ct": _sb(32, I32), "xin": _sb(4 * TOK, B16), "win": _sb(512 * O, B16), "zin": _sb(4 * NZ, B16),
+    "xq": _sb(TOK, MX), "xs": _sb(TOK, U8), "wq": _sb(128 * O, MX), "wsc": _sb(128 * O, U8),
+    "pi": _sb(8, I32), "pb": _sb(8, I32), "pf": _sb(16, F32), "e64": _sb(64, I32), "ec": _sb(64, I32),
+    "l4": _sb(4, I32), "l4s": _sb(4, I32), "l64": _sb(4, U16), "c32": _sb(32, I32), "cz": _sb(32, I32), "ch": _sb(32, I32),
+    "meq": _sb(32, F32), "mlh": _sb(32, F32), "mlt": _sb(32, F32), "v128": _sb(128, I32), "vals": _sb(256, B16),
+    "c16": _sb(16, I32), "tr0": _sb(16, I32), "tr": _sb(16, I32), "ctr": _sb(16, I32), "j0": _sb(20, I32), "jj": _sb(20, F32),
+    "k64": _sb(8, I32), "ones": _sb(32, F32), "z64": _sb(64, F32),
+    "pre": _sb(256, B16), "mt": _sb(256, B16), "tcol": _sb(8, F32), "bc": _sb(96, F32), "tot": _sb(96, F32),
+    "p1": _sb(33, F32), "pn": _sb(32, F32), "pa": _sb(33, F32), "pq": _sb(33, F32), "p2": _sb(33, F32), "bcol": _sb(8, F32),
+    "sc1": _sb(64, F32), "d1": _sb(64, F32), "td1": _sb(64, F32), "cs1": _sb(72, F32), "s1": _sb(16, I32), "x1": _sb(16, I32),
+    "y1": _sb(16, I32), "y1b": _sb(16, I32), "off1": _sb(16, U16),
+    "sca": _sb(64, F32), "scb": _sb(64, F32), "qa": _sb(64, B16), "qb": _sb(64, B16), "wa": _sb(64, F32), "wb": _sb(64, F32),
+    "al": _sb(64, I32), "eqs": _sb(192, B16), "gcol": _sb(8, F32), "bg": _sb(64, F32), "tg": _sb(64, F32), "gs": _sb(8, F32),
+    "ru": _sb(64, B16), "rv": _sb(64, B16), "r2": _sb(64, B16), "b2": _sb(32, F32), "tot2": _sb(32, F32), "m16": _sb(16, F32), "m8": _sb(8, F32),
+    "sc2": _sb(64, F32), "d2": _sb(64, F32), "td2": _sb(64, F32), "cs2": _sb(72, F32), "s2": _sb(16, I32), "x2": _sb(16, I32), "v2": _sb(16, I32),
+    "y2": _sb(16, I32), "y2b": _sb(16, I32), "y2c": _sb(16, I32), "y2d": _sb(16, I32), "off2": _sb(16, U16),
+    "scat": _sb(WIN, B16), "tw": _sb(1024, B16), "self": _sb(32, F32), "so": _sb(32, U16),
+    "sq1": _sb(4 * SLOT, MX), "sp1": _sb(4 * SLOT, U8), "sq2": _sb(3 * SLOT, MX), "sp2": _sb(3 * SLOT, U8),
+    "land": _sb(ZERO + NZ, MX), "lsc": _sb(ZERO + NZ, U8),
+    "b3": _sb(32, F32), "t3": _sb(32, F32), "n16": _sb(16, F32), "n8": _sb(8, F32), "n8s": _sb(8, F32), "pp": _sb(24, F32), "bb": _sb(24, F32),
+    "de": _sb(24, F32), "dd": _sb(24, F32), "tm": _sb(320, F32), "t80": _sb(160, F32), "t40": _sb(80, F32), "t20": _sb(100, F32),
+    "ml": _sb(64, F32), "mb": _sb(64, F32), "fo": _sb(20, U16), "fq": _sb(ROOM, MX), "fs": _sb(ROOM, U8),
+    "acc": ("psum", [128, 512 * O], F32), "yo": _sb(ROOM * O, F32),
+}
+SEMAPHORES = ["cv", "cs", "cg", "ct", "dl0", "dc1", "dc2", "dx", "dw", "dal", "dm", "dml", "dy",
+              "lst", "lsts", "mar", "mars", "dat", "dats"]
+
+ADD, SUB, MUL, MIN = AluOpType.add, AluOpType.subtract, AluOpType.mult, AluOpType.min
+GE, LT, EQ = AluOpType.is_ge, AluOpType.is_lt, AluOpType.is_equal
+AND, SHR = AluOpType.bitwise_and, AluOpType.logical_shift_right
+COPY = ActivationFunctionType.Copy
+
+
+def plan(me, cores, topo):
+    core = cores[me]
+    dst = [cores[(me + 1 + z) % N] for z in range(N - 1)]
+    near = [z for z in range(N - 1) if topo.chip(dst[z]) == topo.chip(core)]
+    far = [z for z in range(N - 1) if z not in near]
+    run = far[-4:] if near[0] == 0 else far[:4]
+    rest = [z for z in range(N - 1) if z not in run]
+    out = topo.engines(core, dst[far[0]])
+    inn = [e for e in topo.engines(core, dst[near[0]]) if e not in out]
+    eng, one = {}, {}
+    for i, z in enumerate(run):
+        k = len(out) // len(run)
+        eng[z] = out[k * i:k * i + k]
+    fr = [z for z in rest if z in far]
+    for i, z in enumerate(fr):
+        k = len(out) // len(fr)
+        eng[z] = out[k * i:k * i + k]
+    for z in near:
+        eng[z] = inn
+        one[z] = inn[:1]
+    for i, z in enumerate(far):
+        one[z] = out[i:i + 1]
+    return run, rest, eng, one
+
+
+def rank_program(g, core, T, topo):
+    me = T.rank_of(core)
+    if me is None:
+        return
+    cores = [int(c) for c in T.cores]
+    run, rest, eng, one = plan(me, cores, topo)
+    queue = {"v": g.vector, "s": g.scalar, "t": g.tensor, "g": g, "y": g.sync}
+    cnt, seen, wr, rd = {}, {}, {}, {}
+
+    def need(q, tok):
+        sem, val = tok
+        if val is None:
+            val = cnt[sem]
+        if seen.get((q, sem), 0) < val:
+            queue[q].wait_ge(T.sem[sem], val)
+            seen[(q, sem)] = val
+
+    def before(q, reads, writes):
+        toks = {}
+        for k in reads:
+            for t in wr.get(k, []):
+                toks.setdefault(t[0], []).append(t)
+        for k in writes:
+            for t in wr.get(k, []) + rd.get(k, []):
+                toks.setdefault(t[0], []).append(t)
+        for sem in toks:
+            v = [t[1] for t in toks[sem]]
+            need(q, (sem, None if None in v else max(v)))
+
+    def after(tok, reads, writes, more):
+        for k in writes:
+            wr[k] = (wr.get(k, []) if more else []) + [tok]
+            if not more:
+                rd[k] = []
+        for k in reads:
+            rd.setdefault(k, []).append(tok)
+
+    def op(q, call, args, reads, writes, **kw):
+        before(q, reads, writes)
+        sem = "c" + q
+        call(*args, **kw).then_inc(T.sem[sem], 1)
+        cnt[sem] = cnt.get(sem, 0) + 1
+        after((sem, cnt[sem]), reads, writes, False)
+
+    def dma(q, sem, out, in_, reads, writes, more=False):
+        if not more:
+            before(q, reads, writes)
+        else:
+            before(q, reads, [])
+        queue[q].dma_start(out, in_).then_inc(T.sem[sem], 16)
+        cnt[sem] = cnt.get(sem, 0) + 16
+        after((sem, None), reads, writes, more)
+
+    V = g.vector
+
+    def ts(out, in0, s1, s2, op0, op1, reads, writes):
+        a = (out, in0, s1, s2, op0) if op1 is None else (out, in0, s1, s2, op0, op1)
+        op("v", V.tensor_scalar, a, reads, writes)
+
+    def tt(out, a, b, o, reads, writes):
+        op("v", V.tensor_tensor, (out, a, b, o), reads, writes)
+
+    def cp(out, a, reads, writes):
+        op("v", V.tensor_copy, (out, a), reads, writes)
+
+    def red(out, a, reads, writes):
+        op("v", V.tensor_reduce, (out, a, AxisListType.X, ADD), reads, writes)
+
+    def tr(out, a, reads, writes):
+        op("v", V.transpose, (out, a), reads, writes)
+
+    def scan(out, a, n, init, reads, writes):
+        op("v", V.tensor_tensor_scan, (out, a, T.z64[:, 0:n], init, ADD, ADD), reads + ["z64"], writes)
+
+    def fill(ap, val, key):
+        op("v", V.memset, (ap, val), [], [key])
+
+    def iota(name, n, pattern, base, chan=0):
+        op("g", g.iota, (T[name][:, 0:n], pattern, base, chan), [], [name])
+
+    def dest(z):
+        rid, pid, _ = topo.addr(cores[(me + 1 + z) % N])
+        return DstId(rid=rid, pnc=pid)
+
+    def mask(engines):
+        m = 0
+        for e in engines:
+            m |= 1 << e
+        return m
+
+    def send(zs, src, dst, engines, sem, lsem, reads):
+        before("g", reads, [])
+        g.remote_dma_fused([RemoteDMATransfer(dst_ids=[dest(z)], dma_engine_mask=mask(engines[z]), remote_sem=T.sem[sem],
+                                              src=src(z), dst=dst(z)) for z in zs], local_sem=T.sem[lsem])
+        cnt[lsem] = cnt.get(lsem, 0) + sum(len(engines[z]) for z in zs)
+
+    others = list(range(N - 1))
+    data_in = list_in = 0
+    for k in range(1, N):
+        _, _, e2, o2 = plan((me + k) % N, cores, topo)
+        data_in += 2 * len(e2[N - 1 - k])
+        list_in += len(o2[N - 1 - k])
+
+    dma("y", "dl0", T.lists[0], T.c1[:, :], [], ["l0"])
+    for b in range(8):
+        dma("ys"[b % 2], "dc1", T.ct[16 * b:16 * b + 16, 0:16], T.c1[:, :], [], ["c1"], more=True)
+    for b in range(8):
+        dma("sy"[b % 2], "dc2", T.ct[16 * b:16 * b + 16, 16:32], T.c2[:, :], [], ["c2"], more=True)
+    dma("y", "dx", T.xin[:, :], T.x[:, :], [], ["xin"])
+    dma("s", "dw", T["win"][:, :], T.w[:, :], [], ["win"])
+
+    iota("pi", 1, [[0, 1]], 0, 1)
+    iota("l4", 4, [[2, 2], [8, 2]], 0)
+    iota("e64", 64, [[1, 64]], me + 1)
+    iota("c32", 32, [[1, 32]], 0)
+    iota("v128", 128, [[32, 2], [64, 4], [1, 16]], 0)
+    iota("c16", 16, [[16, 2], [0, 8]], 0)
+    send(others, lambda z: T.lists[0], lambda z: T.lists[N - 1 - z], one, "lst", "lsts", ["l0"])
+    iota("tr0", 16, [[16, 16]], 1088)
+    iota("j0", 20, [[16, 20]], 0)
+    iota("k64", 8, [[SLOT, 8]], 0)
+
+    fill(T.ones[:, :], 1.0, "ones")
+    fill(T.z64[:, :], 0.0, "z64")
+    fill(T.cs1[:, 0:8], 0.0, "cs1z")
+    fill(T.cs2[:, 0:8], 0.0, "cs2z")
+    fill(T.pa[:, 32:33], float(LATE), "paz")
+    fill(T.pq[:, 32:33], float(LATE), "pqz")
+    fill(T.pp[:, 0:1], 0.0, "pp0")
+    fill(T.bb[:, 16:17], float(ZERO), "bb16")
+    pb, pf = T.pb, T.pf
+    pi = T.pi[:, 0:1]
+    for j, (a, b, o1, o2) in enumerate([(7, None, AND, None), (3, 3, SHR, AND), (15, None, AND, None), (2, 7, SHR, AND),
+                                        (8, 1, AND, SHR), (16, 4, AND, SHR), (16, None, AND, None)]):
+        ts(pb[:, j:j + 1], pi, a, b, o1, o2, ["pi"], ["pb%d" % j])
+    cp(pf[:, 0:7], pb[:, 0:7], ["pb%d" % j for j in range(7)], ["pf"])
+    zc, hc, ic, kc = [pf[:, j:j + 1] for j in range(4)]
+    tt(pf[:, 7:8], pf[:, 4:5], pf[:, 5:6], ADD, ["pf"], ["pc"])
+    ts(T.l64[:, :], T.l4[:, :], pf[:, 7:8], None, ADD, None, ["l4", "pc"], ["l64"])
+    ts(T.ec[:, :], T.e64[:, :], 7, None, AND, None, ["e64"], ["ec"])
+    ts(T.p1[:, 32:33], zc, 128.0, 63.0, MUL, ADD, ["pf"], ["p1z"])
+    ts(T.cz[:, :], T.c32[:, :], 7, None, AND, None, ["c32"], ["cz"])
+    ts(T.ch[:, :], T.c32[:, :], 3, None, SHR, None, ["c32"], ["ch"])
+    ts(T.meq[:, :], T.cz[:, :], zc, None, EQ, None, ["cz", "pf"], ["meq"])
+    ts(T.mlh[:, :], T.ch[:, :], hc, None, LT, None, ["ch", "pf"], ["mlh"])
+    tt(T.mlt[:, :], T.meq[:, :], T.mlh[:, :], MUL, ["meq", "mlh"], ["mlt"])
+    ts(pf[:, 8:9], kc, 1.0, -50.0, LT, MUL, ["pf"], ["g1a"])
+    ts(pf[:, 9:10], kc, 2.0, -50.0, LT, MUL, ["pf"], ["g2a"])
+    ts(pf[:, 10:11], pf[:, 8:9], float((me + 1) % N), None, ADD, None, ["g1a"], ["g1"])
+    ts(pf[:, 11:12], pf[:, 9:10], float((me + 2) % N), None, ADD, None, ["g2a"], ["g2"])
+
+    l64 = T.l64[:, 0:4]
+    c1w, c2w = T.ct[:, 0:16].indirect(l64), T.ct[:, 16:32].indirect(l64)
+    tt(T.pre[:, 0:64], c1w, T.ec[:, :], EQ, ["c1", "l64", "ec"], ["pre0"])
+    ts(T.pre[:, 128:192], c1w, float((me + 1) % N), None, EQ, None, ["c1", "l64"], ["pre2"])
+    ts(T.pre[:, 192:256], c1w, float((me + 2) % N), None, EQ, None, ["c1", "l64"], ["pre3"])
+    tt(T.pre[:, 64:128], c2w, T.ec[:, :], EQ, ["c2", "l64", "ec"], ["pre1"])
+    tr(T.mt[:, :], T.pre[:, :], ["pre0", "pre1", "pre2", "pre3"], ["mt"])
+    m1, mc, ma, mb = [T.mt[:, 64 * i:64 * i + 64] for i in range(4)]
+    for i, m in enumerate((m1, ma, mb)):
+        red(T.tcol[:, i:i + 1], m, ["mt"], ["tcol%d" % i])
+    for i in range(3):
+        ts(T.bc[:, 32 * i:32 * i + 32], T.ones[:, :], T.tcol[:, i:i + 1], None, MUL, None, ["ones", "tcol%d" % i], ["bc%d" % i])
+    tr(T.tot[:, :], T.bc[:, :], ["bc0", "bc1", "bc2"], ["tot"])
+    tt(T.p1[:, 0:32], T.tot[:, 0:32], T.mlt[:, :], MUL, ["tot", "mlt"], ["p1"])
+    tt(T.pn[:, :], T.tot[:, 0:32], T.meq[:, :], MUL, ["tot", "meq"], ["pn"])
+    tt(T.pa[:, 0:32], T.tot[:, 32:64], T.mlt[:, :], MUL, ["tot", "mlt"], ["pa"])
+    tt(T.pq[:, 0:32], T.tot[:, 64:96], T.mlt[:, :], MUL, ["tot", "mlt"], ["pq"])
+    bcol = T.bcol
+    red(bcol[:, 0:1], T.p1[:, :], ["p1", "p1z"], ["b1"])
+    red(bcol[:, 2:3], T.pa[:, :], ["pa", "paz"], ["ba"])
+    red(bcol[:, 3:4], T.pq[:, :], ["pq", "pqz"], ["bq"])
+    red(bcol[:, 1:2], T.pn[:, :], ["pn"], ["bn"])
+    scan(T.sc1[:, :], m1, 64, bcol[:, 0:1], ["mt", "b1"], ["sc1"])
+    scan(T.sca[:, :], ma, 64, bcol[:, 2:3], ["mt", "ba"], ["sca"])
+    scan(T.scb[:, :], mb, 64, bcol[:, 3:4], ["mt", "bq"], ["scb"])
+    tt(T.d1[:, :], m1, T.sc1[:, :], MUL, ["mt", "sc1"], ["d1"])
+    tt(T.qa[:, :], ma, mc, MUL, ["mt"], ["qa"])
+    tt(T.qb[:, :], mb, mc, MUL, ["mt"], ["qb"])
+    tr(T.td1[:, :], T.d1[:, :], ["d1"], ["td1"])
+    tt(T.wa[:, :], T.qa[:, :], T.sca[:, :], MUL, ["qa", "sca"], ["wa"])
+    tt(T.wb[:, :], T.qb[:, :], T.scb[:, :], MUL, ["qb", "scb"], ["wb"])
+    tt(T.p2[:, 32:33], bcol[:, 1:2], T.p1[:, 32:33], ADD, ["bn", "p1z"], ["p2z"])
+    scan(T.cs1[:, 8:72], T.td1[:, :], 64, 0.0, ["td1"], ["cs1"])
+    fill(T.scat[:, :], 0.0, "scat")
+    ts(T.vals[:, 0:128], T.v128[:, :], pf[:, 6:7], None, ADD, None, ["v128", "pf"], ["va0"])
+    ts(T.vals[:, 128:256], T.v128[:, :], pf[:, 6:7], None, ADD, None, ["v128", "pf"], ["va1"])
+    for i in range(2):
+        tt(T.s1[:, 8 * i:8 * i + 8], T.cs1[:, 15:72:8], T.cs1[:, 7:64:8], SUB, ["cs1", "cs1z"], ["s1%d" % i])
+    ts(T.x1[:, :], T.s1[:, :], 48, None, AND, None, ["s10", "s11"], ["x1"])
+    tt(T.y1[:, :], T.s1[:, :], T.c16[:, :], ADD, ["s10", "s11", "c16"], ["y1"])
+    tt(T.y1b[:, :], T.y1[:, :], T.x1[:, :], ADD, ["x1", "y1"], ["y1b"])
+    cp(T.off1[:, :], T.y1b[:, :], ["y1b"], ["off1"])
+    cp(T.scat[:, 0:WIN].indirect(T.off1[:, 0:16]), T.vals[:, :], ["off1", "va0", "va1"], ["scat"])
+    op("v", V.quantize_mx, (T.xq[:, :], T.xs[:, :], T.xin[:, :]), ["xin"], ["xq"])
+    ts(T.tr[:, :], T.tr0[:, :], ic, None, ADD, None, ["tr0", "pf"], ["tr"])
+    tt(T.ctr[:, :], T.c16[:, :], T.tr[:, :], SUB, ["c16", "tr"], ["ctr"])
+
+    cnt["lst"] = list_in
+    wr["lx"] = [("lst", list_in)]
+    for b in range(4):
+        dma("ys"[b % 2], "dal", T.al[32 * b:32 * b + 32, 0:64], T.lists[:, :, :], ["lx", "l0"], ["al"], more=True)
+    eqs, gcol = T.eqs, T.gcol
+    for i in range(2):
+        ts(eqs[:, 64 * i:64 * i + 64], T.al[:, :], pf[:, 10 + i:11 + i], None, EQ, None, ["al", "g%d" % (i + 1)], ["eq%d" % i])
+    for i in range(2):
+        red(gcol[:, i:i + 1], eqs[:, 64 * i:64 * i + 64], ["eq%d" % i], ["gc%d" % i])
+    for i in range(2):
+        ts(T.bg[:, 32 * i:32 * i + 32], T.ones[:, :], gcol[:, i:i + 1], None, MUL, None, ["ones", "gc%d" % i], ["bg%d" % i])
+    tr(T.tg[:, :], T.bg[:, :], ["bg0", "bg1"], ["tg"])
+    for i in range(2):
+        red(T.gs[:, i:i + 1], T.tg[:, 32 * i:32 * i + 32], ["tg"], ["gs%d" % i])
+    lim = float(LATE + CAP + 1)
+    ts(T.ru[:, :], T.wa[:, :], T.gs[:, 0:1], lim, ADD, GE, ["wa", "gs0"], ["ru"])
+    ts(T.rv[:, :], T.wb[:, :], T.gs[:, 1:2], lim, ADD, GE, ["wb", "gs1"], ["rv"])
+    tt(T.r2[:, :], T.ru[:, :], T.rv[:, :], ADD, ["ru", "rv"], ["r2"])
+    red(T.tcol[:, 4:5], T.r2[:, :], ["r2"], ["tcol4"])
+    ts(T.b2[:, :], T.ones[:, :], T.tcol[:, 4:5], None, MUL, None, ["ones", "tcol4"], ["b2"])
+    tr(T.tot2[:, :], T.b2[:, :], ["b2"], ["tot2"])
+    tt(T.p2[:, 0:32], T.tot2[:, :], T.mlt[:, :], MUL, ["tot2", "mlt"], ["p2"])
+    tt(T.m16[:, :], T.tot2[:, 0:16], T.tot2[:, 16:32], ADD, ["tot2"], ["m16"])
+    red(bcol[:, 4:5], T.p2[:, :], ["p2", "p2z"], ["b2c"])
+    tt(T.m8[:, :], T.m16[:, 0:8], T.m16[:, 8:16], ADD, ["m16"], ["m8"])
+    dma("y", "dm", T.marks[0], T.m8[0:32, 0:8], ["m8"], ["mk0"])
+    scan(T.sc2[:, :], T.r2[:, :], 64, bcol[:, 4:5], ["r2", "b2c"], ["sc2"])
+    tt(T.d2[:, :], T.r2[:, :], T.sc2[:, :], MUL, ["r2", "sc2"], ["d2"])
+    tr(T.td2[:, :], T.d2[:, :], ["d2"], ["td2"])
+    scan(T.cs2[:, 8:72], T.td2[:, :], 64, 0.0, ["td2"], ["cs2"])
+    for i in range(2):
+        tt(T.s2[:, 8 * i:8 * i + 8], T.cs2[:, 15:72:8], T.cs2[:, 7:64:8], SUB, ["cs2", "cs2z"], ["s2%d" % i])
+    ts(T.x2[:, :], T.s2[:, :], 48, None, AND, None, ["s20", "s21"], ["x2"])
+    ts(T.v2[:, :], T.s2[:, :], 64, 6, AND, SHR, ["s20", "s21"], ["v2"])
+    tt(T.y2[:, :], T.s2[:, :], T.ctr[:, :], ADD, ["s20", "s21", "ctr"], ["y2"])
+    tt(T.y2b[:, :], T.y2[:, :], T.x2[:, :], ADD, ["x2", "y2"], ["y2b"])
+    tt(T.y2c[:, :], T.y2b[:, :], T.v2[:, :], MUL, ["y2b", "v2"], ["y2c"])
+    tt(T.y2d[:, :], T.y2c[:, :], T.tr[:, :], ADD, ["y2c", "tr"], ["y2d"])
+    cp(T.off2[:, :], T.y2d[:, :], ["y2d"], ["off2"])
+    cp(T.scat[:, 0:WIN].indirect(T.off2[:, 0:16]), T.vals[:, :], ["off2", "va0", "va1"], ["scat"])
+
+    send(others, lambda z: T.marks[0], lambda z: T.marks[N - 1 - z], one, "mar", "mars", ["mk0"])
+
+    def lists_of(za, zb):
+        key = "so%d" % za
+        tr(T.tw[:, 128 * za:128 * zb], T.scat[:, 64 + 128 * za:64 + 128 * zb], ["scat"], ["tw%d" % za])
+        tt(T["self"][:, 4 * za:4 * zb], T.tw[:, 128 * za:128 * zb:32], T.tw[:, 128 * za + 16:128 * zb:32], ADD, ["tw%d" % za], ["sf%d" % za])
+        cp(T.so[:, 4 * za:4 * zb], T["self"][:, 4 * za:4 * zb], ["sf%d" % za], [key])
+        return key
+
+    def pick(oq, os_, n, iq, is_, m, off, n0, reads, writes):
+        op("v", V.tensor_copy, (oq[:, n0:n0 + n].bitcast(dt.uint32), iq[:, 0:m].bitcast(dt.uint32).indirect(off)), reads, [writes + "q"])
+        op("s", g.scalar.activation, (os_[:, n0:n0 + n], is_[:, 0:m].indirect(off), COPY), reads, [writes + "s"])
+
+    def column_sends(zs, sq, sp, key):
+        z0 = zs[0]
+        send(zs, lambda z: sq[:, SLOT * (z - z0):SLOT * (z - z0 + 1)].bitcast(dt.uint8),
+             lambda z: T.land[:, SLOT * (N - 1 - z):SLOT * (N - z)].bitcast(dt.uint8), eng, "dat", "dats", [key + "q"])
+        send(zs, lambda z: sp[:, SLOT * (z - z0):SLOT * (z - z0 + 1)],
+             lambda z: T.lsc[:, SLOT * (N - 1 - z):SLOT * (N - z)], eng, "dat", "dats", [key + "s"])
+
+    for zs, sq, sp, key in ((run, T.sq1, T.sp1, "w1"), (rest, T.sq2, T.sp2, "w2")):
+        za, zb = zs[0], zs[-1] + 1
+        k = lists_of(za, zb)
+        pick(sq, sp, SLOT * (zb - za), T.xq, T.xs, TOK, T.so[:, 4 * za:4 * zb], 0, [k, "xq"], key)
+        column_sends(zs, sq, sp, key)
+    k = lists_of(N - 1, N)
+    pick(T.land, T.lsc, SLOT, T.xq, T.xs, TOK, T.so[:, 4 * (N - 1):4 * N], 0, [k, "xq"], "own")
+
+    ts(eqs[:, 128:192], T.al[:, :], float(me), None, EQ, None, ["al"], ["eq2"])
+    red(gcol[:, 2:3], eqs[:, 128:192], ["eq2"], ["gc2"])
+    ts(T.b3[:, :], T.ones[:, :], gcol[:, 2:3], None, MUL, None, ["ones", "gc2"], ["b3"])
+    tr(T.t3[:, :], T.b3[:, :], ["b3"], ["t3"])
+    tt(T.n16[:, :], T.t3[:, 0:32:2], T.t3[:, 1:32:2], ADD, ["t3"], ["n16"])
+    tt(T.n8[:, :], T.n16[:, 0:16:2], T.n16[:, 1:16:2], ADD, ["n16"], ["n8"])
+    scan(T.n8s[:, :], T.n8[:, :], 8, 0.0, ["n8"], ["n8s"])
+    pp, bb = T.pp, T.bb
+    ts(pp[:, 1:9], T.n8s[:, :], float(CAP), None, MIN, None, ["n8s"], ["pp1"])
+    cp(bb[:, 0:8], T.k64[:, :], ["k64"], ["bb0"])
+    tt(bb[:, 8:16], T.k64[:, :], T.n8[:, :], ADD, ["k64", "n8"], ["bb8"])
+    ts(T.jj[:, :], T.j0[:, :], ic, None, ADD, None, ["j0", "pf"], ["jj"])
+
+    def terms(lo):
+        a, b = 80 * (lo // 8), 40 * (lo // 8)
+        for q in range(lo + 1, lo + 9):
+            ts(T.tm[:, 20 * (q - 1):20 * q], T.jj[:, :], pp[:, q:q + 1], T.dd[:, q - 1:q], GE, MUL, ["jj", "pp1", "pp9", "dd%d" % lo], ["tm%d" % q])
+        c = 20 * lo
+        tt(T.t80[:, a:a + 80], T.tm[:, c:c + 80], T.tm[:, c + 80:c + 160], ADD, ["tm%d" % q for q in range(lo + 1, lo + 9)], ["t80%d" % lo])
+        tt(T.t40[:, b:b + 40], T.t80[:, a:a + 40], T.t80[:, a + 40:a + 80], ADD, ["t80%d" % lo], ["t40%d" % lo])
+        d = 40 * (lo // 8)
+        tt(T.t20[:, d:d + 20], T.t40[:, b:b + 20], T.t40[:, b + 20:b + 40], ADD, ["t40%d" % lo], ["t20%d" % lo])
+        x, key = (T.jj[:, :], "jj") if lo == 0 else (T.t20[:, 20:40], "sum0")
+        tt(T.t20[:, d + 20:d + 40], T.t20[:, d:d + 20], x, ADD, ["t20%d" % lo, key], ["sum%d" % lo])
+
+    tt(T.de[:, 0:9], bb[:, 0:9], pp[:, 0:9], SUB, ["bb0", "bb8", "pp0", "pp1"], ["de0"])
+    tt(T.dd[:, 0:8], T.de[:, 1:9], T.de[:, 0:8], SUB, ["de0"], ["dd0"])
+    terms(0)
+    op("v", V.quantize_mx, (T.wq[:, :], T.wsc[:, :], T["win"][:, :]), ["win"], ["wq"])
+    fill(T.zin[:, :], 0.0, "zin")
+    op("v", V.quantize_mx, (T.land[:, ZERO:ZERO + NZ], T.lsc[:, ZERO:ZERO + NZ], T.zin[:, :]), ["zin"], ["zq"])
+
+    cnt["mar"] = list_in
+    wr["mx"] = [("mar", list_in)]
+    dma("y", "dml", T.ml[0:1, 0:64], T.marks[:, 0:4, :], ["mx", "mk0"], ["ml"])
+    op("g", g.partition_broadcast, (T.mb[:, 0:64], T.ml[0:1, 0:64], 128), ["ml"], ["mb"])
+    scan(pp[:, 9:17], T.mb[:, 7:57:7], 8, pp[:, 8:9], ["mb", "pp1"], ["pp9"])
+    tt(T.de[:, 9:17], bb[:, 9:17], pp[:, 9:17], SUB, ["bb8", "bb16", "pp9"], ["de9"])
+    tt(T.dd[:, 8:16], T.de[:, 9:17], T.de[:, 8:16], SUB, ["de9", "de0"], ["dd8"])
+    terms(8)
+    ts(T.fo[:, :], T.t20[:, 60:80], float(ZERO + NZ - 1), None, MIN, None, ["sum8"], ["fo"])
+
+    cnt["dat"] = data_in
+    wr["dx"] = [("dat", data_in)]
+    got = ["dx", "ownq", "owns", "zq", "fo"]
+    pick(T.fq, T.fs, ROOM, T.land, T.lsc, ZERO + NZ, T.fo[:, 0:20], 0, got, "f")
+    for o in range(O):
+        a = T.acc[:, 512 * o:512 * o + ROOM]
+        op("t", g.tensor.matmul_mx, (a, T.wq[:, 128 * o:128 * o + 128], T.wsc[:, 128 * o:128 * o + 128], T.fq[:, 0:ROOM], T.fs[:, 0:ROOM], True, True),
+           ["wq", "fq", "fs"], ["acc%d" % o])
+    for o in range(O):
+        a, y = T.acc[:, 512 * o:512 * o + ROOM], T.yo[:, ROOM * o:ROOM * o + ROOM]
+        if o % 2 == 0:
+            cp(y, a, ["acc%d" % o], ["yo%d" % o])
+        else:
+            op("s", g.scalar.activation, (y, a, COPY), ["acc%d" % o], ["yo%d" % o])
+        dma("y", "dy", T.y[:, ROOM * o:ROOM * o + ROOM], y, ["yo%d" % o], ["yout"], more=True)
+    for sem in sorted(cnt):
+        need("y", (sem, None))

@@ -1,11 +1,11 @@
 from concourse.bass import DstId, RemoteDMATransfer
 from concourse.mybir import dt, AluOpType, AxisListType, ActivationFunctionType
 
-N, TOK, O, CAP, ROOM = 8, 256, 4, 288, 320
+N, TOK, O, CAP, ROOM, BOTH = 8, 256, 4, 288, 320, 60
 SLOT = 64
 ZERO = N * SLOT
 NZ = 128
-WIN = 1344
+WIN = 1088
 LATE = 400
 
 
@@ -15,38 +15,38 @@ def _sb(n, d):
 
 F32, I32, U16, B16, MX, U8 = "float32", "int32", "uint16", "bfloat16", "float8_e4m3fn_x4", "uint8"
 SCRATCH = {
-    "lists": ("dram", [N, 128, 2], I32), "marks": ("dram", [N, 128, 2], F32),
+    "lists": ("dram", [N, 128, 2], I32),
     "ct": _sb(32, I32), "xin": _sb(4 * TOK, B16), "win": _sb(512 * O, B16), "zin": _sb(4 * NZ, B16),
     "xq": _sb(TOK, MX), "xs": _sb(TOK, U8), "wq": _sb(128 * O, MX), "wsc": _sb(128 * O, U8),
     "pi": _sb(8, I32), "pb": _sb(8, I32), "pf": _sb(16, F32), "e64": _sb(64, I32), "ec": _sb(64, I32),
-    "l4": _sb(4, I32), "l4s": _sb(4, I32), "l64": _sb(4, U16), "c32": _sb(32, I32), "cz": _sb(32, I32), "ch": _sb(32, I32),
-    "meq": _sb(32, F32), "mlh": _sb(32, F32), "mlt": _sb(32, F32), "v128": _sb(128, I32), "vals": _sb(256, B16),
-    "c16": _sb(16, I32), "tr0": _sb(16, I32), "tr": _sb(16, I32), "ctr": _sb(16, I32), "j0": _sb(20, I32), "jj": _sb(20, F32),
+    "l4": _sb(4, I32), "l64": _sb(4, U16), "c32": _sb(32, I32), "cz": _sb(32, I32), "ch": _sb(32, I32),
+    "meq": _sb(32, F32), "mlh": _sb(32, F32), "mlt": _sb(32, F32), "v128": _sb(128, B16), "vals": _sb(256, B16),
+    "c16": _sb(16, I32), "j0": _sb(20, I32), "jj": _sb(20, F32),
     "k64": _sb(8, I32), "ones": _sb(32, F32), "z64": _sb(64, F32),
     "pre": _sb(256, B16), "mt": _sb(256, B16), "tcol": _sb(8, F32), "bc": _sb(96, F32), "tot": _sb(96, F32),
     "p1": _sb(33, F32), "pn": _sb(32, F32), "pa": _sb(33, F32), "pq": _sb(33, F32), "p2": _sb(33, F32), "bcol": _sb(8, F32),
     "sc1": _sb(64, F32), "d1": _sb(64, F32), "td1": _sb(64, F32), "cs1": _sb(72, F32), "s1": _sb(16, I32), "x1": _sb(16, I32),
-    "y1": _sb(16, I32), "y1b": _sb(16, I32), "off1": _sb(16, U16),
+    "y1": _sb(16, I32), "y1b": _sb(16, I32), "cy": _sb(16, I32),
     "sca": _sb(64, F32), "scb": _sb(64, F32), "qa": _sb(64, B16), "qb": _sb(64, B16), "wa": _sb(64, F32), "wb": _sb(64, F32),
     "al": _sb(64, I32), "eqs": _sb(192, B16), "gcol": _sb(8, F32), "bg": _sb(64, F32), "tg": _sb(64, F32), "gs": _sb(8, F32),
     "ru": _sb(64, B16), "rv": _sb(64, B16), "r2": _sb(64, B16), "b2": _sb(32, F32), "tot2": _sb(32, F32), "m16": _sb(16, F32), "m8": _sb(8, F32),
     "sc2": _sb(64, F32), "d2": _sb(64, F32), "td2": _sb(64, F32), "cs2": _sb(72, F32), "s2": _sb(16, I32), "x2": _sb(16, I32), "v2": _sb(16, I32),
     "y2": _sb(16, I32), "y2b": _sb(16, I32), "y2c": _sb(16, I32), "y2d": _sb(16, I32), "off2": _sb(16, U16),
     "scat": _sb(WIN, B16), "tw": _sb(1024, B16), "self": _sb(32, F32), "so": _sb(32, U16),
-    "sq1": _sb(4 * SLOT, MX), "sp1": _sb(4 * SLOT, U8), "sq2": _sb(3 * SLOT, MX), "sp2": _sb(3 * SLOT, U8),
+    "sq1": _sb(3 * SLOT, MX), "sp1": _sb(3 * SLOT, U8), "sq2": _sb(4 * SLOT, MX), "sp2": _sb(4 * SLOT, U8),
     "land": _sb(ZERO + NZ, MX), "lsc": _sb(ZERO + NZ, U8),
     "b3": _sb(32, F32), "t3": _sb(32, F32), "n16": _sb(16, F32), "n8": _sb(8, F32), "n8s": _sb(8, F32), "pp": _sb(24, F32), "bb": _sb(24, F32),
     "de": _sb(24, F32), "dd": _sb(24, F32), "tm": _sb(320, F32), "t80": _sb(160, F32), "t40": _sb(80, F32), "t20": _sb(100, F32),
-    "ml": _sb(64, F32), "mb": _sb(64, F32), "fo": _sb(20, U16), "fq": _sb(ROOM, MX), "fs": _sb(ROOM, U8),
-    "acc": ("psum", [128, 512 * O], F32), "yo": _sb(ROOM * O, F32),
+    "ml": _sb(8, F32), "mf": _sb(8, F32), "mp": _sb(8, F32), "m9": _sb(8, F32), "fo": _sb(20, U16), "fq": _sb(ROOM, MX), "fs": _sb(ROOM, U8),
+    "acc": ("psum", [128, 512 * (O + 1)], F32), "yo": _sb(ROOM * O, F32),
 }
-SEMAPHORES = ["cv", "cs", "cg", "ct", "dl0", "dc1", "dc2", "dx", "dw", "dal", "dm", "dml", "dy",
-              "lst", "lsts", "mar", "mars", "dat", "dats"]
+SEMAPHORES = ["cv", "cs", "cg", "ct", "dl0", "dc1", "dc2", "dx", "dw", "dal", "dy",
+              "lst", "lsts", "mar", "mars", "mfw", "dat", "dats"]
 
 ADD, SUB, MUL, MIN = AluOpType.add, AluOpType.subtract, AluOpType.mult, AluOpType.min
 GE, LT, EQ = AluOpType.is_ge, AluOpType.is_lt, AluOpType.is_equal
 AND, SHR = AluOpType.bitwise_and, AluOpType.logical_shift_right
-COPY = ActivationFunctionType.Copy
+COPY, IDENT = ActivationFunctionType.Copy, ActivationFunctionType.Identity
 
 
 def plan(me, cores, topo):
@@ -54,24 +54,25 @@ def plan(me, cores, topo):
     dst = [cores[(me + 1 + z) % N] for z in range(N - 1)]
     near = [z for z in range(N - 1) if topo.chip(dst[z]) == topo.chip(core)]
     far = [z for z in range(N - 1) if z not in near]
-    run = far[-4:] if near[0] == 0 else far[:4]
-    rest = [z for z in range(N - 1) if z not in run]
     out = topo.engines(core, dst[far[0]])
     inn = [e for e in topo.engines(core, dst[near[0]]) if e not in out]
-    eng, one = {}, {}
-    for i, z in enumerate(run):
-        k = len(out) // len(run)
-        eng[z] = out[k * i:k * i + k]
-    fr = [z for z in rest if z in far]
-    for i, z in enumerate(fr):
-        k = len(out) // len(fr)
-        eng[z] = out[k * i:k * i + k]
-    for z in near:
-        eng[z] = inn
-        one[z] = inn[:1]
-    for i, z in enumerate(far):
-        one[z] = out[i:i + 1]
-    return run, rest, eng, one
+
+    def deal(zs):
+        k = len(out) // len(zs)
+        return {z: out[k * i:k * i + k] for i, z in enumerate(zs)}
+
+    some = far[:2] if near[0] == 0 else far[-2:]
+    rest = [z for z in far if z not in some]
+    some_e = deal(some)
+    some_e.update({z: inn for z in near})
+    some = sorted(some + near)
+    calls = []
+    for zs, e in ((some, some_e), (rest, deal(rest))):
+        n = SLOT if 0 in zs or 1 in zs else BOTH
+        calls += [("q", zs, n, e), ("s", zs, n, e)]
+    single = {z: out[i:i + 1] for i, z in enumerate(far)}
+    single.update({z: inn[:1] for z in near})
+    return near[0], calls, single, inn
 
 
 def rank_program(g, core, T, topo):
@@ -79,7 +80,7 @@ def rank_program(g, core, T, topo):
     if me is None:
         return
     cores = [int(c) for c in T.cores]
-    run, rest, eng, one = plan(me, cores, topo)
+    near, calls, one, inn = plan(me, cores, topo)
     queue = {"v": g.vector, "s": g.scalar, "t": g.tensor, "g": g, "y": g.sync}
     cnt, seen, wr, rd = {}, {}, {}, {}
 
@@ -151,11 +152,12 @@ def rank_program(g, core, T, topo):
     def fill(ap, val, key):
         op("v", V.memset, (ap, val), [], [key])
 
-    def iota(name, n, pattern, base, chan=0):
-        op("g", g.iota, (T[name][:, 0:n], pattern, base, chan), [], [name])
+    def iota(name, n, pattern, base, chan=0, flag=False):
+        kw = {"allow_small_or_imprecise_dtypes": True} if flag else {}
+        op("g", g.iota, (T[name][:, 0:n], pattern, base, chan), [], [name], **kw)
 
-    def dest(z):
-        rid, pid, _ = topo.addr(cores[(me + 1 + z) % N])
+    def at(r):
+        rid, pid, _ = topo.addr(cores[r])
         return DstId(rid=rid, pnc=pid)
 
     def mask(engines):
@@ -164,17 +166,23 @@ def rank_program(g, core, T, topo):
             m |= 1 << e
         return m
 
-    def send(zs, src, dst, engines, sem, lsem, reads):
+    def fused(moves, sem, lsem, reads):
         before("g", reads, [])
-        g.remote_dma_fused([RemoteDMATransfer(dst_ids=[dest(z)], dma_engine_mask=mask(engines[z]), remote_sem=T.sem[sem],
-                                              src=src(z), dst=dst(z)) for z in zs], local_sem=T.sem[lsem])
-        cnt[lsem] = cnt.get(lsem, 0) + sum(len(engines[z]) for z in zs)
+        g.remote_dma_fused([RemoteDMATransfer(dst_ids=[at(r)], dma_engine_mask=mask(w), remote_sem=T.sem[sem], src=a, dst=b)
+                            for r, w, a, b in moves], local_sem=T.sem[lsem])
+        cnt[lsem] = cnt.get(lsem, 0) + sum(len(w) for _, w, _, _ in moves)
 
-    others = list(range(N - 1))
+    def send(zs, src, dst, engines, sem, lsem, reads):
+        fused([((me + 1 + z) % N, engines[z], src(z), dst(z)) for z in zs], sem, lsem, reads)
+
+    mate = [r for r in range(N) if r != me and topo.chip(cores[r]) == topo.chip(core)][0]
+    side = int(me > mate)
+    far = [r for r in range(side, N, 2) if r != me]
+    out = topo.engines(core, cores[far[0]])
     data_in = list_in = 0
     for k in range(1, N):
-        _, _, e2, o2 = plan((me + k) % N, cores, topo)
-        data_in += 2 * len(e2[N - 1 - k])
+        _, c2, o2, _ = plan((me + k) % N, cores, topo)
+        data_in += sum(len(e[N - 1 - k]) for _, zs, _, e in c2 if N - 1 - k in zs)
         list_in += len(o2[N - 1 - k])
 
     dma("y", "dl0", T.lists[0], T.c1[:, :], [], ["l0"])
@@ -182,19 +190,19 @@ def rank_program(g, core, T, topo):
         dma("ys"[b % 2], "dc1", T.ct[16 * b:16 * b + 16, 0:16], T.c1[:, :], [], ["c1"], more=True)
     for b in range(8):
         dma("sy"[b % 2], "dc2", T.ct[16 * b:16 * b + 16, 16:32], T.c2[:, :], [], ["c2"], more=True)
-    dma("y", "dx", T.xin[:, :], T.x[:, :], [], ["xin"])
-    dma("s", "dw", T["win"][:, :], T.w[:, :], [], ["win"])
+    dma("y", "dx", T.xin[:, :], T.x[:, :], ["c2"], ["xin"])
 
     iota("pi", 1, [[0, 1]], 0, 1)
     iota("l4", 4, [[2, 2], [8, 2]], 0)
     iota("e64", 64, [[1, 64]], me + 1)
     iota("c32", 32, [[1, 32]], 0)
-    iota("v128", 128, [[32, 2], [64, 4], [1, 16]], 0)
     iota("c16", 16, [[16, 2], [0, 8]], 0)
-    send(others, lambda z: T.lists[0], lambda z: T.lists[N - 1 - z], one, "lst", "lsts", ["l0"])
-    iota("tr0", 16, [[16, 16]], 1088)
+    send(range(N - 1), lambda z: T.lists[0], lambda z: T.lists[N - 1 - z], one, "lst", "lsts", ["l0"])
     iota("j0", 20, [[16, 20]], 0)
     iota("k64", 8, [[SLOT, 8]], 0)
+    iota("v128", 128, [[32, 2], [64, 4], [1, 16]], 0, flag=True)
+    iota("zin", 4 * NZ, [[0, 4 * NZ]], 0, flag=True)
+    iota("scat", WIN, [[0, WIN]], 0, flag=True)
 
     fill(T.ones[:, :], 1.0, "ones")
     fill(T.z64[:, :], 0.0, "z64")
@@ -224,6 +232,8 @@ def rank_program(g, core, T, topo):
     ts(pf[:, 9:10], kc, 2.0, -50.0, LT, MUL, ["pf"], ["g2a"])
     ts(pf[:, 10:11], pf[:, 8:9], float((me + 1) % N), None, ADD, None, ["g1a"], ["g1"])
     ts(pf[:, 11:12], pf[:, 9:10], float((me + 2) % N), None, ADD, None, ["g2a"], ["g2"])
+    for i in range(2):
+        op("s", g.scalar.activation, (T.vals[:, 128 * i:128 * i + 128], T.v128[:, :], IDENT, pf[:, 6:7]), ["v128", "pf"], ["va%d" % i])
 
     l64 = T.l64[:, 0:4]
     c1w, c2w = T.ct[:, 0:16].indirect(l64), T.ct[:, 16:32].indirect(l64)
@@ -258,24 +268,20 @@ def rank_program(g, core, T, topo):
     tt(T.wb[:, :], T.qb[:, :], T.scb[:, :], MUL, ["qb", "scb"], ["wb"])
     tt(T.p2[:, 32:33], bcol[:, 1:2], T.p1[:, 32:33], ADD, ["bn", "p1z"], ["p2z"])
     scan(T.cs1[:, 8:72], T.td1[:, :], 64, 0.0, ["td1"], ["cs1"])
-    fill(T.scat[:, :], 0.0, "scat")
-    ts(T.vals[:, 0:128], T.v128[:, :], pf[:, 6:7], None, ADD, None, ["v128", "pf"], ["va0"])
-    ts(T.vals[:, 128:256], T.v128[:, :], pf[:, 6:7], None, ADD, None, ["v128", "pf"], ["va1"])
     for i in range(2):
         tt(T.s1[:, 8 * i:8 * i + 8], T.cs1[:, 15:72:8], T.cs1[:, 7:64:8], SUB, ["cs1", "cs1z"], ["s1%d" % i])
     ts(T.x1[:, :], T.s1[:, :], 48, None, AND, None, ["s10", "s11"], ["x1"])
     tt(T.y1[:, :], T.s1[:, :], T.c16[:, :], ADD, ["s10", "s11", "c16"], ["y1"])
     tt(T.y1b[:, :], T.y1[:, :], T.x1[:, :], ADD, ["x1", "y1"], ["y1b"])
-    cp(T.off1[:, :], T.y1b[:, :], ["y1b"], ["off1"])
-    cp(T.scat[:, 0:WIN].indirect(T.off1[:, 0:16]), T.vals[:, :], ["off1", "va0", "va1"], ["scat"])
+    tt(T.cy[:, :], T.c16[:, :], T.y1b[:, :], SUB, ["c16", "y1b"], ["cy"])
     op("v", V.quantize_mx, (T.xq[:, :], T.xs[:, :], T.xin[:, :]), ["xin"], ["xq"])
-    ts(T.tr[:, :], T.tr0[:, :], ic, None, ADD, None, ["tr0", "pf"], ["tr"])
-    tt(T.ctr[:, :], T.c16[:, :], T.tr[:, :], SUB, ["c16", "tr"], ["ctr"])
+    op("v", V.quantize_mx, (T.land[:, ZERO:ZERO + NZ], T.lsc[:, ZERO:ZERO + NZ], T.zin[:, :]), ["zin"], ["zq"])
 
     cnt["lst"] = list_in
     wr["lx"] = [("lst", list_in)]
     for b in range(4):
         dma("ys"[b % 2], "dal", T.al[32 * b:32 * b + 32, 0:64], T.lists[:, :, :], ["lx", "l0"], ["al"], more=True)
+    dma("y", "dw", T["win"][:, :], T.w[:, :], ["lx"], ["win"])
     eqs, gcol = T.eqs, T.gcol
     for i in range(2):
         ts(eqs[:, 64 * i:64 * i + 64], T.al[:, :], pf[:, 10 + i:11 + i], None, EQ, None, ["al", "g%d" % (i + 1)], ["eq%d" % i])
@@ -297,7 +303,13 @@ def rank_program(g, core, T, topo):
     tt(T.m16[:, :], T.tot2[:, 0:16], T.tot2[:, 16:32], ADD, ["tot2"], ["m16"])
     red(bcol[:, 4:5], T.p2[:, :], ["p2", "p2z"], ["b2c"])
     tt(T.m8[:, :], T.m16[:, 0:8], T.m16[:, 8:16], ADD, ["m16"], ["m8"])
-    dma("y", "dm", T.marks[0], T.m8[0:32, 0:8], ["m8"], ["mk0"])
+    ways = [out[0:4], out[4:6], out[6:8]]
+    moves = [(r, ways[(me - r) % N // 2 - 1], T.m8[:, (r - side - me - 1) % N:(r - side - me - 1) % N + 2],
+              T.ml[:, (me - r) % N - 2:(me - r) % N]) for r in far]
+    moves.append((mate, inn, T.m8[:, near - side:near - side + 2], T.mp[:, 0:2]))
+    fused(moves, "mar", "mars", ["m8"])
+    cnt["mar"] = cnt["mars"]
+    wr["mx"] = [("mar", cnt["mar"])]
     scan(T.sc2[:, :], T.r2[:, :], 64, bcol[:, 4:5], ["r2", "b2c"], ["sc2"])
     tt(T.d2[:, :], T.r2[:, :], T.sc2[:, :], MUL, ["r2", "sc2"], ["d2"])
     tr(T.td2[:, :], T.d2[:, :], ["d2"], ["td2"])
@@ -306,14 +318,12 @@ def rank_program(g, core, T, topo):
         tt(T.s2[:, 8 * i:8 * i + 8], T.cs2[:, 15:72:8], T.cs2[:, 7:64:8], SUB, ["cs2", "cs2z"], ["s2%d" % i])
     ts(T.x2[:, :], T.s2[:, :], 48, None, AND, None, ["s20", "s21"], ["x2"])
     ts(T.v2[:, :], T.s2[:, :], 64, 6, AND, SHR, ["s20", "s21"], ["v2"])
-    tt(T.y2[:, :], T.s2[:, :], T.ctr[:, :], ADD, ["s20", "s21", "ctr"], ["y2"])
+    tt(T.y2[:, :], T.s2[:, :], T.cy[:, :], ADD, ["s20", "s21", "cy"], ["y2"])
     tt(T.y2b[:, :], T.y2[:, :], T.x2[:, :], ADD, ["x2", "y2"], ["y2b"])
     tt(T.y2c[:, :], T.y2b[:, :], T.v2[:, :], MUL, ["y2b", "v2"], ["y2c"])
-    tt(T.y2d[:, :], T.y2c[:, :], T.tr[:, :], ADD, ["y2c", "tr"], ["y2d"])
+    tt(T.y2d[:, :], T.y2c[:, :], T.y1b[:, :], ADD, ["y2c", "y1b"], ["y2d"])
     cp(T.off2[:, :], T.y2d[:, :], ["y2d"], ["off2"])
     cp(T.scat[:, 0:WIN].indirect(T.off2[:, 0:16]), T.vals[:, :], ["off2", "va0", "va1"], ["scat"])
-
-    send(others, lambda z: T.marks[0], lambda z: T.marks[N - 1 - z], one, "mar", "mars", ["mk0"])
 
     def lists_of(za, zb):
         key = "so%d" % za
@@ -326,18 +336,32 @@ def rank_program(g, core, T, topo):
         op("v", V.tensor_copy, (oq[:, n0:n0 + n].bitcast(dt.uint32), iq[:, 0:m].bitcast(dt.uint32).indirect(off)), reads, [writes + "q"])
         op("s", g.scalar.activation, (os_[:, n0:n0 + n], is_[:, 0:m].indirect(off), COPY), reads, [writes + "s"])
 
-    def column_sends(zs, sq, sp, key):
-        z0 = zs[0]
-        send(zs, lambda z: sq[:, SLOT * (z - z0):SLOT * (z - z0 + 1)].bitcast(dt.uint8),
-             lambda z: T.land[:, SLOT * (N - 1 - z):SLOT * (N - z)].bitcast(dt.uint8), eng, "dat", "dats", [key + "q"])
-        send(zs, lambda z: sp[:, SLOT * (z - z0):SLOT * (z - z0 + 1)],
-             lambda z: T.lsc[:, SLOT * (N - 1 - z):SLOT * (N - z)], eng, "dat", "dats", [key + "s"])
-
-    for zs, sq, sp, key in ((run, T.sq1, T.sp1, "w1"), (rest, T.sq2, T.sp2, "w2")):
+    def make(zs, sq, sp, key):
         za, zb = zs[0], zs[-1] + 1
         k = lists_of(za, zb)
         pick(sq, sp, SLOT * (zb - za), T.xq, T.xs, TOK, T.so[:, 4 * za:4 * zb], 0, [k, "xq"], key)
-        column_sends(zs, sq, sp, key)
+
+    def columns(call, sq, sp, key):
+        kind, zs, n, engines = call
+
+        def src(z):
+            c = SLOT * (z - zs[0])
+            return sq[:, c:c + n].bitcast(dt.uint8) if kind == "q" else sp[:, c:c + n]
+
+        def dst(z):
+            c = SLOT * (N - 1 - z)
+            return T.land[:, c:c + n].bitcast(dt.uint8) if kind == "q" else T.lsc[:, c:c + n]
+        send(zs, src, dst, engines, "dat", "dats", [key + kind])
+
+    make(calls[0][1], T.sq1, T.sp1, "w1")
+    columns(calls[0], T.sq1, T.sp1, "w1")
+    columns(calls[1], T.sq1, T.sp1, "w1")
+    make(calls[2][1], T.sq2, T.sp2, "w2")
+    columns(calls[2], T.sq2, T.sp2, "w2")
+    fused([(mate, inn, T.ml[:, 0:6], T.mf[:, 0:6])], "mfw", "mars", ["mx"])
+    columns(calls[3], T.sq2, T.sp2, "w2")
+    cnt["mfw"] = len(inn)
+    wr["mf"] = [("mfw", cnt["mfw"])]
     k = lists_of(N - 1, N)
     pick(T.land, T.lsc, SLOT, T.xq, T.xs, TOK, T.so[:, 4 * (N - 1):4 * N], 0, [k, "xq"], "own")
 
@@ -355,13 +379,11 @@ def rank_program(g, core, T, topo):
     ts(T.jj[:, :], T.j0[:, :], ic, None, ADD, None, ["j0", "pf"], ["jj"])
 
     def terms(lo):
-        a, b = 80 * (lo // 8), 40 * (lo // 8)
+        a, b, d, c = 10 * lo, 5 * lo, 5 * lo, 20 * lo
         for q in range(lo + 1, lo + 9):
             ts(T.tm[:, 20 * (q - 1):20 * q], T.jj[:, :], pp[:, q:q + 1], T.dd[:, q - 1:q], GE, MUL, ["jj", "pp1", "pp9", "dd%d" % lo], ["tm%d" % q])
-        c = 20 * lo
         tt(T.t80[:, a:a + 80], T.tm[:, c:c + 80], T.tm[:, c + 80:c + 160], ADD, ["tm%d" % q for q in range(lo + 1, lo + 9)], ["t80%d" % lo])
         tt(T.t40[:, b:b + 40], T.t80[:, a:a + 40], T.t80[:, a + 40:a + 80], ADD, ["t80%d" % lo], ["t40%d" % lo])
-        d = 40 * (lo // 8)
         tt(T.t20[:, d:d + 20], T.t40[:, b:b + 20], T.t40[:, b + 20:b + 40], ADD, ["t40%d" % lo], ["t20%d" % lo])
         x, key = (T.jj[:, :], "jj") if lo == 0 else (T.t20[:, 20:40], "sum0")
         tt(T.t20[:, d + 20:d + 40], T.t20[:, d:d + 20], x, ADD, ["t20%d" % lo, key], ["sum%d" % lo])
@@ -370,14 +392,13 @@ def rank_program(g, core, T, topo):
     tt(T.dd[:, 0:8], T.de[:, 1:9], T.de[:, 0:8], SUB, ["de0"], ["dd0"])
     terms(0)
     op("v", V.quantize_mx, (T.wq[:, :], T.wsc[:, :], T["win"][:, :]), ["win"], ["wq"])
-    fill(T.zin[:, :], 0.0, "zin")
-    op("v", V.quantize_mx, (T.land[:, ZERO:ZERO + NZ], T.lsc[:, ZERO:ZERO + NZ], T.zin[:, :]), ["zin"], ["zq"])
 
-    cnt["mar"] = list_in
-    wr["mx"] = [("mar", list_in)]
-    dma("y", "dml", T.ml[0:1, 0:64], T.marks[:, 0:4, :], ["mx", "mk0"], ["ml"])
-    op("g", g.partition_broadcast, (T.mb[:, 0:64], T.ml[0:1, 0:64], 128), ["ml"], ["mb"])
-    scan(pp[:, 9:17], T.mb[:, 7:57:7], 8, pp[:, 8:9], ["mb", "pp1"], ["pp9"])
+    kn, kf = (mate - me) % N, (mate - me + 2) % N
+    cp(T.m9[:, 0:1], T.m8[:, N - 1:N], ["m8"], ["m90"])
+    cp(T.m9[:, 2:8:2], T.ml[:, side:6:2], ["mx"], ["m91"])
+    cp(T.m9[:, kn:kn + 1], T.mp[:, 1 - side:2 - side], ["mx"], ["m92"])
+    cp(T.m9[:, kf:kf + 5:2], T.mf[:, side:6:2], ["mf"], ["m93"])
+    scan(pp[:, 9:17], T.m9[:, :], 8, pp[:, 8:9], ["m90", "m91", "m92", "m93", "pp1"], ["pp9"])
     tt(T.de[:, 9:17], bb[:, 9:17], pp[:, 9:17], SUB, ["bb8", "bb16", "pp9"], ["de9"])
     tt(T.dd[:, 8:16], T.de[:, 9:17], T.de[:, 8:16], SUB, ["de9", "de0"], ["dd8"])
     terms(8)
@@ -386,17 +407,22 @@ def rank_program(g, core, T, topo):
     cnt["dat"] = data_in
     wr["dx"] = [("dat", data_in)]
     got = ["dx", "ownq", "owns", "zq", "fo"]
-    pick(T.fq, T.fs, ROOM, T.land, T.lsc, ZERO + NZ, T.fo[:, 0:20], 0, got, "f")
-    for o in range(O):
-        a = T.acc[:, 512 * o:512 * o + ROOM]
-        op("t", g.tensor.matmul_mx, (a, T.wq[:, 128 * o:128 * o + 128], T.wsc[:, 128 * o:128 * o + 128], T.fq[:, 0:ROOM], T.fs[:, 0:ROOM], True, True),
-           ["wq", "fq", "fs"], ["acc%d" % o])
-    for o in range(O):
-        a, y = T.acc[:, 512 * o:512 * o + ROOM], T.yo[:, ROOM * o:ROOM * o + ROOM]
-        if o % 2 == 0:
-            cp(y, a, ["acc%d" % o], ["yo%d" % o])
+    cuts = ((0, 192), (192, ROOM))
+    for i, (a, b) in enumerate(cuts):
+        pick(T.fq, T.fs, b - a, T.land, T.lsc, ZERO + NZ, T.fo[:, a // 16:b // 16], a, got, "f%d" % i)
+    pieces = [(0, a, b, 512 * O * (i > 0), ["f%dq" % i, "f%ds" % i]) for i, (a, b) in enumerate(cuts)]
+    pieces += [(o, 0, ROOM, 512 * o, ["f0q", "f0s", "f1q", "f1s"]) for o in range(1, O)]
+    for i, (o, a, b, p, keys) in enumerate(pieces):
+        op("t", g.tensor.matmul_mx, (T.acc[:, p:p + b - a], T.wq[:, 128 * o:128 * o + 128], T.wsc[:, 128 * o:128 * o + 128],
+                                     T.fq[:, a:b], T.fs[:, a:b], True, True), ["wq"] + keys, ["acc%d" % i])
+    for i, (o, a, b, p, keys) in enumerate(pieces):
+        src, dst = T.acc[:, p:p + b - a], T.yo[:, ROOM * o + a:ROOM * o + b]
+        if i % 2 == 0:
+            cp(dst, src, ["acc%d" % i], ["yo%d" % i])
         else:
-            op("s", g.scalar.activation, (y, a, COPY), ["acc%d" % o], ["yo%d" % o])
-        dma("y", "dy", T.y[:, ROOM * o:ROOM * o + ROOM], y, ["yo%d" % o], ["yout"], more=True)
+            op("s", g.scalar.activation, (dst, src, COPY), ["acc%d" % i], ["yo%d" % i])
+        if b == ROOM:
+            dma("y", "dy", T.y[:, ROOM * o:ROOM * o + ROOM], T.yo[:, ROOM * o:ROOM * o + ROOM],
+                ["yo%d" % j for j in range(len(pieces)) if pieces[j][0] == o], ["yout"], more=True)
     for sem in sorted(cnt):
         need("y", (sem, None))

@@ -5,7 +5,8 @@ N, TOK, O, CAP, ROOM, BOTH = 8, 256, 4, 288, 320, 60
 SLOT = 64
 ZERO = N * SLOT
 NZ = 128
-WIN = 1088
+WSLOT = 256
+WIN = N * WSLOT
 LATE = 400
 
 
@@ -18,34 +19,30 @@ SCRATCH = {
     "lists": ("dram", [N, 128, 2], I32),
     "ct": _sb(32, I32), "xin": _sb(4 * TOK, B16), "win": _sb(512 * O, B16), "zin": _sb(4 * NZ, B16),
     "xq": _sb(TOK, MX), "xs": _sb(TOK, U8), "wq": _sb(128 * O, MX), "wsc": _sb(128 * O, U8),
-    "pi": _sb(8, I32), "pb": _sb(8, I32), "pf": _sb(16, F32), "e64": _sb(64, I32), "ec": _sb(64, I32),
-    "l4": _sb(4, I32), "l64": _sb(4, U16), "c32": _sb(32, I32), "cz": _sb(32, I32), "ch": _sb(32, I32),
-    "meq": _sb(32, F32), "mlh": _sb(32, F32), "mlt": _sb(32, F32), "v128": _sb(128, B16), "vals": _sb(256, B16),
-    "c16": _sb(16, I32), "j0": _sb(20, I32), "jj": _sb(20, F32),
-    "k64": _sb(8, I32), "ones": _sb(32, F32), "z64": _sb(64, F32),
-    "pre": _sb(256, B16), "mt": _sb(256, B16), "tcol": _sb(8, F32), "bc": _sb(96, F32), "tot": _sb(96, F32),
-    "p1": _sb(33, F32), "pn": _sb(32, F32), "pa": _sb(33, F32), "pq": _sb(33, F32), "p2": _sb(33, F32), "bcol": _sb(8, F32),
-    "sc1": _sb(64, F32), "d1": _sb(64, F32), "td1": _sb(64, F32), "cs1": _sb(72, F32), "s1": _sb(16, I32), "x1": _sb(16, I32),
-    "y1": _sb(16, I32), "y1b": _sb(16, I32), "cy": _sb(16, I32),
-    "sca": _sb(64, F32), "scb": _sb(64, F32), "qa": _sb(64, B16), "qb": _sb(64, B16), "wa": _sb(64, F32), "wb": _sb(64, F32),
+    "ra": _sb(128, F32), "ca": _sb(128, F32), "rb": _sb(64, F32), "cb": _sb(64, F32), "e64": _sb(64, I32), "ec": _sb(64, I32),
+    "l4": _sb(4, I32), "l64": _sb(4, U16), "meq": _sb(32, F32), "mgt": _sb(32, F32), "mlt": _sb(32, F32),
+    "v128": _sb(128, B16), "vals": _sb(256, B16), "j0": _sb(20, I32), "jj": _sb(20, F32), "ones": _sb(32, F32), "z64": _sb(64, F32),
+    "pre": _sb(256, B16), "mt": _sb(256, B16), "tcol": _sb(8, F32), "bm": _sb(128, F32), "tb": _sb(168, F32), "bcol": _sb(8, F32),
+    "sc1": _sb(64, F32), "d1": _sb(64, F32), "sca": _sb(64, F32), "scb": _sb(64, F32), "wa": _sb(64, F32), "wb": _sb(64, F32),
     "al": _sb(64, I32), "eqs": _sb(192, B16), "gcol": _sb(8, F32), "bg": _sb(64, F32), "tg": _sb(64, F32), "gs": _sb(8, F32),
-    "ru": _sb(64, B16), "rv": _sb(64, B16), "r2": _sb(64, B16), "b2": _sb(32, F32), "tot2": _sb(32, F32), "m16": _sb(16, F32), "m8": _sb(8, F32),
-    "sc2": _sb(64, F32), "d2": _sb(64, F32), "td2": _sb(64, F32), "cs2": _sb(72, F32), "s2": _sb(16, I32), "x2": _sb(16, I32), "v2": _sb(16, I32),
-    "y2": _sb(16, I32), "y2b": _sb(16, I32), "y2c": _sb(16, I32), "y2d": _sb(16, I32), "off2": _sb(16, U16),
+    "ka": _sb(64, B16), "kb": _sb(64, B16), "kk": _sb(64, B16), "r2": _sb(64, B16), "bm2": _sb(64, F32), "p2": _sb(96, F32),
+    "m16": _sb(16, F32), "m8": _sb(8, F32), "sc2": _sb(64, F32), "d2": _sb(64, F32), "d1k": _sb(64, F32), "dd1": _sb(64, F32),
+    "td": _sb(64, F32), "cs": _sb(72, F32), "s8": _sb(8, I32), "x8": _sb(8, I32), "y8": _sb(8, I32), "off": _sb(16, U16),
     "scat": _sb(WIN, B16), "tw": _sb(1024, B16), "self": _sb(32, F32), "so": _sb(32, U16),
-    "sq1": _sb(3 * SLOT, MX), "sp1": _sb(3 * SLOT, U8), "sq2": _sb(4 * SLOT, MX), "sp2": _sb(4 * SLOT, U8),
+    "sq1": _sb(2 * SLOT, MX), "sp1": _sb(2 * SLOT, U8), "sq2": _sb(4 * SLOT, MX), "sp2": _sb(4 * SLOT, U8),
+    "sq3": _sb(SLOT, MX), "sp3": _sb(SLOT, U8),
     "land": _sb(ZERO + NZ, MX), "lsc": _sb(ZERO + NZ, U8),
     "b3": _sb(32, F32), "t3": _sb(32, F32), "n16": _sb(16, F32), "n8": _sb(8, F32), "n8s": _sb(8, F32), "pp": _sb(24, F32), "bb": _sb(24, F32),
-    "de": _sb(24, F32), "dd": _sb(24, F32), "tm": _sb(320, F32), "t80": _sb(160, F32), "t40": _sb(80, F32), "t20": _sb(100, F32),
-    "ml": _sb(8, F32), "mf": _sb(8, F32), "mp": _sb(8, F32), "m9": _sb(8, F32), "fo": _sb(20, U16), "fq": _sb(ROOM, MX), "fs": _sb(ROOM, U8),
-    "acc": ("psum", [128, 512 * (O + 1)], F32), "yo": _sb(ROOM * O, F32),
+    "de": _sb(16, F32), "dd": _sb(24, F32), "bd": _sb(8, F32), "tm": _sb(320, F32), "t80": _sb(160, F32), "t40": _sb(80, F32), "t20": _sb(80, F32),
+    "ml": _sb(8, F32), "fo": _sb(20, U16), "fq": _sb(ROOM, MX), "fs": _sb(ROOM, U8),
+    "acc": ("psum", [128, 512 * (O + 2)], F32), "yo": _sb(ROOM * O, F32),
 }
 SEMAPHORES = ["cv", "cs", "cg", "ct", "dl0", "dc1", "dc2", "dx", "dw", "dal", "dy",
-              "lst", "lsts", "mar", "mars", "mfw", "dat", "dats"]
+              "lst", "lsts", "mar", "mars", "dat", "dats"]
 
 ADD, SUB, MUL, MIN = AluOpType.add, AluOpType.subtract, AluOpType.mult, AluOpType.min
-GE, LT, EQ = AluOpType.is_ge, AluOpType.is_lt, AluOpType.is_equal
-AND, SHR = AluOpType.bitwise_and, AluOpType.logical_shift_right
+GE, GT, LT, EQ = AluOpType.is_ge, AluOpType.is_gt, AluOpType.is_lt, AluOpType.is_equal
+AND = AluOpType.bitwise_and
 COPY, IDENT = ActivationFunctionType.Copy, ActivationFunctionType.Identity
 
 
@@ -63,16 +60,18 @@ def plan(me, cores, topo):
 
     some = far[:2] if near[0] == 0 else far[-2:]
     rest = [z for z in far if z not in some]
-    some_e = deal(some)
-    some_e.update({z: inn for z in near})
-    some = sorted(some + near)
     calls = []
-    for zs, e in ((some, some_e), (rest, deal(rest))):
+    for zs, e in ((some, deal(some)), (rest, deal(rest)), (near, {z: inn for z in near})):
         n = SLOT if 0 in zs or 1 in zs else BOTH
         calls += [("q", zs, n, e), ("s", zs, n, e)]
-    single = {z: out[i:i + 1] for i, z in enumerate(far)}
-    single.update({z: inn[:1] for z in near})
-    return near[0], calls, single, inn
+    extra = len(out) - len(far)
+    counts, at = {}, 0
+    for i, z in enumerate(far):
+        k = 2 if i < extra else 1
+        counts[z] = out[at:at + k]
+        at += k
+    counts.update({z: inn for z in near})
+    return calls, counts, out[::4]
 
 
 def rank_program(g, core, T, topo):
@@ -80,7 +79,7 @@ def rank_program(g, core, T, topo):
     if me is None:
         return
     cores = [int(c) for c in T.cores]
-    near, calls, one, inn = plan(me, cores, topo)
+    calls, ways, few = plan(me, cores, topo)
     queue = {"v": g.vector, "s": g.scalar, "t": g.tensor, "g": g, "y": g.sync}
     cnt, seen, wr, rd = {}, {}, {}, {}
 
@@ -152,9 +151,12 @@ def rank_program(g, core, T, topo):
     def fill(ap, val, key):
         op("v", V.memset, (ap, val), [], [key])
 
-    def iota(name, n, pattern, base, chan=0, flag=False):
+    def iota(ap, key, pattern, base, flag=False):
         kw = {"allow_small_or_imprecise_dtypes": True} if flag else {}
-        op("g", g.iota, (T[name][:, 0:n], pattern, base, chan), [], [name], **kw)
+        op("g", g.iota, (ap, pattern, base, 0), [], [key], **kw)
+
+    def act(out, a, reads, writes):
+        op("s", g.scalar.activation, (out, a, COPY), reads, writes)
 
     def at(r):
         rid, pid, _ = topo.addr(cores[r])
@@ -166,115 +168,90 @@ def rank_program(g, core, T, topo):
             m |= 1 << e
         return m
 
-    def fused(moves, sem, lsem, reads):
-        before("g", reads, [])
-        g.remote_dma_fused([RemoteDMATransfer(dst_ids=[at(r)], dma_engine_mask=mask(w), remote_sem=T.sem[sem], src=a, dst=b)
-                            for r, w, a, b in moves], local_sem=T.sem[lsem])
-        cnt[lsem] = cnt.get(lsem, 0) + sum(len(w) for _, w, _, _ in moves)
-
     def send(zs, src, dst, engines, sem, lsem, reads):
-        fused([((me + 1 + z) % N, engines[z], src(z), dst(z)) for z in zs], sem, lsem, reads)
+        before("g", reads, [])
+        g.remote_dma_fused([RemoteDMATransfer(dst_ids=[at((me + 1 + z) % N)], dma_engine_mask=mask(engines[z]),
+                                              remote_sem=T.sem[sem], src=src(z), dst=dst(z)) for z in zs], local_sem=T.sem[lsem])
+        cnt[lsem] = cnt.get(lsem, 0) + sum(len(engines[z]) for z in zs)
 
-    mate = [r for r in range(N) if r != me and topo.chip(cores[r]) == topo.chip(core)][0]
-    side = int(me > mate)
-    far = [r for r in range(side, N, 2) if r != me]
-    out = topo.engines(core, cores[far[0]])
-    data_in = list_in = 0
+    data_in = list_in = count_in = 0
     for k in range(1, N):
-        _, c2, o2, _ = plan((me + k) % N, cores, topo)
+        c2, w2, f2 = plan((me + k) % N, cores, topo)
         data_in += sum(len(e[N - 1 - k]) for _, zs, _, e in c2 if N - 1 - k in zs)
-        list_in += len(o2[N - 1 - k])
+        count_in += len(w2[N - 1 - k])
+        list_in += len(f2)
 
     dma("y", "dl0", T.lists[0], T.c1[:, :], [], ["l0"])
     for b in range(8):
         dma("ys"[b % 2], "dc1", T.ct[16 * b:16 * b + 16, 0:16], T.c1[:, :], [], ["c1"], more=True)
     for b in range(8):
         dma("sy"[b % 2], "dc2", T.ct[16 * b:16 * b + 16, 16:32], T.c2[:, :], [], ["c2"], more=True)
-    dma("y", "dx", T.xin[:, :], T.x[:, :], ["c2"], ["xin"])
+    dma("y", "dx", T.xin[:, :], T.x[:, :], [], ["xin"])
 
-    iota("pi", 1, [[0, 1]], 0, 1)
-    iota("l4", 4, [[2, 2], [8, 2]], 0)
-    iota("e64", 64, [[1, 64]], me + 1)
-    iota("c32", 32, [[1, 32]], 0)
-    iota("c16", 16, [[16, 2], [0, 8]], 0)
-    send(range(N - 1), lambda z: T.lists[0], lambda z: T.lists[N - 1 - z], one, "lst", "lsts", ["l0"])
-    iota("j0", 20, [[16, 20]], 0)
-    iota("k64", 8, [[SLOT, 8]], 0)
-    iota("v128", 128, [[32, 2], [64, 4], [1, 16]], 0, flag=True)
-    iota("zin", 4 * NZ, [[0, 4 * NZ]], 0, flag=True)
-    iota("scat", WIN, [[0, WIN]], 0, flag=True)
+    ra, rb = T.ra, T.rb
+    iota(T.l4[:, :], "l4", [[2, 2], [8, 2]], 0)
+    iota(ra[:, 64:96], "ra2", [[1, 2], [4, 2], [0, 8]], 0, flag=True)
+    iota(ra[:, 0:32], "ra0", [[0, 4], [1, 8]], 0, flag=True)
+    iota(ra[:, 32:64], "ra1", [[1, 4], [0, 8]], 0, flag=True)
+    iota(ra[:, 96:128], "ra3", [[0, 4], [WSLOT, 8]], -1, flag=True)
+    iota(T.e64[:, :], "e64", [[1, 64]], me + 1)
+    before("g", ["l0"], [])
+    g.remote_dma_fused([RemoteDMATransfer(dst_ids=[at((me + 1 + z) % N) for z in range(N - 1)], dma_engine_mask=mask(few),
+                                          remote_sem=T.sem["lst"], srcs=[T.lists[0]],
+                                          dsts=[T.lists[N - 1 - z] for z in range(N - 1)])], local_sem=T.sem["lsts"])
+    cnt["lsts"] = len(few)
+    iota(T.zin[:, :], "zin", [[0, 4 * NZ]], 0, flag=True)
+    iota(rb[:, 32:64], "rb1", [[16, 2], [0, 16]], 0, flag=True)
+    iota(rb[:, 0:32], "rb0", [[0, 2], [1, 16]], 0, flag=True)
+    iota(T.v128[:, :], "v128", [[32, 2], [64, 4], [1, 16]], 0, flag=True)
+    iota(T.j0[:, :], "j0", [[16, 20]], 0)
+    iota(T.bb[:, 0:8], "bb0", [[SLOT, 8]], 0, flag=True)
 
     fill(T.ones[:, :], 1.0, "ones")
     fill(T.z64[:, :], 0.0, "z64")
-    fill(T.cs1[:, 0:8], 0.0, "cs1z")
-    fill(T.cs2[:, 0:8], 0.0, "cs2z")
-    fill(T.pa[:, 32:33], float(LATE), "paz")
-    fill(T.pq[:, 32:33], float(LATE), "pqz")
+    fill(T.cs[:, 0:8], 0.0, "csz")
     fill(T.pp[:, 0:1], 0.0, "pp0")
     fill(T.bb[:, 16:17], float(ZERO), "bb16")
-    pb, pf = T.pb, T.pf
-    pi = T.pi[:, 0:1]
-    for j, (a, b, o1, o2) in enumerate([(7, None, AND, None), (3, 3, SHR, AND), (15, None, AND, None), (2, 7, SHR, AND),
-                                        (8, 1, AND, SHR), (16, 4, AND, SHR), (16, None, AND, None)]):
-        ts(pb[:, j:j + 1], pi, a, b, o1, o2, ["pi"], ["pb%d" % j])
-    cp(pf[:, 0:7], pb[:, 0:7], ["pb%d" % j for j in range(7)], ["pf"])
-    zc, hc, ic, kc = [pf[:, j:j + 1] for j in range(4)]
-    tt(pf[:, 7:8], pf[:, 4:5], pf[:, 5:6], ADD, ["pf"], ["pc"])
-    ts(T.l64[:, :], T.l4[:, :], pf[:, 7:8], None, ADD, None, ["l4", "pc"], ["l64"])
+    tr(T.ca[:, :], ra[:, :], ["ra0", "ra1", "ra2", "ra3"], ["ca"])
+    zc, hc, pc, sc = [T.ca[:, 32 * j:32 * j + 1] for j in range(4)]
     ts(T.ec[:, :], T.e64[:, :], 7, None, AND, None, ["e64"], ["ec"])
-    ts(T.p1[:, 32:33], zc, 128.0, 63.0, MUL, ADD, ["pf"], ["p1z"])
-    ts(T.cz[:, :], T.c32[:, :], 7, None, AND, None, ["c32"], ["cz"])
-    ts(T.ch[:, :], T.c32[:, :], 3, None, SHR, None, ["c32"], ["ch"])
-    ts(T.meq[:, :], T.cz[:, :], zc, None, EQ, None, ["cz", "pf"], ["meq"])
-    ts(T.mlh[:, :], T.ch[:, :], hc, None, LT, None, ["ch", "pf"], ["mlh"])
-    tt(T.mlt[:, :], T.meq[:, :], T.mlh[:, :], MUL, ["meq", "mlh"], ["mlt"])
-    ts(pf[:, 8:9], kc, 1.0, -50.0, LT, MUL, ["pf"], ["g1a"])
-    ts(pf[:, 9:10], kc, 2.0, -50.0, LT, MUL, ["pf"], ["g2a"])
-    ts(pf[:, 10:11], pf[:, 8:9], float((me + 1) % N), None, ADD, None, ["g1a"], ["g1"])
-    ts(pf[:, 11:12], pf[:, 9:10], float((me + 2) % N), None, ADD, None, ["g2a"], ["g2"])
-    for i in range(2):
-        op("s", g.scalar.activation, (T.vals[:, 128 * i:128 * i + 128], T.v128[:, :], IDENT, pf[:, 6:7]), ["v128", "pf"], ["va%d" % i])
+    ts(T.l64[:, :], T.l4[:, :], pc, None, ADD, None, ["l4", "ca"], ["l64"])
+    ts(T.meq[:, :], ra[:, 0:32], zc, None, EQ, None, ["ra0", "ca"], ["meq"])
+    ts(T.mgt[:, :], ra[:, 32:64], hc, None, GT, None, ["ra1", "ca"], ["mgt"])
+    tt(T.mlt[:, :], T.meq[:, :], T.mgt[:, :], MUL, ["meq", "mgt"], ["mlt"])
+    act(T.tb[:, 31:32], sc, ["ca"], ["tb0"])
+    act(T.tb[:, 160:161], sc, ["ca"], ["tb1"])
 
     l64 = T.l64[:, 0:4]
     c1w, c2w = T.ct[:, 0:16].indirect(l64), T.ct[:, 16:32].indirect(l64)
     tt(T.pre[:, 0:64], c1w, T.ec[:, :], EQ, ["c1", "l64", "ec"], ["pre0"])
-    ts(T.pre[:, 128:192], c1w, float((me + 1) % N), None, EQ, None, ["c1", "l64"], ["pre2"])
-    ts(T.pre[:, 192:256], c1w, float((me + 2) % N), None, EQ, None, ["c1", "l64"], ["pre3"])
-    tt(T.pre[:, 64:128], c2w, T.ec[:, :], EQ, ["c2", "l64", "ec"], ["pre1"])
-    tr(T.mt[:, :], T.pre[:, :], ["pre0", "pre1", "pre2", "pre3"], ["mt"])
-    m1, mc, ma, mb = [T.mt[:, 64 * i:64 * i + 64] for i in range(4)]
+    ts(T.pre[:, 64:128], c1w, float((me + 1) % N), None, EQ, None, ["c1", "l64"], ["pre1"])
+    ts(T.pre[:, 128:192], c1w, float((me + 2) % N), None, EQ, None, ["c1", "l64"], ["pre2"])
+    tr(T.mt[:, 0:192], T.pre[:, 0:192], ["pre0", "pre1", "pre2"], ["mt"])
+    tt(T.pre[:, 192:256], c2w, T.ec[:, :], EQ, ["c2", "l64", "ec"], ["pre3"])
+    m1, ma, mb, mc = [T.mt[:, 64 * i:64 * i + 64] for i in range(4)]
     for i, m in enumerate((m1, ma, mb)):
         red(T.tcol[:, i:i + 1], m, ["mt"], ["tcol%d" % i])
-    for i in range(3):
-        ts(T.bc[:, 32 * i:32 * i + 32], T.ones[:, :], T.tcol[:, i:i + 1], None, MUL, None, ["ones", "tcol%d" % i], ["bc%d" % i])
-    tr(T.tot[:, :], T.bc[:, :], ["bc0", "bc1", "bc2"], ["tot"])
-    tt(T.p1[:, 0:32], T.tot[:, 0:32], T.mlt[:, :], MUL, ["tot", "mlt"], ["p1"])
-    tt(T.pn[:, :], T.tot[:, 0:32], T.meq[:, :], MUL, ["tot", "meq"], ["pn"])
-    tt(T.pa[:, 0:32], T.tot[:, 32:64], T.mlt[:, :], MUL, ["tot", "mlt"], ["pa"])
-    tt(T.pq[:, 0:32], T.tot[:, 64:96], T.mlt[:, :], MUL, ["tot", "mlt"], ["pq"])
+    tr(mc, T.pre[:, 192:256], ["pre3"], ["mc"])
+    ts(T.bm[:, 0:32], T.mlt[:, :], T.tcol[:, 0:1], None, MUL, None, ["mlt", "tcol0"], ["bm0"])
+    ts(T.bm[:, 32:64], T.mlt[:, :], T.tcol[:, 1:2], LATE / 32, MUL, ADD, ["mlt", "tcol1"], ["bm1"])
+    ts(T.bm[:, 64:96], T.mlt[:, :], T.tcol[:, 2:3], LATE / 32, MUL, ADD, ["mlt", "tcol2"], ["bm2"])
+    ts(T.bm[:, 96:128], T.meq[:, :], T.tcol[:, 0:1], None, MUL, None, ["meq", "tcol0"], ["bm3"])
+    tr(T.tb[:, 32:160], T.bm[:, :], ["bm0", "bm1", "bm2", "bm3"], ["tb"])
     bcol = T.bcol
-    red(bcol[:, 0:1], T.p1[:, :], ["p1", "p1z"], ["b1"])
-    red(bcol[:, 2:3], T.pa[:, :], ["pa", "paz"], ["ba"])
-    red(bcol[:, 3:4], T.pq[:, :], ["pq", "pqz"], ["bq"])
-    red(bcol[:, 1:2], T.pn[:, :], ["pn"], ["bn"])
+    red(bcol[:, 0:1], T.tb[:, 31:64], ["tb", "tb0"], ["b1"])
+    red(bcol[:, 1:2], T.tb[:, 64:96], ["tb"], ["ba"])
+    red(bcol[:, 2:3], T.tb[:, 96:128], ["tb"], ["bq"])
+    red(T.p2[:, 31:32], T.tb[:, 128:161], ["tb", "tb1"], ["p2k"])
     scan(T.sc1[:, :], m1, 64, bcol[:, 0:1], ["mt", "b1"], ["sc1"])
-    scan(T.sca[:, :], ma, 64, bcol[:, 2:3], ["mt", "ba"], ["sca"])
-    scan(T.scb[:, :], mb, 64, bcol[:, 3:4], ["mt", "bq"], ["scb"])
+    scan(T.sca[:, :], ma, 64, bcol[:, 1:2], ["mt", "ba"], ["sca"])
+    scan(T.scb[:, :], mb, 64, bcol[:, 2:3], ["mt", "bq"], ["scb"])
     tt(T.d1[:, :], m1, T.sc1[:, :], MUL, ["mt", "sc1"], ["d1"])
-    tt(T.qa[:, :], ma, mc, MUL, ["mt"], ["qa"])
-    tt(T.qb[:, :], mb, mc, MUL, ["mt"], ["qb"])
-    tr(T.td1[:, :], T.d1[:, :], ["d1"], ["td1"])
-    tt(T.wa[:, :], T.qa[:, :], T.sca[:, :], MUL, ["qa", "sca"], ["wa"])
-    tt(T.wb[:, :], T.qb[:, :], T.scb[:, :], MUL, ["qb", "scb"], ["wb"])
-    tt(T.p2[:, 32:33], bcol[:, 1:2], T.p1[:, 32:33], ADD, ["bn", "p1z"], ["p2z"])
-    scan(T.cs1[:, 8:72], T.td1[:, :], 64, 0.0, ["td1"], ["cs1"])
-    for i in range(2):
-        tt(T.s1[:, 8 * i:8 * i + 8], T.cs1[:, 15:72:8], T.cs1[:, 7:64:8], SUB, ["cs1", "cs1z"], ["s1%d" % i])
-    ts(T.x1[:, :], T.s1[:, :], 48, None, AND, None, ["s10", "s11"], ["x1"])
-    tt(T.y1[:, :], T.s1[:, :], T.c16[:, :], ADD, ["s10", "s11", "c16"], ["y1"])
-    tt(T.y1b[:, :], T.y1[:, :], T.x1[:, :], ADD, ["x1", "y1"], ["y1b"])
-    tt(T.cy[:, :], T.c16[:, :], T.y1b[:, :], SUB, ["c16", "y1b"], ["cy"])
+    tt(T.wa[:, :], ma, T.sca[:, :], MUL, ["mt", "sca"], ["wa"])
+    tt(T.wb[:, :], mb, T.scb[:, :], MUL, ["mt", "scb"], ["wb"])
     op("v", V.quantize_mx, (T.xq[:, :], T.xs[:, :], T.xin[:, :]), ["xin"], ["xq"])
+    tr(T.cb[:, :], rb[:, :], ["rb0", "rb1"], ["cb"])
+    ts(T.jj[:, :], T.j0[:, :], T.cb[:, 0:1], None, ADD, None, ["j0", "cb"], ["jj"])
     op("v", V.quantize_mx, (T.land[:, ZERO:ZERO + NZ], T.lsc[:, ZERO:ZERO + NZ], T.zin[:, :]), ["zin"], ["zq"])
 
     cnt["lst"] = list_in
@@ -282,64 +259,60 @@ def rank_program(g, core, T, topo):
     for b in range(4):
         dma("ys"[b % 2], "dal", T.al[32 * b:32 * b + 32, 0:64], T.lists[:, :, :], ["lx", "l0"], ["al"], more=True)
     dma("y", "dw", T["win"][:, :], T.w[:, :], ["lx"], ["win"])
+    for i in range(2):
+        op("s", g.scalar.activation, (T.vals[:, 128 * i:128 * i + 128], T.v128[:, :], IDENT, T.cb[:, 32:33]), ["v128", "cb"], ["va%d" % i])
+    for z in range(N):
+        act(T.scat[:, WSLOT * z:WSLOT * z + 128], T.zin[:, 0:128], ["zin"], ["sz%d" % z])
     eqs, gcol = T.eqs, T.gcol
     for i in range(2):
-        ts(eqs[:, 64 * i:64 * i + 64], T.al[:, :], pf[:, 10 + i:11 + i], None, EQ, None, ["al", "g%d" % (i + 1)], ["eq%d" % i])
+        ts(eqs[:, 64 * i:64 * i + 64], T.al[:, :], float((me + 1 + i) % N), None, EQ, None, ["al"], ["eq%d" % i])
     for i in range(2):
         red(gcol[:, i:i + 1], eqs[:, 64 * i:64 * i + 64], ["eq%d" % i], ["gc%d" % i])
     for i in range(2):
         ts(T.bg[:, 32 * i:32 * i + 32], T.ones[:, :], gcol[:, i:i + 1], None, MUL, None, ["ones", "gc%d" % i], ["bg%d" % i])
     tr(T.tg[:, :], T.bg[:, :], ["bg0", "bg1"], ["tg"])
     for i in range(2):
-        red(T.gs[:, i:i + 1], T.tg[:, 32 * i:32 * i + 32], ["tg"], ["gs%d" % i])
+        red(T.gs[:, i:i + 1], T.tg[:, 36 * i + 4:32 * i + 32], ["tg"], ["gs%d" % i])
     lim = float(LATE + CAP + 1)
-    ts(T.ru[:, :], T.wa[:, :], T.gs[:, 0:1], lim, ADD, GE, ["wa", "gs0"], ["ru"])
-    ts(T.rv[:, :], T.wb[:, :], T.gs[:, 1:2], lim, ADD, GE, ["wb", "gs1"], ["rv"])
-    tt(T.r2[:, :], T.ru[:, :], T.rv[:, :], ADD, ["ru", "rv"], ["r2"])
+    ts(T.ka[:, :], T.wa[:, :], T.gs[:, 0:1], lim, ADD, LT, ["wa", "gs0"], ["ka"])
+    ts(T.kb[:, :], T.wb[:, :], T.gs[:, 1:2], lim, ADD, LT, ["wb", "gs1"], ["kb"])
+    tt(T.kk[:, :], T.ka[:, :], T.kb[:, :], MUL, ["ka", "kb"], ["kk"])
+    tt(T.r2[:, :], T.kk[:, :], mc, LT, ["kk", "mc"], ["r2"])
     red(T.tcol[:, 4:5], T.r2[:, :], ["r2"], ["tcol4"])
-    ts(T.b2[:, :], T.ones[:, :], T.tcol[:, 4:5], None, MUL, None, ["ones", "tcol4"], ["b2"])
-    tr(T.tot2[:, :], T.b2[:, :], ["b2"], ["tot2"])
-    tt(T.p2[:, 0:32], T.tot2[:, :], T.mlt[:, :], MUL, ["tot2", "mlt"], ["p2"])
-    tt(T.m16[:, :], T.tot2[:, 0:16], T.tot2[:, 16:32], ADD, ["tot2"], ["m16"])
-    red(bcol[:, 4:5], T.p2[:, :], ["p2", "p2z"], ["b2c"])
-    tt(T.m8[:, :], T.m16[:, 0:8], T.m16[:, 8:16], ADD, ["m16"], ["m8"])
-    ways = [out[0:4], out[4:6], out[6:8]]
-    moves = [(r, ways[(me - r) % N // 2 - 1], T.m8[:, (r - side - me - 1) % N:(r - side - me - 1) % N + 2],
-              T.ml[:, (me - r) % N - 2:(me - r) % N]) for r in far]
-    moves.append((mate, inn, T.m8[:, near - side:near - side + 2], T.mp[:, 0:2]))
-    fused(moves, "mar", "mars", ["m8"])
-    cnt["mar"] = cnt["mars"]
-    wr["mx"] = [("mar", cnt["mar"])]
+    ts(T.bm2[:, 0:32], T.mlt[:, :], T.tcol[:, 4:5], None, MUL, None, ["mlt", "tcol4"], ["bm4"])
+    ts(T.bm2[:, 32:64], T.ones[:, :], T.tcol[:, 4:5], None, MUL, None, ["ones", "tcol4"], ["bm5"])
+    tr(T.p2[:, 32:96], T.bm2[:, :], ["bm4", "bm5"], ["p2"])
+    red(bcol[:, 4:5], T.p2[:, 31:64], ["p2", "p2k"], ["b2c"])
+    tt(T.m16[:, :], T.p2[:, 64:80], T.p2[:, 80:96], ADD, ["p2"], ["m16"])
     scan(T.sc2[:, :], T.r2[:, :], 64, bcol[:, 4:5], ["r2", "b2c"], ["sc2"])
+    tt(T.m8[:, :], T.m16[:, 0:8], T.m16[:, 8:16], ADD, ["m16"], ["m8"])
+    send(range(N - 1), lambda z: T.m8[:, z:z + 1], lambda z: T.ml[:, N - 1 - z:N - z], ways, "mar", "mars", ["m8"])
+    cnt["mar"] = count_in
+    wr["mx"] = [("mar", count_in)]
     tt(T.d2[:, :], T.r2[:, :], T.sc2[:, :], MUL, ["r2", "sc2"], ["d2"])
-    tr(T.td2[:, :], T.d2[:, :], ["d2"], ["td2"])
-    scan(T.cs2[:, 8:72], T.td2[:, :], 64, 0.0, ["td2"], ["cs2"])
-    for i in range(2):
-        tt(T.s2[:, 8 * i:8 * i + 8], T.cs2[:, 15:72:8], T.cs2[:, 7:64:8], SUB, ["cs2", "cs2z"], ["s2%d" % i])
-    ts(T.x2[:, :], T.s2[:, :], 48, None, AND, None, ["s20", "s21"], ["x2"])
-    ts(T.v2[:, :], T.s2[:, :], 64, 6, AND, SHR, ["s20", "s21"], ["v2"])
-    tt(T.y2[:, :], T.s2[:, :], T.cy[:, :], ADD, ["s20", "s21", "cy"], ["y2"])
-    tt(T.y2b[:, :], T.y2[:, :], T.x2[:, :], ADD, ["x2", "y2"], ["y2b"])
-    tt(T.y2c[:, :], T.y2b[:, :], T.v2[:, :], MUL, ["y2b", "v2"], ["y2c"])
-    tt(T.y2d[:, :], T.y2c[:, :], T.y1b[:, :], ADD, ["y2c", "y1b"], ["y2d"])
-    cp(T.off2[:, :], T.y2d[:, :], ["y2d"], ["off2"])
-    cp(T.scat[:, 0:WIN].indirect(T.off2[:, 0:16]), T.vals[:, :], ["off2", "va0", "va1"], ["scat"])
+    tt(T.d1k[:, :], T.d1[:, :], T.kk[:, :], MUL, ["d1", "kk"], ["d1k"])
+    tt(T.dd1[:, :], T.d1k[:, :], T.d2[:, :], ADD, ["d1k", "d2"], ["dd1"])
+    tr(T.td[:, :], T.dd1[:, :], ["dd1"], ["td"])
+    scan(T.cs[:, 8:72], T.td[:, :], 64, 0.0, ["td"], ["cs"])
+    tt(T.s8[:, :], T.cs[:, 15:72:8], T.cs[:, 7:64:8], SUB, ["cs", "csz"], ["s8"])
+    ts(T.x8[:, :], T.s8[:, :], 112, None, AND, None, ["s8"], ["x8"])
+    tt(T.y8[:, :], T.s8[:, :], T.x8[:, :], ADD, ["s8", "x8"], ["y8"])
+    cp(T.off[:, 0:8], T.y8[:, :], ["y8"], ["of0"])
+    ts(T.off[:, 8:16], T.y8[:, :], 16.0, None, ADD, None, ["y8"], ["of1"])
+    cp(T.scat[:, 0:WIN].indirect(T.off[:, 0:16]), T.vals[:, :], ["of0", "of1", "va0", "va1"] + ["sz%d" % z for z in range(N)], ["scat"])
 
     def lists_of(za, zb):
         key = "so%d" % za
-        tr(T.tw[:, 128 * za:128 * zb], T.scat[:, 64 + 128 * za:64 + 128 * zb], ["scat"], ["tw%d" % za])
-        tt(T["self"][:, 4 * za:4 * zb], T.tw[:, 128 * za:128 * zb:32], T.tw[:, 128 * za + 16:128 * zb:32], ADD, ["tw%d" % za], ["sf%d" % za])
+        for z in range(za, zb):
+            tr(T.tw[:, 128 * z:128 * z + 128], T.scat[:, WSLOT * z:WSLOT * z + 128], ["scat"], ["tw%d" % z])
+        tt(T["self"][:, 4 * za:4 * zb], T.tw[:, 128 * za:128 * zb:32], T.tw[:, 128 * za + 16:128 * zb:32], ADD,
+           ["tw%d" % z for z in range(za, zb)], ["sf%d" % za])
         cp(T.so[:, 4 * za:4 * zb], T["self"][:, 4 * za:4 * zb], ["sf%d" % za], [key])
         return key
 
     def pick(oq, os_, n, iq, is_, m, off, n0, reads, writes):
         op("v", V.tensor_copy, (oq[:, n0:n0 + n].bitcast(dt.uint32), iq[:, 0:m].bitcast(dt.uint32).indirect(off)), reads, [writes + "q"])
         op("s", g.scalar.activation, (os_[:, n0:n0 + n], is_[:, 0:m].indirect(off), COPY), reads, [writes + "s"])
-
-    def make(zs, sq, sp, key):
-        za, zb = zs[0], zs[-1] + 1
-        k = lists_of(za, zb)
-        pick(sq, sp, SLOT * (zb - za), T.xq, T.xs, TOK, T.so[:, 4 * za:4 * zb], 0, [k, "xq"], key)
 
     def columns(call, sq, sp, key):
         kind, zs, n, engines = call
@@ -353,15 +326,13 @@ def rank_program(g, core, T, topo):
             return T.land[:, c:c + n].bitcast(dt.uint8) if kind == "q" else T.lsc[:, c:c + n]
         send(zs, src, dst, engines, "dat", "dats", [key + kind])
 
-    make(calls[0][1], T.sq1, T.sp1, "w1")
-    columns(calls[0], T.sq1, T.sp1, "w1")
-    columns(calls[1], T.sq1, T.sp1, "w1")
-    make(calls[2][1], T.sq2, T.sp2, "w2")
-    columns(calls[2], T.sq2, T.sp2, "w2")
-    fused([(mate, inn, T.ml[:, 0:6], T.mf[:, 0:6])], "mfw", "mars", ["mx"])
-    columns(calls[3], T.sq2, T.sp2, "w2")
-    cnt["mfw"] = len(inn)
-    wr["mf"] = [("mfw", cnt["mfw"])]
+    for i, (sq, sp) in enumerate(((T.sq1, T.sp1), (T.sq2, T.sp2), (T.sq3, T.sp3))):
+        zs, key = calls[2 * i][1], "w%d" % i
+        za, zb = zs[0], zs[-1] + 1
+        k = lists_of(za, zb)
+        pick(sq, sp, SLOT * (zb - za), T.xq, T.xs, TOK, T.so[:, 4 * za:4 * zb], 0, [k, "xq"], key)
+        columns(calls[2 * i], sq, sp, key)
+        columns(calls[2 * i + 1], sq, sp, key)
     k = lists_of(N - 1, N)
     pick(T.land, T.lsc, SLOT, T.xq, T.xs, TOK, T.so[:, 4 * (N - 1):4 * N], 0, [k, "xq"], "own")
 
@@ -371,38 +342,38 @@ def rank_program(g, core, T, topo):
     tr(T.t3[:, :], T.b3[:, :], ["b3"], ["t3"])
     tt(T.n16[:, :], T.t3[:, 0:32:2], T.t3[:, 1:32:2], ADD, ["t3"], ["n16"])
     tt(T.n8[:, :], T.n16[:, 0:16:2], T.n16[:, 1:16:2], ADD, ["n16"], ["n8"])
+    pp, bb, dd, tm, jj = T.pp, T.bb, T.dd, T.tm, T.jj
     scan(T.n8s[:, :], T.n8[:, :], 8, 0.0, ["n8"], ["n8s"])
-    pp, bb = T.pp, T.bb
+    tt(bb[:, 8:16], bb[:, 0:8], T.n8[:, :], ADD, ["bb0", "n8"], ["bb8"])
     ts(pp[:, 1:9], T.n8s[:, :], float(CAP), None, MIN, None, ["n8s"], ["pp1"])
-    cp(bb[:, 0:8], T.k64[:, :], ["k64"], ["bb0"])
-    tt(bb[:, 8:16], T.k64[:, :], T.n8[:, :], ADD, ["k64", "n8"], ["bb8"])
-    ts(T.jj[:, :], T.j0[:, :], ic, None, ADD, None, ["j0", "pf"], ["jj"])
+    tt(T.bd[:, :], bb[:, 9:17], bb[:, 8:16], SUB, ["bb8", "bb16"], ["bd"])
+    tt(T.de[:, 0:9], bb[:, 0:9], pp[:, 0:9], SUB, ["bb0", "bb8", "pp0", "pp1"], ["de"])
+    tt(pp[:, 9:10], pp[:, 8:9], T.m8[:, 7:8], ADD, ["pp1", "m8"], ["pp9"])
+    tt(dd[:, 9:10], T.bd[:, 0:1], T.m8[:, 7:8], SUB, ["bd", "m8"], ["dd9"])
+    tt(dd[:, 1:9], T.de[:, 1:9], T.de[:, 0:8], SUB, ["de"], ["dd1e"])
 
-    def terms(lo):
-        a, b, d, c = 10 * lo, 5 * lo, 5 * lo, 20 * lo
-        for q in range(lo + 1, lo + 9):
-            ts(T.tm[:, 20 * (q - 1):20 * q], T.jj[:, :], pp[:, q:q + 1], T.dd[:, q - 1:q], GE, MUL, ["jj", "pp1", "pp9", "dd%d" % lo], ["tm%d" % q])
-        tt(T.t80[:, a:a + 80], T.tm[:, c:c + 80], T.tm[:, c + 80:c + 160], ADD, ["tm%d" % q for q in range(lo + 1, lo + 9)], ["t80%d" % lo])
-        tt(T.t40[:, b:b + 40], T.t80[:, a:a + 40], T.t80[:, a + 40:a + 80], ADD, ["t80%d" % lo], ["t40%d" % lo])
-        tt(T.t20[:, d:d + 20], T.t40[:, b:b + 20], T.t40[:, b + 20:b + 40], ADD, ["t40%d" % lo], ["t20%d" % lo])
-        x, key = (T.jj[:, :], "jj") if lo == 0 else (T.t20[:, 20:40], "sum0")
-        tt(T.t20[:, d + 20:d + 40], T.t20[:, d:d + 20], x, ADD, ["t20%d" % lo, key], ["sum%d" % lo])
+    def term(q, block, keys):
+        ts(tm[:, 20 * block:20 * block + 20], jj[:, :], pp[:, q:q + 1], dd[:, q:q + 1], GE, MUL, ["jj"] + keys, ["tm%d" % block])
 
-    tt(T.de[:, 0:9], bb[:, 0:9], pp[:, 0:9], SUB, ["bb0", "bb8", "pp0", "pp1"], ["de0"])
-    tt(T.dd[:, 0:8], T.de[:, 1:9], T.de[:, 0:8], SUB, ["de0"], ["dd0"])
-    terms(0)
+    def total(b, i):
+        c, d, e = 20 * b, 80 * i, 40 * i
+        tt(T.t80[:, d:d + 80], tm[:, c:c + 80], tm[:, c + 80:c + 160], ADD, ["tm%d" % k for k in range(b, b + 8)], ["t80%d" % i])
+        tt(T.t40[:, e:e + 40], T.t80[:, d:d + 40], T.t80[:, d + 40:d + 80], ADD, ["t80%d" % i], ["t40%d" % i])
+        tt(T.t20[:, e:e + 20], T.t40[:, e:e + 20], T.t40[:, e + 20:e + 40], ADD, ["t40%d" % i], ["t20%d" % i])
+
+    ts(T.t20[:, 20:40], jj[:, :], pp[:, 9:10], dd[:, 9:10], GE, MUL, ["jj", "pp9", "dd9"], ["t9"])
+    for q in range(1, 9):
+        term(q, q - 1, ["pp1", "dd1e"])
+    tt(T.t20[:, 60:80], T.t20[:, 20:40], jj[:, :], ADD, ["t9", "jj"], ["t9j"])
+    total(0, 0)
+    tt(tm[:, 300:320], T.t20[:, 0:20], T.t20[:, 60:80], ADD, ["t200", "t9j"], ["tm15"])
     op("v", V.quantize_mx, (T.wq[:, :], T.wsc[:, :], T["win"][:, :]), ["win"], ["wq"])
-
-    kn, kf = (mate - me) % N, (mate - me + 2) % N
-    cp(T.m9[:, 0:1], T.m8[:, N - 1:N], ["m8"], ["m90"])
-    cp(T.m9[:, 2:8:2], T.ml[:, side:6:2], ["mx"], ["m91"])
-    cp(T.m9[:, kn:kn + 1], T.mp[:, 1 - side:2 - side], ["mx"], ["m92"])
-    cp(T.m9[:, kf:kf + 5:2], T.mf[:, side:6:2], ["mf"], ["m93"])
-    scan(pp[:, 9:17], T.m9[:, :], 8, pp[:, 8:9], ["m90", "m91", "m92", "m93", "pp1"], ["pp9"])
-    tt(T.de[:, 9:17], bb[:, 9:17], pp[:, 9:17], SUB, ["bb8", "bb16", "pp9"], ["de9"])
-    tt(T.dd[:, 8:16], T.de[:, 9:17], T.de[:, 8:16], SUB, ["de9", "de0"], ["dd8"])
-    terms(8)
-    ts(T.fo[:, :], T.t20[:, 60:80], float(ZERO + NZ - 1), None, MIN, None, ["sum8"], ["fo"])
+    op("v", V.tensor_tensor_scan, (pp[:, 10:17], T.ml[:, 1:8], T.z64[:, 0:7], pp[:, 9:10], ADD, ADD), ["mx", "z64", "pp9"], ["pp10"])
+    tt(dd[:, 10:17], T.bd[:, 1:8], T.ml[:, 1:8], SUB, ["bd", "mx"], ["dd10"])
+    for q in range(10, 17):
+        term(q, q - 2, ["pp10", "dd10"])
+    total(8, 1)
+    ts(T.fo[:, :], T.t20[:, 40:60], float(ZERO + NZ - 1), None, MIN, None, ["t201"], ["fo"])
 
     cnt["dat"] = data_in
     wr["dx"] = [("dat", data_in)]
@@ -410,17 +381,19 @@ def rank_program(g, core, T, topo):
     cuts = ((0, 192), (192, ROOM))
     for i, (a, b) in enumerate(cuts):
         pick(T.fq, T.fs, b - a, T.land, T.lsc, ZERO + NZ, T.fo[:, a // 16:b // 16], a, got, "f%d" % i)
-    pieces = [(0, a, b, 512 * O * (i > 0), ["f%dq" % i, "f%ds" % i]) for i, (a, b) in enumerate(cuts)]
-    pieces += [(o, 0, ROOM, 512 * o, ["f0q", "f0s", "f1q", "f1s"]) for o in range(1, O)]
+    first, every = ["f0q", "f0s"], ["f0q", "f0s", "f1q", "f1s"]
+    pieces = [(0, 0, 192, 0, first), (0, 192, ROOM, O, ["f1q", "f1s"])]
+    pieces += [(o, 0, ROOM, o, every) for o in range(1, O - 1)]
+    pieces += [(O - 1, 0, ROOM // 2, O - 1, every), (O - 1, ROOM // 2, ROOM, O + 1, every)]
     for i, (o, a, b, p, keys) in enumerate(pieces):
-        op("t", g.tensor.matmul_mx, (T.acc[:, p:p + b - a], T.wq[:, 128 * o:128 * o + 128], T.wsc[:, 128 * o:128 * o + 128],
+        op("t", g.tensor.matmul_mx, (T.acc[:, 512 * p:512 * p + b - a], T.wq[:, 128 * o:128 * o + 128], T.wsc[:, 128 * o:128 * o + 128],
                                      T.fq[:, a:b], T.fs[:, a:b], True, True), ["wq"] + keys, ["acc%d" % i])
     for i, (o, a, b, p, keys) in enumerate(pieces):
-        src, dst = T.acc[:, p:p + b - a], T.yo[:, ROOM * o + a:ROOM * o + b]
+        src, dst = T.acc[:, 512 * p:512 * p + b - a], T.yo[:, ROOM * o + a:ROOM * o + b]
         if i % 2 == 0:
             cp(dst, src, ["acc%d" % i], ["yo%d" % i])
         else:
-            op("s", g.scalar.activation, (dst, src, COPY), ["acc%d" % i], ["yo%d" % i])
+            act(dst, src, ["acc%d" % i], ["yo%d" % i])
         if b == ROOM:
             dma("y", "dy", T.y[:, ROOM * o:ROOM * o + ROOM], T.yo[:, ROOM * o:ROOM * o + ROOM],
                 ["yo%d" % j for j in range(len(pieces)) if pieces[j][0] == o], ["yout"], more=True)

@@ -7,6 +7,7 @@ ZERO = N * SLOT
 NZ = 128
 WSLOT = 256
 WIN = N * WSLOT
+HIGH = 2 * WIN
 LATE = 400
 
 
@@ -21,57 +22,51 @@ SCRATCH = {
     "xq": _sb(TOK, MX), "xs": _sb(TOK, U8), "wq": _sb(128 * O, MX), "wsc": _sb(128 * O, U8),
     "ra": _sb(128, F32), "ca": _sb(128, F32), "rb": _sb(64, F32), "cb": _sb(64, F32), "e64": _sb(64, I32), "ec": _sb(64, I32),
     "l4": _sb(4, I32), "l64": _sb(4, U16), "meq": _sb(32, F32), "mgt": _sb(32, F32), "mlt": _sb(32, F32),
-    "v128": _sb(128, B16), "vals": _sb(256, B16), "j0": _sb(20, I32), "jj": _sb(20, F32), "ones": _sb(32, F32), "z64": _sb(64, F32),
+    "v128": _sb(128, B16), "vals": _sb(128, B16), "j0": _sb(20, I32), "jj": _sb(20, F32), "ones": _sb(32, F32), "z64": _sb(64, F32),
     "pre": _sb(256, B16), "mt": _sb(256, B16), "tcol": _sb(8, F32), "bm": _sb(128, F32), "tb": _sb(168, F32), "bcol": _sb(8, F32),
     "sc1": _sb(64, F32), "d1": _sb(64, F32), "sca": _sb(64, F32), "scb": _sb(64, F32), "wa": _sb(64, F32), "wb": _sb(64, F32),
+    "qa": _sb(64, B16), "qb": _sb(64, B16), "td1": _sb(64, F32), "cs1": _sb(72, F32), "s1": _sb(8, F32),
     "al": _sb(64, I32), "eqs": _sb(192, B16), "gcol": _sb(8, F32), "bg": _sb(64, F32), "tg": _sb(64, F32), "gs": _sb(8, F32),
-    "ka": _sb(64, B16), "kb": _sb(64, B16), "kk": _sb(64, B16), "r2": _sb(64, B16), "bm2": _sb(64, F32), "p2": _sb(96, F32),
-    "m16": _sb(16, F32), "m8": _sb(8, F32), "sc2": _sb(64, F32), "d2": _sb(64, F32), "d1k": _sb(64, F32), "dd1": _sb(64, F32),
-    "td": _sb(64, F32), "cs": _sb(72, F32), "s8": _sb(8, I32), "x8": _sb(8, I32), "y8": _sb(8, I32), "off": _sb(16, U16),
-    "scat": _sb(WIN, B16), "tw": _sb(1024, B16), "self": _sb(32, F32), "so": _sb(32, U16),
+    "fa": _sb(64, B16), "fb": _sb(64, B16), "r2": _sb(64, B16), "cum": _sb(64, F32), "bm2": _sb(64, F32), "p2": _sb(96, F32),
+    "m16": _sb(16, F32), "m8": _sb(8, F32), "d2c": _sb(64, F32), "d2b": _sb(64, F32), "tdc": _sb(64, F32), "tdb": _sb(64, F32),
+    "cs2": _sb(72, F32), "s2": _sb(8, F32), "s8": _sb(8, I32), "x8": _sb(8, I32), "u8": _sb(8, I32), "y8": _sb(8, I32), "off": _sb(8, U16),
+    "scat": _sb(WIN + 32, B16), "twa": _sb(1024, B16), "twb": _sb(1024, B16), "half": _sb(64, F32), "self": _sb(32, F32), "so": _sb(32, U16),
     "sq1": _sb(2 * SLOT, MX), "sp1": _sb(2 * SLOT, U8), "sq2": _sb(4 * SLOT, MX), "sp2": _sb(4 * SLOT, U8),
     "sq3": _sb(SLOT, MX), "sp3": _sb(SLOT, U8),
     "land": _sb(ZERO + NZ, MX), "lsc": _sb(ZERO + NZ, U8),
     "b3": _sb(32, F32), "t3": _sb(32, F32), "n16": _sb(16, F32), "n8": _sb(8, F32), "n8s": _sb(8, F32), "pp": _sb(24, F32), "bb": _sb(24, F32),
-    "de": _sb(16, F32), "dd": _sb(24, F32), "bd": _sb(8, F32), "tm": _sb(320, F32), "t80": _sb(160, F32), "t40": _sb(80, F32), "t20": _sb(80, F32),
-    "ml": _sb(8, F32), "fo": _sb(20, U16), "fq": _sb(ROOM, MX), "fs": _sb(ROOM, U8),
-    "acc": ("psum", [128, 512 * (O + 2)], F32), "yo": _sb(ROOM * O, F32),
+    "de": _sb(24, F32), "dd": _sb(24, F32), "tm": _sb(320, F32), "t160": _sb(160, F32), "t80": _sb(80, F32), "t40": _sb(40, F32),
+    "t20": _sb(40, F32), "ml": _sb(8, F32), "fo": _sb(20, U16), "fq": _sb(ROOM, MX), "fs": _sb(ROOM, U8),
+    "acc": ("psum", [128, 512 * 2 * O], F32), "yo": _sb(ROOM * O, F32),
 }
 SEMAPHORES = ["cv", "cs", "cg", "ct", "dl0", "dc1", "dc2", "dx", "dw", "dal", "dy",
               "lst", "lsts", "mar", "mars", "dat", "dats"]
 
-ADD, SUB, MUL, MIN = AluOpType.add, AluOpType.subtract, AluOpType.mult, AluOpType.min
-GE, GT, LT, EQ = AluOpType.is_ge, AluOpType.is_gt, AluOpType.is_lt, AluOpType.is_equal
+ADD, SUB, MUL, MIN, MAX = AluOpType.add, AluOpType.subtract, AluOpType.mult, AluOpType.min, AluOpType.max
+GE, GT, EQ = AluOpType.is_ge, AluOpType.is_gt, AluOpType.is_equal
 AND = AluOpType.bitwise_and
 COPY, IDENT = ActivationFunctionType.Copy, ActivationFunctionType.Identity
 
 
 def plan(me, cores, topo):
     core = cores[me]
-    dst = [cores[(me + 1 + z) % N] for z in range(N - 1)]
-    near = [z for z in range(N - 1) if topo.chip(dst[z]) == topo.chip(core)]
-    far = [z for z in range(N - 1) if z not in near]
-    out = topo.engines(core, dst[far[0]])
-    inn = [e for e in topo.engines(core, dst[near[0]]) if e not in out]
+    mate = [r for r in range(N) if r != me and topo.chip(cores[r]) == topo.chip(core)][0]
+    rot = 2 if mate == (me + 1) % N else 1
+    near = (mate - me - rot) % N
+    own = (N - rot) % N
+    far = [z for z in range(N) if z not in (near, own)]
+    out = topo.engines(core, cores[(me + rot + far[0]) % N])
+    inn = [e for e in topo.engines(core, cores[mate]) if e not in out]
 
     def deal(zs):
         k = len(out) // len(zs)
         return {z: out[k * i:k * i + k] for i, z in enumerate(zs)}
 
-    some = far[:2] if near[0] == 0 else far[-2:]
-    rest = [z for z in far if z not in some]
     calls = []
-    for zs, e in ((some, deal(some)), (rest, deal(rest)), (near, {z: inn for z in near})):
-        n = SLOT if 0 in zs or 1 in zs else BOTH
+    for zs, e in ((far[:2], deal(far[:2])), (far[2:], deal(far[2:])), ([near], {near: inn})):
+        n = SLOT if any(rot + z in (1, 2) or rot + z == N + 1 for z in zs) else BOTH
         calls += [("q", zs, n, e), ("s", zs, n, e)]
-    extra = len(out) - len(far)
-    counts, at = {}, 0
-    for i, z in enumerate(far):
-        k = 2 if i < extra else 1
-        counts[z] = out[at:at + k]
-        at += k
-    counts.update({z: inn for z in near})
-    return calls, counts, out[::4]
+    return rot, near, own, calls, out[::4]
 
 
 def rank_program(g, core, T, topo):
@@ -79,7 +74,7 @@ def rank_program(g, core, T, topo):
     if me is None:
         return
     cores = [int(c) for c in T.cores]
-    calls, ways, few = plan(me, cores, topo)
+    rot, near, own, calls, few = plan(me, cores, topo)
     queue = {"v": g.vector, "s": g.scalar, "t": g.tensor, "g": g, "y": g.sync}
     cnt, seen, wr, rd = {}, {}, {}, {}
 
@@ -145,8 +140,11 @@ def rank_program(g, core, T, topo):
     def tr(out, a, reads, writes):
         op("v", V.transpose, (out, a), reads, writes)
 
+    def scan2(out, a, b, init, reads, writes):
+        op("v", V.tensor_tensor_scan, (out, a, b, init, ADD, ADD), reads, writes)
+
     def scan(out, a, n, init, reads, writes):
-        op("v", V.tensor_tensor_scan, (out, a, T.z64[:, 0:n], init, ADD, ADD), reads + ["z64"], writes)
+        scan2(out, a, T.z64[:, 0:n], init, reads + ["z64"], writes)
 
     def fill(ap, val, key):
         op("v", V.memset, (ap, val), [], [key])
@@ -158,9 +156,12 @@ def rank_program(g, core, T, topo):
     def act(out, a, reads, writes):
         op("s", g.scalar.activation, (out, a, COPY), reads, writes)
 
-    def at(r):
-        rid, pid, _ = topo.addr(cores[r])
+    def at(z):
+        rid, pid, _ = topo.addr(cores[(me + rot + z) % N])
         return DstId(rid=rid, pnc=pid)
+
+    def place(z):
+        return (N - rot - z) % N
 
     def mask(engines):
         m = 0
@@ -170,15 +171,16 @@ def rank_program(g, core, T, topo):
 
     def send(zs, src, dst, engines, sem, lsem, reads):
         before("g", reads, [])
-        g.remote_dma_fused([RemoteDMATransfer(dst_ids=[at((me + 1 + z) % N)], dma_engine_mask=mask(engines[z]),
+        g.remote_dma_fused([RemoteDMATransfer(dst_ids=[at(z)], dma_engine_mask=mask(engines[z]),
                                               remote_sem=T.sem[sem], src=src(z), dst=dst(z)) for z in zs], local_sem=T.sem[lsem])
         cnt[lsem] = cnt.get(lsem, 0) + sum(len(engines[z]) for z in zs)
 
     data_in = list_in = count_in = 0
     for k in range(1, N):
-        c2, w2, f2 = plan((me + k) % N, cores, topo)
-        data_in += sum(len(e[N - 1 - k]) for _, zs, _, e in c2 if N - 1 - k in zs)
-        count_in += len(w2[N - 1 - k])
+        r2, _, _, c2, f2 = plan((me + k) % N, cores, topo)
+        z = (N - k - r2) % N
+        data_in += sum(len(e[z]) for _, zs, _, e in c2 if z in zs)
+        count_in += sum(len(e[z]) for kind, zs, _, e in c2 if z in zs and kind == "q")
         list_in += len(f2)
 
     dma("y", "dl0", T.lists[0], T.c1[:, :], [], ["l0"])
@@ -194,11 +196,11 @@ def rank_program(g, core, T, topo):
     iota(ra[:, 0:32], "ra0", [[0, 4], [1, 8]], 0, flag=True)
     iota(ra[:, 32:64], "ra1", [[1, 4], [0, 8]], 0, flag=True)
     iota(ra[:, 96:128], "ra3", [[0, 4], [WSLOT, 8]], -1, flag=True)
-    iota(T.e64[:, :], "e64", [[1, 64]], me + 1)
+    iota(T.e64[:, :], "e64", [[1, 64]], me + rot)
+    others = [z for z in range(N) if z != own]
     before("g", ["l0"], [])
-    g.remote_dma_fused([RemoteDMATransfer(dst_ids=[at((me + 1 + z) % N) for z in range(N - 1)], dma_engine_mask=mask(few),
-                                          remote_sem=T.sem["lst"], srcs=[T.lists[0]],
-                                          dsts=[T.lists[N - 1 - z] for z in range(N - 1)])], local_sem=T.sem["lsts"])
+    g.remote_dma_fused([RemoteDMATransfer(dst_ids=[at(z) for z in others], dma_engine_mask=mask(few), remote_sem=T.sem["lst"],
+                                          srcs=[T.lists[0]], dsts=[T.lists[place(z)] for z in others])], local_sem=T.sem["lsts"])
     cnt["lsts"] = len(few)
     iota(T.zin[:, :], "zin", [[0, 4 * NZ]], 0, flag=True)
     iota(rb[:, 32:64], "rb1", [[16, 2], [0, 16]], 0, flag=True)
@@ -209,7 +211,8 @@ def rank_program(g, core, T, topo):
 
     fill(T.ones[:, :], 1.0, "ones")
     fill(T.z64[:, :], 0.0, "z64")
-    fill(T.cs[:, 0:8], 0.0, "csz")
+    fill(T.cs1[:, 0:8], 0.0, "cs1z")
+    fill(T.cs2[:, 0:8], 0.0, "cs2z")
     fill(T.pp[:, 0:1], 0.0, "pp0")
     fill(T.bb[:, 16:17], float(ZERO), "bb16")
     tr(T.ca[:, :], ra[:, :], ["ra0", "ra1", "ra2", "ra3"], ["ca"])
@@ -220,7 +223,7 @@ def rank_program(g, core, T, topo):
     ts(T.mgt[:, :], ra[:, 32:64], hc, None, GT, None, ["ra1", "ca"], ["mgt"])
     tt(T.mlt[:, :], T.meq[:, :], T.mgt[:, :], MUL, ["meq", "mgt"], ["mlt"])
     act(T.tb[:, 31:32], sc, ["ca"], ["tb0"])
-    act(T.tb[:, 160:161], sc, ["ca"], ["tb1"])
+    op("s", g.scalar.activation, (T.tb[:, 160:161], sc, IDENT, float(HIGH)), ["ca"], ["tb1"])
 
     l64 = T.l64[:, 0:4]
     c1w, c2w = T.ct[:, 0:16].indirect(l64), T.ct[:, 16:32].indirect(l64)
@@ -238,6 +241,7 @@ def rank_program(g, core, T, topo):
     ts(T.bm[:, 64:96], T.mlt[:, :], T.tcol[:, 2:3], LATE / 32, MUL, ADD, ["mlt", "tcol2"], ["bm2"])
     ts(T.bm[:, 96:128], T.meq[:, :], T.tcol[:, 0:1], None, MUL, None, ["meq", "tcol0"], ["bm3"])
     tr(T.tb[:, 32:160], T.bm[:, :], ["bm0", "bm1", "bm2", "bm3"], ["tb"])
+    tt(T.qa[:, :], ma, mc, MUL, ["mt", "mc"], ["qa"])
     bcol = T.bcol
     red(bcol[:, 0:1], T.tb[:, 31:64], ["tb", "tb0"], ["b1"])
     red(bcol[:, 1:2], T.tb[:, 64:96], ["tb"], ["ba"])
@@ -247,22 +251,25 @@ def rank_program(g, core, T, topo):
     scan(T.sca[:, :], ma, 64, bcol[:, 1:2], ["mt", "ba"], ["sca"])
     scan(T.scb[:, :], mb, 64, bcol[:, 2:3], ["mt", "bq"], ["scb"])
     tt(T.d1[:, :], m1, T.sc1[:, :], MUL, ["mt", "sc1"], ["d1"])
-    tt(T.wa[:, :], ma, T.sca[:, :], MUL, ["mt", "sca"], ["wa"])
-    tt(T.wb[:, :], mb, T.scb[:, :], MUL, ["mt", "scb"], ["wb"])
-    op("v", V.quantize_mx, (T.xq[:, :], T.xs[:, :], T.xin[:, :]), ["xin"], ["xq"])
+    tt(T.qb[:, :], mb, mc, MUL, ["mt", "mc"], ["qb"])
+    tr(T.td1[:, :], T.d1[:, :], ["d1"], ["td1"])
+    tt(T.wa[:, :], T.qa[:, :], T.sca[:, :], MUL, ["qa", "sca"], ["wa"])
+    tt(T.wb[:, :], T.qb[:, :], T.scb[:, :], MUL, ["qb", "scb"], ["wb"])
+    scan(T.cs1[:, 8:72], T.td1[:, :], 64, 0.0, ["td1"], ["cs1"])
     tr(T.cb[:, :], rb[:, :], ["rb0", "rb1"], ["cb"])
-    ts(T.jj[:, :], T.j0[:, :], T.cb[:, 0:1], None, ADD, None, ["j0", "cb"], ["jj"])
+    tt(T.s1[:, :], T.cs1[:, 15:72:8], T.cs1[:, 7:64:8], SUB, ["cs1", "cs1z"], ["s1"])
+    op("v", V.quantize_mx, (T.xq[:, :], T.xs[:, :], T.xin[:, :]), ["xin"], ["xq"])
     op("v", V.quantize_mx, (T.land[:, ZERO:ZERO + NZ], T.lsc[:, ZERO:ZERO + NZ], T.zin[:, :]), ["zin"], ["zq"])
+    ts(T.jj[:, :], T.j0[:, :], T.cb[:, 0:1], None, ADD, None, ["j0", "cb"], ["jj"])
 
     cnt["lst"] = list_in
     wr["lx"] = [("lst", list_in)]
     for b in range(4):
         dma("ys"[b % 2], "dal", T.al[32 * b:32 * b + 32, 0:64], T.lists[:, :, :], ["lx", "l0"], ["al"], more=True)
     dma("y", "dw", T["win"][:, :], T.w[:, :], ["lx"], ["win"])
-    for i in range(2):
-        op("s", g.scalar.activation, (T.vals[:, 128 * i:128 * i + 128], T.v128[:, :], IDENT, T.cb[:, 32:33]), ["v128", "cb"], ["va%d" % i])
+    op("s", g.scalar.activation, (T.vals[:, :], T.v128[:, :], IDENT, T.cb[:, 32:33]), ["v128", "cb"], ["vals"])
     for z in range(N):
-        act(T.scat[:, WSLOT * z:WSLOT * z + 128], T.zin[:, 0:128], ["zin"], ["sz%d" % z])
+        act(T.scat[:, WSLOT * z + 16:WSLOT * z + 160], T.zin[:, 0:144], ["zin"], ["sz%d" % z])
     eqs, gcol = T.eqs, T.gcol
     for i in range(2):
         ts(eqs[:, 64 * i:64 * i + 64], T.al[:, :], float((me + 1 + i) % N), None, EQ, None, ["al"], ["eq%d" % i])
@@ -274,40 +281,63 @@ def rank_program(g, core, T, topo):
     for i in range(2):
         red(T.gs[:, i:i + 1], T.tg[:, 36 * i + 4:32 * i + 32], ["tg"], ["gs%d" % i])
     lim = float(LATE + CAP + 1)
-    ts(T.ka[:, :], T.wa[:, :], T.gs[:, 0:1], lim, ADD, LT, ["wa", "gs0"], ["ka"])
-    ts(T.kb[:, :], T.wb[:, :], T.gs[:, 1:2], lim, ADD, LT, ["wb", "gs1"], ["kb"])
-    tt(T.kk[:, :], T.ka[:, :], T.kb[:, :], MUL, ["ka", "kb"], ["kk"])
-    tt(T.r2[:, :], T.kk[:, :], mc, LT, ["kk", "mc"], ["r2"])
-    red(T.tcol[:, 4:5], T.r2[:, :], ["r2"], ["tcol4"])
-    ts(T.bm2[:, 0:32], T.mlt[:, :], T.tcol[:, 4:5], None, MUL, None, ["mlt", "tcol4"], ["bm4"])
-    ts(T.bm2[:, 32:64], T.ones[:, :], T.tcol[:, 4:5], None, MUL, None, ["ones", "tcol4"], ["bm5"])
+    ts(T.fa[:, :], T.wa[:, :], T.gs[:, 0:1], lim, ADD, GE, ["wa", "gs0"], ["fa"])
+    ts(T.fb[:, :], T.wb[:, :], T.gs[:, 1:2], lim, ADD, GE, ["wb", "gs1"], ["fb"])
+    scan2(T.cum[:, :], T.fa[:, :], T.fb[:, :], 0.0, ["fa", "fb"], ["cum"])
+    tt(T.r2[:, :], T.fa[:, :], T.fb[:, :], ADD, ["fa", "fb"], ["r2"])
+    ts(T.bm2[:, 0:32], T.mlt[:, :], T.cum[:, 63:64], None, MUL, None, ["mlt", "cum"], ["bm4"])
+    ts(T.bm2[:, 32:64], T.ones[:, :], T.cum[:, 63:64], None, MUL, None, ["ones", "cum"], ["bm5"])
+    tt(T.d2c[:, :], T.r2[:, :], T.cum[:, :], MUL, ["r2", "cum"], ["d2c"])
     tr(T.p2[:, 32:96], T.bm2[:, :], ["bm4", "bm5"], ["p2"])
+    tr(T.tdc[:, :], T.d2c[:, :], ["d2c"], ["tdc"])
     red(bcol[:, 4:5], T.p2[:, 31:64], ["p2", "p2k"], ["b2c"])
     tt(T.m16[:, :], T.p2[:, 64:80], T.p2[:, 80:96], ADD, ["p2"], ["m16"])
-    scan(T.sc2[:, :], T.r2[:, :], 64, bcol[:, 4:5], ["r2", "b2c"], ["sc2"])
+    ts(T.d2b[:, :], T.r2[:, :], bcol[:, 4:5], None, MUL, None, ["r2", "b2c"], ["d2b"])
     tt(T.m8[:, :], T.m16[:, 0:8], T.m16[:, 8:16], ADD, ["m16"], ["m8"])
-    send(range(N - 1), lambda z: T.m8[:, z:z + 1], lambda z: T.ml[:, N - 1 - z:N - z], ways, "mar", "mars", ["m8"])
+    for c in (0, 2, 4):
+        send(calls[c][1], lambda z: T.m8[:, z:z + 1], lambda z: T.ml[:, place(z):place(z) + 1], calls[c][3], "mar", "mars", ["m8"])
     cnt["mar"] = count_in
     wr["mx"] = [("mar", count_in)]
-    tt(T.d2[:, :], T.r2[:, :], T.sc2[:, :], MUL, ["r2", "sc2"], ["d2"])
-    tt(T.d1k[:, :], T.d1[:, :], T.kk[:, :], MUL, ["d1", "kk"], ["d1k"])
-    tt(T.dd1[:, :], T.d1k[:, :], T.d2[:, :], ADD, ["d1k", "d2"], ["dd1"])
-    tr(T.td[:, :], T.dd1[:, :], ["dd1"], ["td"])
-    scan(T.cs[:, 8:72], T.td[:, :], 64, 0.0, ["td"], ["cs"])
-    tt(T.s8[:, :], T.cs[:, 15:72:8], T.cs[:, 7:64:8], SUB, ["cs", "csz"], ["s8"])
+    tr(T.tdb[:, :], T.d2b[:, :], ["d2b"], ["tdb"])
+    scan2(T.cs2[:, 8:72], T.tdc[:, :], T.tdb[:, :], 0.0, ["tdc", "tdb"], ["cs2"])
+    tt(T.s2[:, :], T.cs2[:, 15:72:8], T.cs2[:, 7:64:8], SUB, ["cs2", "cs2z"], ["s2"])
+    tt(T.s8[:, :], T.s1[:, :], T.s2[:, :], MAX, ["s1", "s2"], ["s8"])
     ts(T.x8[:, :], T.s8[:, :], 112, None, AND, None, ["s8"], ["x8"])
-    tt(T.y8[:, :], T.s8[:, :], T.x8[:, :], ADD, ["s8", "x8"], ["y8"])
-    cp(T.off[:, 0:8], T.y8[:, :], ["y8"], ["of0"])
-    ts(T.off[:, 8:16], T.y8[:, :], 16.0, None, ADD, None, ["y8"], ["of1"])
-    cp(T.scat[:, 0:WIN].indirect(T.off[:, 0:16]), T.vals[:, :], ["of0", "of1", "va0", "va1"] + ["sz%d" % z for z in range(N)], ["scat"])
+    ts(T.u8[:, :], T.s8[:, :], WIN - 1, None, AND, None, ["s8"], ["u8"])
+    tt(T.y8[:, :], T.u8[:, :], T.x8[:, :], ADD, ["u8", "x8"], ["y8"])
+    cp(T.off[:, :], T.y8[:, :], ["y8"], ["off"])
+    cp(T.scat[:, 32:32 + WIN].indirect(T.off[:, 0:8]), T.vals[:, :], ["off", "vals"] + ["sz%d" % z for z in range(N)], ["scat"])
 
-    def lists_of(za, zb):
-        key = "so%d" % za
+    pp, bb, dd, tm, jj = T.pp, T.bb, T.dd, T.tm, T.jj
+
+    def aside(name):
+        if name == "eq":
+            ts(eqs[:, 128:192], T.al[:, :], float(me), None, EQ, None, ["al"], ["eq2"])
+        elif name == "sum":
+            red(gcol[:, 2:3], eqs[:, 128:192], ["eq2"], ["gc2"])
+        elif name == "row":
+            ts(T.b3[:, :], T.ones[:, :], gcol[:, 2:3], None, MUL, None, ["ones", "gc2"], ["b3"])
+        elif name == "turn":
+            tr(T.t3[:, :], T.b3[:, :], ["b3"], ["t3"])
+        elif name == "n16":
+            tt(T.n16[:, :], T.t3[:, 0:32:2], T.t3[:, 1:32:2], ADD, ["t3"], ["n16"])
+        elif name == "n8":
+            tt(T.n8[:, :], T.n16[:, 0:16:2], T.n16[:, 1:16:2], ADD, ["n16"], ["n8"])
+        elif name == "n8s":
+            scan(T.n8s[:, :], T.n8[:, :], 8, 0.0, ["n8"], ["n8s"])
+
+    def lists_of(za, zb, gaps):
+        key, a, b = "so%d" % za, 128 * za, 128 * zb
         for z in range(za, zb):
-            tr(T.tw[:, 128 * z:128 * z + 128], T.scat[:, WSLOT * z:WSLOT * z + 128], ["scat"], ["tw%d" % z])
-        tt(T["self"][:, 4 * za:4 * zb], T.tw[:, 128 * za:128 * zb:32], T.tw[:, 128 * za + 16:128 * zb:32], ADD,
-           ["tw%d" % z for z in range(za, zb)], ["sf%d" % za])
+            tr(T.twa[:, 128 * z:128 * z + 128], T.scat[:, WSLOT * z + 32:WSLOT * z + 160], ["scat"], ["twa%d" % z])
+            tr(T.twb[:, 128 * z:128 * z + 128], T.scat[:, WSLOT * z + 16:WSLOT * z + 144], ["scat"], ["twb%d" % z])
+        aside(gaps[0])
+        tt(T.half[:, 8 * za:8 * zb], T.twa[:, a:b:16], T.twb[:, a:b:16], ADD, [t + str(z) for t in ("twa", "twb") for z in range(za, zb)], ["hf%d" % za])
+        aside(gaps[1])
+        tt(T["self"][:, 4 * za:4 * zb], T.half[:, 8 * za:8 * zb:2], T.half[:, 8 * za + 1:8 * zb:2], ADD, ["hf%d" % za], ["sf%d" % za])
+        aside(gaps[2])
         cp(T.so[:, 4 * za:4 * zb], T["self"][:, 4 * za:4 * zb], ["sf%d" % za], [key])
+        aside(gaps[3])
         return key
 
     def pick(oq, os_, n, iq, is_, m, off, n0, reads, writes):
@@ -322,79 +352,57 @@ def rank_program(g, core, T, topo):
             return sq[:, c:c + n].bitcast(dt.uint8) if kind == "q" else sp[:, c:c + n]
 
         def dst(z):
-            c = SLOT * (N - 1 - z)
+            c = SLOT * place(z)
             return T.land[:, c:c + n].bitcast(dt.uint8) if kind == "q" else T.lsc[:, c:c + n]
         send(zs, src, dst, engines, "dat", "dats", [key + kind])
 
+    gaps = (("", "", "", ""), ("eq", "", "sum", "row"), ("turn", "n16", "n8", "n8s"))
     for i, (sq, sp) in enumerate(((T.sq1, T.sp1), (T.sq2, T.sp2), (T.sq3, T.sp3))):
         zs, key = calls[2 * i][1], "w%d" % i
         za, zb = zs[0], zs[-1] + 1
-        k = lists_of(za, zb)
+        k = lists_of(min(za, near, own) if i == 2 else za, max(zb, own + 1) if i == 2 else zb, gaps[i])
         pick(sq, sp, SLOT * (zb - za), T.xq, T.xs, TOK, T.so[:, 4 * za:4 * zb], 0, [k, "xq"], key)
         columns(calls[2 * i], sq, sp, key)
         columns(calls[2 * i + 1], sq, sp, key)
-    k = lists_of(N - 1, N)
-    pick(T.land, T.lsc, SLOT, T.xq, T.xs, TOK, T.so[:, 4 * (N - 1):4 * N], 0, [k, "xq"], "own")
+    pick(T.land, T.lsc, SLOT, T.xq, T.xs, TOK, T.so[:, 4 * own:4 * own + 4], 0, [k, "xq"], "own")
 
-    ts(eqs[:, 128:192], T.al[:, :], float(me), None, EQ, None, ["al"], ["eq2"])
-    red(gcol[:, 2:3], eqs[:, 128:192], ["eq2"], ["gc2"])
-    ts(T.b3[:, :], T.ones[:, :], gcol[:, 2:3], None, MUL, None, ["ones", "gc2"], ["b3"])
-    tr(T.t3[:, :], T.b3[:, :], ["b3"], ["t3"])
-    tt(T.n16[:, :], T.t3[:, 0:32:2], T.t3[:, 1:32:2], ADD, ["t3"], ["n16"])
-    tt(T.n8[:, :], T.n16[:, 0:16:2], T.n16[:, 1:16:2], ADD, ["n16"], ["n8"])
-    pp, bb, dd, tm, jj = T.pp, T.bb, T.dd, T.tm, T.jj
-    scan(T.n8s[:, :], T.n8[:, :], 8, 0.0, ["n8"], ["n8s"])
     tt(bb[:, 8:16], bb[:, 0:8], T.n8[:, :], ADD, ["bb0", "n8"], ["bb8"])
     ts(pp[:, 1:9], T.n8s[:, :], float(CAP), None, MIN, None, ["n8s"], ["pp1"])
-    tt(T.bd[:, :], bb[:, 9:17], bb[:, 8:16], SUB, ["bb8", "bb16"], ["bd"])
-    tt(T.de[:, 0:9], bb[:, 0:9], pp[:, 0:9], SUB, ["bb0", "bb8", "pp0", "pp1"], ["de"])
-    tt(pp[:, 9:10], pp[:, 8:9], T.m8[:, 7:8], ADD, ["pp1", "m8"], ["pp9"])
-    tt(dd[:, 9:10], T.bd[:, 0:1], T.m8[:, 7:8], SUB, ["bd", "m8"], ["dd9"])
-    tt(dd[:, 1:9], T.de[:, 1:9], T.de[:, 0:8], SUB, ["de"], ["dd1e"])
-
-    def term(q, block, keys):
-        ts(tm[:, 20 * block:20 * block + 20], jj[:, :], pp[:, q:q + 1], dd[:, q:q + 1], GE, MUL, ["jj"] + keys, ["tm%d" % block])
-
-    def total(b, i):
-        c, d, e = 20 * b, 80 * i, 40 * i
-        tt(T.t80[:, d:d + 80], tm[:, c:c + 80], tm[:, c + 80:c + 160], ADD, ["tm%d" % k for k in range(b, b + 8)], ["t80%d" % i])
-        tt(T.t40[:, e:e + 40], T.t80[:, d:d + 40], T.t80[:, d + 40:d + 80], ADD, ["t80%d" % i], ["t40%d" % i])
-        tt(T.t20[:, e:e + 20], T.t40[:, e:e + 20], T.t40[:, e + 20:e + 40], ADD, ["t40%d" % i], ["t20%d" % i])
-
-    ts(T.t20[:, 20:40], jj[:, :], pp[:, 9:10], dd[:, 9:10], GE, MUL, ["jj", "pp9", "dd9"], ["t9"])
-    for q in range(1, 9):
-        term(q, q - 1, ["pp1", "dd1e"])
-    tt(T.t20[:, 60:80], T.t20[:, 20:40], jj[:, :], ADD, ["t9", "jj"], ["t9j"])
-    total(0, 0)
-    tt(tm[:, 300:320], T.t20[:, 0:20], T.t20[:, 60:80], ADD, ["t200", "t9j"], ["tm15"])
     op("v", V.quantize_mx, (T.wq[:, :], T.wsc[:, :], T["win"][:, :]), ["win"], ["wq"])
-    op("v", V.tensor_tensor_scan, (pp[:, 10:17], T.ml[:, 1:8], T.z64[:, 0:7], pp[:, 9:10], ADD, ADD), ["mx", "z64", "pp9"], ["pp10"])
-    tt(dd[:, 10:17], T.bd[:, 1:8], T.ml[:, 1:8], SUB, ["bd", "mx"], ["dd10"])
-    for q in range(10, 17):
-        term(q, q - 2, ["pp10", "dd10"])
-    total(8, 1)
-    ts(T.fo[:, :], T.t20[:, 40:60], float(ZERO + NZ - 1), None, MIN, None, ["t201"], ["fo"])
+    tt(pp[:, 9:10], pp[:, 8:9], T.m8[:, own:own + 1], ADD, ["pp1", "m8"], ["pp9"])
+    scan2(pp[:, 10:17], T.ml[:, 1:8], T.z64[:, 0:7], pp[:, 9:10], ["mx", "z64", "pp9"], ["pp10"])
+    places = ["pp0", "pp1", "pp9", "pp10"]
+    tt(T.de[:, 0:17], bb[:, 0:17], pp[:, 0:17], SUB, ["bb0", "bb8", "bb16"] + places, ["de"])
+    tt(dd[:, 1:17], T.de[:, 1:17], T.de[:, 0:16], SUB, ["de"], ["dd"])
+    for q in range(1, 17):
+        ts(tm[:, 20 * q - 20:20 * q], jj[:, :], pp[:, q:q + 1], dd[:, q:q + 1], GE, MUL, ["jj", "dd"] + places, ["tm%d" % q])
+    tt(T.t160[:, :], tm[:, 0:160], tm[:, 160:320], ADD, ["tm%d" % q for q in range(1, 17)], ["t160"])
+    tt(T.t80[:, :], T.t160[:, 0:80], T.t160[:, 80:160], ADD, ["t160"], ["t80"])
+    tt(T.t40[:, :], T.t80[:, 0:40], T.t80[:, 40:80], ADD, ["t80"], ["t40"])
+    tt(T.t20[:, 0:20], T.t40[:, 0:20], T.t40[:, 20:40], ADD, ["t40"], ["t20"])
+    tt(T.t20[:, 20:40], T.t20[:, 0:20], jj[:, :], ADD, ["t20", "jj"], ["t20j"])
+    ts(T.fo[:, :], T.t20[:, 20:40], float(ZERO + NZ - 1), None, MIN, None, ["t20j"], ["fo"])
 
     cnt["dat"] = data_in
     wr["dx"] = [("dat", data_in)]
     got = ["dx", "ownq", "owns", "zq", "fo"]
-    cuts = ((0, 192), (192, ROOM))
-    for i, (a, b) in enumerate(cuts):
+    cut = 192
+    for i, (a, b) in enumerate(((0, cut), (cut, ROOM))):
         pick(T.fq, T.fs, b - a, T.land, T.lsc, ZERO + NZ, T.fo[:, a // 16:b // 16], a, got, "f%d" % i)
-    first, every = ["f0q", "f0s"], ["f0q", "f0s", "f1q", "f1s"]
-    pieces = [(0, 0, 192, 0, first), (0, 192, ROOM, O, ["f1q", "f1s"])]
-    pieces += [(o, 0, ROOM, o, every) for o in range(1, O - 1)]
-    pieces += [(O - 1, 0, ROOM // 2, O - 1, every), (O - 1, ROOM // 2, ROOM, O + 1, every)]
-    for i, (o, a, b, p, keys) in enumerate(pieces):
-        op("t", g.tensor.matmul_mx, (T.acc[:, 512 * p:512 * p + b - a], T.wq[:, 128 * o:128 * o + 128], T.wsc[:, 128 * o:128 * o + 128],
+    low, top = ["f0q", "f0s"], ["f1q", "f1s"]
+    pieces = [(0, 0, cut, low), (1, 0, cut, low), (0, cut, ROOM, top), (1, cut, ROOM, top)]
+    for o in range(2, O):
+        pieces += [(o, 0, ROOM // 2, low + top), (o, ROOM // 2, ROOM, low + top)]
+    for i, (o, a, b, keys) in enumerate(pieces):
+        op("t", g.tensor.matmul_mx, (T.acc[:, 512 * i:512 * i + b - a], T.wq[:, 128 * o:128 * o + 128], T.wsc[:, 128 * o:128 * o + 128],
                                      T.fq[:, a:b], T.fs[:, a:b], True, True), ["wq"] + keys, ["acc%d" % i])
-    for i, (o, a, b, p, keys) in enumerate(pieces):
-        src, dst = T.acc[:, 512 * p:512 * p + b - a], T.yo[:, ROOM * o + a:ROOM * o + b]
-        if i % 2 == 0:
+    for i in [0, 2, 1, 3] + list(range(4, len(pieces))):
+        o, a, b, keys = pieces[i]
+        src, dst = T.acc[:, 512 * i:512 * i + b - a], T.yo[:, ROOM * o + a:ROOM * o + b]
+        if a == 0:
             cp(dst, src, ["acc%d" % i], ["yo%d" % i])
         else:
             act(dst, src, ["acc%d" % i], ["yo%d" % i])
-        if b == ROOM:
             dma("y", "dy", T.y[:, ROOM * o:ROOM * o + ROOM], T.yo[:, ROOM * o:ROOM * o + ROOM],
                 ["yo%d" % j for j in range(len(pieces)) if pieces[j][0] == o], ["yout"], more=True)
     for sem in sorted(cnt):

@@ -3,11 +3,12 @@ from concourse.mybir import dt, AluOpType, AxisListType, ActivationFunctionType
 
 N, TOK, O, CAP, ROOM, BOTH = 8, 256, 4, 288, 320, 60
 SLOT = 64
+FIRST = 48
 ZERO = N * SLOT
 NZ = 128
-WSLOT = 256
+WSLOT = 80
 WIN = N * WSLOT
-HIGH = 2 * WIN
+BACK = 9
 LATE = 400
 
 
@@ -21,22 +22,24 @@ SCRATCH = {
     "ct": _sb(32, I32), "xin": _sb(4 * TOK, B16), "win": _sb(512 * O, B16), "zin": _sb(4 * NZ, B16),
     "xq": _sb(TOK, MX), "xs": _sb(TOK, U8), "wq": _sb(128 * O, MX), "wsc": _sb(128 * O, U8),
     "ra": _sb(128, F32), "ca": _sb(128, F32), "rb": _sb(64, F32), "cb": _sb(64, F32), "e64": _sb(64, I32), "ec": _sb(64, I32),
-    "l4": _sb(4, I32), "l64": _sb(4, U16), "meq": _sb(32, F32), "mgt": _sb(32, F32), "mlt": _sb(32, F32),
-    "v128": _sb(128, B16), "vals": _sb(128, B16), "j0": _sb(20, I32), "jj": _sb(20, F32), "ones": _sb(32, F32), "z64": _sb(64, F32),
+    "gr": _sb(64, F32), "gt": _sb(64, F32), "gl": _sb(4, U16), "zpos": _sb(8, F32), "zfix": _sb(8, F32),
+    "l4": _sb(4, I32), "l64": _sb(4, U16), "meq": _sb(32, F32), "meqn": _sb(32, F32), "mgt": _sb(32, F32), "mlt": _sb(32, F32),
+    "v128": _sb(128, B16), "vals": _sb(128, B16), "j0": _sb(20, I32), "ones": _sb(32, F32), "z64": _sb(64, F32),
     "pre": _sb(256, B16), "mt": _sb(256, B16), "tcol": _sb(8, F32), "bm": _sb(128, F32), "tb": _sb(168, F32), "bcol": _sb(8, F32),
     "sc1": _sb(64, F32), "d1": _sb(64, F32), "sca": _sb(64, F32), "scb": _sb(64, F32), "wa": _sb(64, F32), "wb": _sb(64, F32),
     "qa": _sb(64, B16), "qb": _sb(64, B16), "td1": _sb(64, F32), "cs1": _sb(72, F32), "s1": _sb(8, F32),
-    "al": _sb(64, I32), "eqs": _sb(192, B16), "gcol": _sb(8, F32), "bg": _sb(64, F32), "tg": _sb(64, F32), "gs": _sb(8, F32),
+    "al": _sb(64, I32), "eqs": _sb(192, B16), "eqj": _sb(64, B16), "gcol": _sb(8, F32), "gme": _sb(8, F32), "bg": _sb(64, F32),
+    "tg": _sb(64, F32), "gs": _sb(8, F32), "b3": _sb(32, F32), "t3": _sb(32, F32), "n16": _sb(16, F32), "n8": _sb(8, F32),
     "fa": _sb(64, B16), "fb": _sb(64, B16), "r2": _sb(64, B16), "cum": _sb(64, F32), "bm2": _sb(64, F32), "p2": _sb(96, F32),
     "m16": _sb(16, F32), "m8": _sb(8, F32), "d2c": _sb(64, F32), "d2b": _sb(64, F32), "tdc": _sb(64, F32), "tdb": _sb(64, F32),
-    "cs2": _sb(72, F32), "s2": _sb(8, F32), "s8": _sb(8, I32), "x8": _sb(8, I32), "u8": _sb(8, I32), "y8": _sb(8, I32), "off": _sb(8, U16),
-    "scat": _sb(WIN + 32, B16), "twa": _sb(1024, B16), "twb": _sb(1024, B16), "half": _sb(64, F32), "self": _sb(32, F32), "so": _sb(32, U16),
+    "cs2": _sb(72, F32), "s2": _sb(8, F32), "s8": _sb(8, F32), "off": _sb(8, U16),
+    "scat": _sb(WIN + 32, B16), "tw": _sb(2 * WIN, B16), "hh": _sb(WIN // 16, F32), "so": _sb(4 * N, U16),
     "sq1": _sb(2 * SLOT, MX), "sp1": _sb(2 * SLOT, U8), "sq2": _sb(4 * SLOT, MX), "sp2": _sb(4 * SLOT, U8),
     "sq3": _sb(SLOT, MX), "sp3": _sb(SLOT, U8),
     "land": _sb(ZERO + NZ, MX), "lsc": _sb(ZERO + NZ, U8),
-    "b3": _sb(32, F32), "t3": _sb(32, F32), "n16": _sb(16, F32), "n8": _sb(8, F32), "n8s": _sb(8, F32), "pp": _sb(24, F32), "bb": _sb(24, F32),
-    "de": _sb(24, F32), "dd": _sb(24, F32), "tm": _sb(320, F32), "t160": _sb(160, F32), "t80": _sb(80, F32), "t40": _sb(40, F32),
-    "t20": _sb(40, F32), "ml": _sb(8, F32), "fo": _sb(20, U16), "fq": _sb(ROOM, MX), "fs": _sb(ROOM, U8),
+    "n8s": _sb(8, F32), "pp": _sb(24, F32), "bb": _sb(24, F32), "de": _sb(24, F32), "dd": _sb(24, F32), "ml": _sb(8, F32),
+    "ta": _sb(180, F32), "tz": _sb(180, F32), "cs3": _sb(192, F32), "t20": _sb(20, F32),
+    "fo": _sb(20, U16), "fq": _sb(ROOM, MX), "fs": _sb(ROOM, U8),
     "acc": ("psum", [128, 512 * 2 * O], F32), "yo": _sb(ROOM * O, F32),
 }
 SEMAPHORES = ["cv", "cs", "cg", "ct", "dl0", "dc1", "dc2", "dx", "dw", "dal", "dy",
@@ -51,11 +54,9 @@ COPY, IDENT = ActivationFunctionType.Copy, ActivationFunctionType.Identity
 def plan(me, cores, topo):
     core = cores[me]
     mate = [r for r in range(N) if r != me and topo.chip(cores[r]) == topo.chip(core)][0]
-    rot = 2 if mate == (me + 1) % N else 1
-    near = (mate - me - rot) % N
-    own = (N - rot) % N
-    far = [z for z in range(N) if z not in (near, own)]
-    out = topo.engines(core, cores[(me + rot + far[0]) % N])
+    near = (mate - me - 1) % N
+    far = [z for z in range(N - 1) if z != near]
+    out = topo.engines(core, cores[(me + 1 + far[0]) % N])
     inn = [e for e in topo.engines(core, cores[mate]) if e not in out]
 
     def deal(zs):
@@ -64,9 +65,9 @@ def plan(me, cores, topo):
 
     calls = []
     for zs, e in ((far[:2], deal(far[:2])), (far[2:], deal(far[2:])), ([near], {near: inn})):
-        n = SLOT if any(rot + z in (1, 2) or rot + z == N + 1 for z in zs) else BOTH
+        n = SLOT if min(zs) < 2 else BOTH
         calls += [("q", zs, n, e), ("s", zs, n, e)]
-    return rot, near, own, calls, out[::4]
+    return near, calls, out[::4]
 
 
 def rank_program(g, core, T, topo):
@@ -74,7 +75,8 @@ def rank_program(g, core, T, topo):
     if me is None:
         return
     cores = [int(c) for c in T.cores]
-    rot, near, own, calls, few = plan(me, cores, topo)
+    near, calls, few = plan(me, cores, topo)
+    own = N - 1
     queue = {"v": g.vector, "s": g.scalar, "t": g.tensor, "g": g, "y": g.sync}
     cnt, seen, wr, rd = {}, {}, {}, {}
 
@@ -140,6 +142,9 @@ def rank_program(g, core, T, topo):
     def tr(out, a, reads, writes):
         op("v", V.transpose, (out, a), reads, writes)
 
+    def quant(oq, os_, tile, reads, writes):
+        op("v", V.quantize_mx, (oq, os_, tile), reads, writes)
+
     def scan2(out, a, b, init, reads, writes):
         op("v", V.tensor_tensor_scan, (out, a, b, init, ADD, ADD), reads, writes)
 
@@ -153,15 +158,15 @@ def rank_program(g, core, T, topo):
         kw = {"allow_small_or_imprecise_dtypes": True} if flag else {}
         op("g", g.iota, (ap, pattern, base, 0), [], [key], **kw)
 
-    def act(out, a, reads, writes):
-        op("s", g.scalar.activation, (out, a, COPY), reads, writes)
+    def act(out, a, reads, writes, **kw):
+        op("s", g.scalar.activation, (out, a, COPY), reads, writes, **kw)
 
     def at(z):
-        rid, pid, _ = topo.addr(cores[(me + rot + z) % N])
+        rid, pid, _ = topo.addr(cores[(me + 1 + z) % N])
         return DstId(rid=rid, pnc=pid)
 
     def place(z):
-        return (N - rot - z) % N
+        return N - 1 - z
 
     def mask(engines):
         m = 0
@@ -177,8 +182,8 @@ def rank_program(g, core, T, topo):
 
     data_in = list_in = count_in = 0
     for k in range(1, N):
-        r2, _, _, c2, f2 = plan((me + k) % N, cores, topo)
-        z = (N - k - r2) % N
+        _, c2, f2 = plan((me + k) % N, cores, topo)
+        z = N - 1 - k
         data_in += sum(len(e[z]) for _, zs, _, e in c2 if z in zs)
         count_in += sum(len(e[z]) for kind, zs, _, e in c2 if z in zs and kind == "q")
         list_in += len(f2)
@@ -196,16 +201,20 @@ def rank_program(g, core, T, topo):
     iota(ra[:, 0:32], "ra0", [[0, 4], [1, 8]], 0, flag=True)
     iota(ra[:, 32:64], "ra1", [[1, 4], [0, 8]], 0, flag=True)
     iota(ra[:, 96:128], "ra3", [[0, 4], [WSLOT, 8]], -1, flag=True)
-    iota(T.e64[:, :], "e64", [[1, 64]], me + rot)
+    iota(T.e64[:, :], "e64", [[1, 64]], me + 1)
     others = [z for z in range(N) if z != own]
     before("g", ["l0"], [])
     g.remote_dma_fused([RemoteDMATransfer(dst_ids=[at(z) for z in others], dma_engine_mask=mask(few), remote_sem=T.sem["lst"],
                                           srcs=[T.lists[0]], dsts=[T.lists[place(z)] for z in others])], local_sem=T.sem["lsts"])
     cnt["lsts"] = len(few)
-    iota(T.zin[:, :], "zin", [[0, 4 * NZ]], 0, flag=True)
+    cnt["lst"] = list_in
+    wr["lx"] = [("lst", list_in)]
     iota(rb[:, 32:64], "rb1", [[16, 2], [0, 16]], 0, flag=True)
     iota(rb[:, 0:32], "rb0", [[0, 2], [1, 16]], 0, flag=True)
     iota(T.v128[:, :], "v128", [[32, 2], [64, 4], [1, 16]], 0, flag=True)
+    iota(T.gr[:, 0:32], "gr0", [[-1, 2], [WSLOT // 16, 4], [1, 4]], 1, flag=True)
+    iota(T.gr[:, 32:64], "gr1", [[-1, 2], [WSLOT // 16, 4], [1, 4]], 1 + WSLOT // 4, flag=True)
+    iota(T.gr[:, 3:32:16], "gr0", [[-1, 2]], 1 + BACK, flag=True)
     iota(T.j0[:, :], "j0", [[16, 20]], 0)
     iota(T.bb[:, 0:8], "bb0", [[SLOT, 8]], 0, flag=True)
 
@@ -214,6 +223,10 @@ def rank_program(g, core, T, topo):
     fill(T.cs1[:, 0:8], 0.0, "cs1z")
     fill(T.cs2[:, 0:8], 0.0, "cs2z")
     fill(T.pp[:, 0:1], 0.0, "pp0")
+    fill(T.zin[:, :], 0.0, "zin")
+    fill(T.tz[:, :], 0.0, "tzz")
+    fill(T.cs3[:, 0:12], 0.0, "cs3z")
+    fill(T.bb[:, 15:16], float(SLOT * (N - 1) + FIRST), "bb15")
     fill(T.bb[:, 16:17], float(ZERO), "bb16")
     tr(T.ca[:, :], ra[:, :], ["ra0", "ra1", "ra2", "ra3"], ["ca"])
     zc, hc, pc, sc = [T.ca[:, 32 * j:32 * j + 1] for j in range(4)]
@@ -221,55 +234,56 @@ def rank_program(g, core, T, topo):
     ts(T.l64[:, :], T.l4[:, :], pc, None, ADD, None, ["l4", "ca"], ["l64"])
     ts(T.meq[:, :], ra[:, 0:32], zc, None, EQ, None, ["ra0", "ca"], ["meq"])
     ts(T.mgt[:, :], ra[:, 32:64], hc, None, GT, None, ["ra1", "ca"], ["mgt"])
+    ts(T.zpos[:, 0:1], zc, 0.0, None, GT, None, ["ca"], ["zpos"])
+    ts(T.zfix[:, 0:1], zc, 0.0, 16.0 * BACK, EQ, MUL, ["ca"], ["zfix"])
     tt(T.mlt[:, :], T.meq[:, :], T.mgt[:, :], MUL, ["meq", "mgt"], ["mlt"])
+    ts(T.meqn[:, :], ra[:, 0:32], zc, T.zpos[:, 0:1], EQ, MUL, ["ra0", "ca", "zpos"], ["meqn"])
     act(T.tb[:, 31:32], sc, ["ca"], ["tb0"])
-    op("s", g.scalar.activation, (T.tb[:, 160:161], sc, IDENT, float(HIGH)), ["ca"], ["tb1"])
+    op("s", g.scalar.activation, (T.tb[:, 160:161], T.zfix[:, 0:1], IDENT, sc), ["zfix", "ca"], ["tb1"])
 
     l64 = T.l64[:, 0:4]
     c1w, c2w = T.ct[:, 0:16].indirect(l64), T.ct[:, 16:32].indirect(l64)
+    m1, ma, mb, mc = [T.mt[:, 64 * i:64 * i + 64] for i in range(4)]
     tt(T.pre[:, 0:64], c1w, T.ec[:, :], EQ, ["c1", "l64", "ec"], ["pre0"])
     ts(T.pre[:, 64:128], c1w, float((me + 1) % N), None, EQ, None, ["c1", "l64"], ["pre1"])
     ts(T.pre[:, 128:192], c1w, float((me + 2) % N), None, EQ, None, ["c1", "l64"], ["pre2"])
-    tr(T.mt[:, 0:192], T.pre[:, 0:192], ["pre0", "pre1", "pre2"], ["mt"])
     tt(T.pre[:, 192:256], c2w, T.ec[:, :], EQ, ["c2", "l64", "ec"], ["pre3"])
-    m1, ma, mb, mc = [T.mt[:, 64 * i:64 * i + 64] for i in range(4)]
+    tr(T.mt[:, :], T.pre[:, :], ["pre0", "pre1", "pre2", "pre3"], ["mt"])
     for i, m in enumerate((m1, ma, mb)):
         red(T.tcol[:, i:i + 1], m, ["mt"], ["tcol%d" % i])
-    tr(mc, T.pre[:, 192:256], ["pre3"], ["mc"])
     ts(T.bm[:, 0:32], T.mlt[:, :], T.tcol[:, 0:1], None, MUL, None, ["mlt", "tcol0"], ["bm0"])
     ts(T.bm[:, 32:64], T.mlt[:, :], T.tcol[:, 1:2], LATE / 32, MUL, ADD, ["mlt", "tcol1"], ["bm1"])
     ts(T.bm[:, 64:96], T.mlt[:, :], T.tcol[:, 2:3], LATE / 32, MUL, ADD, ["mlt", "tcol2"], ["bm2"])
-    ts(T.bm[:, 96:128], T.meq[:, :], T.tcol[:, 0:1], None, MUL, None, ["meq", "tcol0"], ["bm3"])
+    ts(T.bm[:, 96:128], T.meqn[:, :], T.tcol[:, 0:1], None, MUL, None, ["meqn", "tcol0"], ["bm3"])
     tr(T.tb[:, 32:160], T.bm[:, :], ["bm0", "bm1", "bm2", "bm3"], ["tb"])
-    tt(T.qa[:, :], ma, mc, MUL, ["mt", "mc"], ["qa"])
+    tr(T.cb[:, :], rb[:, :], ["rb0", "rb1"], ["cb"])
+    tt(T.qa[:, :], ma, mc, MUL, ["mt"], ["qa"])
     bcol = T.bcol
-    red(bcol[:, 0:1], T.tb[:, 31:64], ["tb", "tb0"], ["b1"])
     red(bcol[:, 1:2], T.tb[:, 64:96], ["tb"], ["ba"])
     red(bcol[:, 2:3], T.tb[:, 96:128], ["tb"], ["bq"])
+    red(bcol[:, 0:1], T.tb[:, 31:64], ["tb", "tb0"], ["b1"])
     red(T.p2[:, 31:32], T.tb[:, 128:161], ["tb", "tb1"], ["p2k"])
-    scan(T.sc1[:, :], m1, 64, bcol[:, 0:1], ["mt", "b1"], ["sc1"])
     scan(T.sca[:, :], ma, 64, bcol[:, 1:2], ["mt", "ba"], ["sca"])
     scan(T.scb[:, :], mb, 64, bcol[:, 2:3], ["mt", "bq"], ["scb"])
-    tt(T.d1[:, :], m1, T.sc1[:, :], MUL, ["mt", "sc1"], ["d1"])
-    tt(T.qb[:, :], mb, mc, MUL, ["mt", "mc"], ["qb"])
-    tr(T.td1[:, :], T.d1[:, :], ["d1"], ["td1"])
+    scan(T.sc1[:, :], m1, 64, bcol[:, 0:1], ["mt", "b1"], ["sc1"])
+    tt(T.qb[:, :], mb, mc, MUL, ["mt"], ["qb"])
     tt(T.wa[:, :], T.qa[:, :], T.sca[:, :], MUL, ["qa", "sca"], ["wa"])
+    tt(T.d1[:, :], m1, T.sc1[:, :], MUL, ["mt", "sc1"], ["d1"])
     tt(T.wb[:, :], T.qb[:, :], T.scb[:, :], MUL, ["qb", "scb"], ["wb"])
+    tr(T.td1[:, :], T.d1[:, :], ["d1"], ["td1"])
+    quant(T.xq[:, :], T.xs[:, :], T.xin[:, :], ["xin"], ["xq"])
     scan(T.cs1[:, 8:72], T.td1[:, :], 64, 0.0, ["td1"], ["cs1"])
-    tr(T.cb[:, :], rb[:, :], ["rb0", "rb1"], ["cb"])
+    tr(T.gt[:, :], T.gr[:, :], ["gr0", "gr1"], ["gt"])
     tt(T.s1[:, :], T.cs1[:, 15:72:8], T.cs1[:, 7:64:8], SUB, ["cs1", "cs1z"], ["s1"])
-    op("v", V.quantize_mx, (T.xq[:, :], T.xs[:, :], T.xin[:, :]), ["xin"], ["xq"])
-    op("v", V.quantize_mx, (T.land[:, ZERO:ZERO + NZ], T.lsc[:, ZERO:ZERO + NZ], T.zin[:, :]), ["zin"], ["zq"])
-    ts(T.jj[:, :], T.j0[:, :], T.cb[:, 0:1], None, ADD, None, ["j0", "cb"], ["jj"])
+    cp(T.gl[:, 0:4:2], T.gt[:, 0:64:32], ["gt"], ["gl"])
 
-    cnt["lst"] = list_in
-    wr["lx"] = [("lst", list_in)]
     for b in range(4):
         dma("ys"[b % 2], "dal", T.al[32 * b:32 * b + 32, 0:64], T.lists[:, :, :], ["lx", "l0"], ["al"], more=True)
     dma("y", "dw", T["win"][:, :], T.w[:, :], ["lx"], ["win"])
     op("s", g.scalar.activation, (T.vals[:, :], T.v128[:, :], IDENT, T.cb[:, 32:33]), ["v128", "cb"], ["vals"])
-    for z in range(N):
-        act(T.scat[:, WSLOT * z + 16:WSLOT * z + 160], T.zin[:, 0:144], ["zin"], ["sz%d" % z])
+    half = (WIN + 32) // 2
+    for i in range(2):
+        act(T.scat[:, half * i:half * i + half], T.zin[:, 0:half], ["zin"], ["sz%d" % i])
     eqs, gcol = T.eqs, T.gcol
     for i in range(2):
         ts(eqs[:, 64 * i:64 * i + 64], T.al[:, :], float((me + 1 + i) % N), None, EQ, None, ["al"], ["eq%d" % i])
@@ -277,16 +291,20 @@ def rank_program(g, core, T, topo):
         red(gcol[:, i:i + 1], eqs[:, 64 * i:64 * i + 64], ["eq%d" % i], ["gc%d" % i])
     for i in range(2):
         ts(T.bg[:, 32 * i:32 * i + 32], T.ones[:, :], gcol[:, i:i + 1], None, MUL, None, ["ones", "gc%d" % i], ["bg%d" % i])
+    ts(eqs[:, 128:192], T.al[:, :], float(me), None, EQ, None, ["al"], ["eq2"])
     tr(T.tg[:, :], T.bg[:, :], ["bg0", "bg1"], ["tg"])
     for i in range(2):
         red(T.gs[:, i:i + 1], T.tg[:, 36 * i + 4:32 * i + 32], ["tg"], ["gs%d" % i])
+    act(T.eqj[:, :], eqs[:, 128:192], ["eq2"], ["eqj", "gme"], accum_out=T.gme[:, 0:1])
+    act(T.b3[:, :], T.ones[:, :], ["ones", "gme"], ["b3"], scale=T.gme[:, 0:1])
+
     lim = float(LATE + CAP + 1)
     ts(T.fa[:, :], T.wa[:, :], T.gs[:, 0:1], lim, ADD, GE, ["wa", "gs0"], ["fa"])
     ts(T.fb[:, :], T.wb[:, :], T.gs[:, 1:2], lim, ADD, GE, ["wb", "gs1"], ["fb"])
     scan2(T.cum[:, :], T.fa[:, :], T.fb[:, :], 0.0, ["fa", "fb"], ["cum"])
+    act(T.bm2[:, 32:64], T.ones[:, :], ["ones", "cum"], ["bm5"], scale=T.cum[:, 63:64])
     tt(T.r2[:, :], T.fa[:, :], T.fb[:, :], ADD, ["fa", "fb"], ["r2"])
     ts(T.bm2[:, 0:32], T.mlt[:, :], T.cum[:, 63:64], None, MUL, None, ["mlt", "cum"], ["bm4"])
-    ts(T.bm2[:, 32:64], T.ones[:, :], T.cum[:, 63:64], None, MUL, None, ["ones", "cum"], ["bm5"])
     tt(T.d2c[:, :], T.r2[:, :], T.cum[:, :], MUL, ["r2", "cum"], ["d2c"])
     tr(T.p2[:, 32:96], T.bm2[:, :], ["bm4", "bm5"], ["p2"])
     tr(T.tdc[:, :], T.d2c[:, :], ["d2c"], ["tdc"])
@@ -299,50 +317,37 @@ def rank_program(g, core, T, topo):
     cnt["mar"] = count_in
     wr["mx"] = [("mar", count_in)]
     tr(T.tdb[:, :], T.d2b[:, :], ["d2b"], ["tdb"])
+    tr(T.t3[:, :], T.b3[:, :], ["b3"], ["t3"])
     scan2(T.cs2[:, 8:72], T.tdc[:, :], T.tdb[:, :], 0.0, ["tdc", "tdb"], ["cs2"])
+    tt(T.n16[:, :], T.t3[:, 0:32:2], T.t3[:, 1:32:2], ADD, ["t3"], ["n16"])
     tt(T.s2[:, :], T.cs2[:, 15:72:8], T.cs2[:, 7:64:8], SUB, ["cs2", "cs2z"], ["s2"])
+    tt(T.n8[:, :], T.n16[:, 0:16:2], T.n16[:, 1:16:2], ADD, ["n16"], ["n8"])
     tt(T.s8[:, :], T.s1[:, :], T.s2[:, :], MAX, ["s1", "s2"], ["s8"])
-    ts(T.x8[:, :], T.s8[:, :], 112, None, AND, None, ["s8"], ["x8"])
-    ts(T.u8[:, :], T.s8[:, :], WIN - 1, None, AND, None, ["s8"], ["u8"])
-    tt(T.y8[:, :], T.u8[:, :], T.x8[:, :], ADD, ["u8", "x8"], ["y8"])
-    cp(T.off[:, :], T.y8[:, :], ["y8"], ["off"])
-    cp(T.scat[:, 32:32 + WIN].indirect(T.off[:, 0:8]), T.vals[:, :], ["off", "vals"] + ["sz%d" % z for z in range(N)], ["scat"])
+    scan(T.n8s[:, :], T.n8[:, :], 8, 0.0, ["n8"], ["n8s"])
+    cp(T.off[:, :], T.s8[:, :], ["s8"], ["off"])
+    ts(T.ta[:, 0:180:9], T.j0[:, :], T.cb[:, 0:1], None, ADD, None, ["j0", "cb"], ["jj"])
+    cp(T.scat[:, 32:32 + WIN].indirect(T.off[:, 0:8]), T.vals[:, :], ["off", "vals", "sz0", "sz1"], ["scat"])
 
-    pp, bb, dd, tm, jj = T.pp, T.bb, T.dd, T.tm, T.jj
+    pp, bb, dd = T.pp, T.bb, T.dd
+    tw, hh, so = T.tw, T.hh, T.so
+    H = WIN // 2
 
-    def aside(name):
-        if name == "eq":
-            ts(eqs[:, 128:192], T.al[:, :], float(me), None, EQ, None, ["al"], ["eq2"])
-        elif name == "sum":
-            red(gcol[:, 2:3], eqs[:, 128:192], ["eq2"], ["gc2"])
-        elif name == "row":
-            ts(T.b3[:, :], T.ones[:, :], gcol[:, 2:3], None, MUL, None, ["ones", "gc2"], ["b3"])
-        elif name == "turn":
-            tr(T.t3[:, :], T.b3[:, :], ["b3"], ["t3"])
-        elif name == "n16":
-            tt(T.n16[:, :], T.t3[:, 0:32:2], T.t3[:, 1:32:2], ADD, ["t3"], ["n16"])
-        elif name == "n8":
-            tt(T.n8[:, :], T.n16[:, 0:16:2], T.n16[:, 1:16:2], ADD, ["n16"], ["n8"])
-        elif name == "n8s":
-            scan(T.n8s[:, :], T.n8[:, :], 8, 0.0, ["n8"], ["n8s"])
+    def turn(i, late):
+        tr(tw[:, late * WIN + H * i:late * WIN + H * i + H], T.scat[:, 32 - 16 * late + H * i:32 - 16 * late + H * i + H],
+           ["scat"], ["tw%d%d" % (late, i)])
 
-    def lists_of(za, zb, gaps):
-        key, a, b = "so%d" % za, 128 * za, 128 * zb
-        for z in range(za, zb):
-            tr(T.twa[:, 128 * z:128 * z + 128], T.scat[:, WSLOT * z + 32:WSLOT * z + 160], ["scat"], ["twa%d" % z])
-            tr(T.twb[:, 128 * z:128 * z + 128], T.scat[:, WSLOT * z + 16:WSLOT * z + 144], ["scat"], ["twb%d" % z])
-        aside(gaps[0])
-        tt(T.half[:, 8 * za:8 * zb], T.twa[:, a:b:16], T.twb[:, a:b:16], ADD, [t + str(z) for t in ("twa", "twb") for z in range(za, zb)], ["hf%d" % za])
-        aside(gaps[1])
-        tt(T["self"][:, 4 * za:4 * zb], T.half[:, 8 * za:8 * zb:2], T.half[:, 8 * za + 1:8 * zb:2], ADD, ["hf%d" % za], ["sf%d" % za])
-        aside(gaps[2])
-        cp(T.so[:, 4 * za:4 * zb], T["self"][:, 4 * za:4 * zb], ["sf%d" % za], [key])
-        aside(gaps[3])
-        return key
+    def join(i, late):
+        a = late * WIN + H * i
+        tt(hh[:, 20 * i + 1 - late:20 * i + 20:2], tw[:, a:a + H:32], tw[:, a + 16:a + H:32], ADD, ["tw%d%d" % (late, i)],
+           ["hh%d%d" % (late, i)])
+
+    def entries(i):
+        cp(so[:, 16 * i:16 * i + 16], hh[:, 0:20 * i + 20].indirect(T.gl[:, 2 * i:2 * i + 1]),
+           ["gl"] + ["hh%d%d" % (a, b) for a in range(2) for b in range(i + 1)], ["so%d" % i])
 
     def pick(oq, os_, n, iq, is_, m, off, n0, reads, writes):
         op("v", V.tensor_copy, (oq[:, n0:n0 + n].bitcast(dt.uint32), iq[:, 0:m].bitcast(dt.uint32).indirect(off)), reads, [writes + "q"])
-        op("s", g.scalar.activation, (os_[:, n0:n0 + n], is_[:, 0:m].indirect(off), COPY), reads, [writes + "s"])
+        act(os_[:, n0:n0 + n], is_[:, 0:m].indirect(off), reads, [writes + "s"])
 
     def columns(call, sq, sp, key):
         kind, zs, n, engines = call
@@ -356,37 +361,48 @@ def rank_program(g, core, T, topo):
             return T.land[:, c:c + n].bitcast(dt.uint8) if kind == "q" else T.lsc[:, c:c + n]
         send(zs, src, dst, engines, "dat", "dats", [key + kind])
 
-    gaps = (("", "", "", ""), ("eq", "", "sum", "row"), ("turn", "n16", "n8", "n8s"))
-    for i, (sq, sp) in enumerate(((T.sq1, T.sp1), (T.sq2, T.sp2), (T.sq3, T.sp3))):
-        zs, key = calls[2 * i][1], "w%d" % i
+    def wave(i, lists):
+        (sq, sp), zs, key = ((T.sq1, T.sp1), (T.sq2, T.sp2), (T.sq3, T.sp3))[i], calls[2 * i][1], "w%d" % i
         za, zb = zs[0], zs[-1] + 1
-        k = lists_of(min(za, near, own) if i == 2 else za, max(zb, own + 1) if i == 2 else zb, gaps[i])
-        pick(sq, sp, SLOT * (zb - za), T.xq, T.xs, TOK, T.so[:, 4 * za:4 * zb], 0, [k, "xq"], key)
+        pick(sq, sp, SLOT * (zb - za), T.xq, T.xs, TOK, so[:, 4 * za:4 * zb], 0, lists + ["xq"], key)
         columns(calls[2 * i], sq, sp, key)
         columns(calls[2 * i + 1], sq, sp, key)
-    pick(T.land, T.lsc, SLOT, T.xq, T.xs, TOK, T.so[:, 4 * own:4 * own + 4], 0, [k, "xq"], "own")
 
-    tt(bb[:, 8:16], bb[:, 0:8], T.n8[:, :], ADD, ["bb0", "n8"], ["bb8"])
+    turn(0, 0)
+    turn(0, 1)
+    join(0, 0)
+    join(0, 1)
+    turn(1, 0)
+    entries(0)
+    turn(1, 1)
+    wave(0, ["so0"])
+    join(1, 0)
+    join(1, 1)
+    tt(bb[:, 8:15], bb[:, 0:7], T.n8[:, 0:7], ADD, ["bb0", "n8"], ["bb8"])
+    entries(1)
     ts(pp[:, 1:9], T.n8s[:, :], float(CAP), None, MIN, None, ["n8s"], ["pp1"])
-    op("v", V.quantize_mx, (T.wq[:, :], T.wsc[:, :], T["win"][:, :]), ["win"], ["wq"])
+    wave(1, ["so0", "so1"])
+    wave(2, ["so0", "so1"])
+    pick(T.land, T.lsc, SLOT, T.xq, T.xs, TOK, so[:, 4 * own:4 * own + 4], 0, ["so1", "xq"], "own")
+
     tt(pp[:, 9:10], pp[:, 8:9], T.m8[:, own:own + 1], ADD, ["pp1", "m8"], ["pp9"])
+    quant(T.land[:, ZERO:ZERO + NZ], T.lsc[:, ZERO:ZERO + NZ], T.zin[:, :], ["zin"], ["zq"])
     scan2(pp[:, 10:17], T.ml[:, 1:8], T.z64[:, 0:7], pp[:, 9:10], ["mx", "z64", "pp9"], ["pp10"])
+    quant(T.wq[:, :], T.wsc[:, :], T["win"][:, :], ["win"], ["wq"])
     places = ["pp0", "pp1", "pp9", "pp10"]
-    tt(T.de[:, 0:17], bb[:, 0:17], pp[:, 0:17], SUB, ["bb0", "bb8", "bb16"] + places, ["de"])
+    tt(T.de[:, 0:17], bb[:, 0:17], pp[:, 0:17], SUB, ["bb0", "bb8", "bb15", "bb16"] + places, ["de"])
     tt(dd[:, 1:17], T.de[:, 1:17], T.de[:, 0:16], SUB, ["de"], ["dd"])
     for q in range(1, 17):
-        ts(tm[:, 20 * q - 20:20 * q], jj[:, :], pp[:, q:q + 1], dd[:, q:q + 1], GE, MUL, ["jj", "dd"] + places, ["tm%d" % q])
-    tt(T.t160[:, :], tm[:, 0:160], tm[:, 160:320], ADD, ["tm%d" % q for q in range(1, 17)], ["t160"])
-    tt(T.t80[:, :], T.t160[:, 0:80], T.t160[:, 80:160], ADD, ["t160"], ["t80"])
-    tt(T.t40[:, :], T.t80[:, 0:40], T.t80[:, 40:80], ADD, ["t80"], ["t40"])
-    tt(T.t20[:, 0:20], T.t40[:, 0:20], T.t40[:, 20:40], ADD, ["t40"], ["t20"])
-    tt(T.t20[:, 20:40], T.t20[:, 0:20], jj[:, :], ADD, ["t20", "jj"], ["t20j"])
-    ts(T.fo[:, :], T.t20[:, 20:40], float(ZERO + NZ - 1), None, MIN, None, ["t20j"], ["fo"])
+        t, i = (T.ta, q) if q < 9 else (T.tz, q - 8)
+        ts(t[:, i:180:9], T.ta[:, 0:180:9], pp[:, q:q + 1], dd[:, q:q + 1], GE, MUL, ["jj", "dd", "tzz"] + places, ["tm%d" % q])
+    scan2(T.cs3[:, 12:192], T.ta[:, :], T.tz[:, :], 0.0, ["jj", "tzz"] + ["tm%d" % q for q in range(1, 17)], ["cs3"])
+    tt(T.t20[:, :], T.cs3[:, 20:192:9], T.cs3[:, 11:183:9], SUB, ["cs3", "cs3z"], ["t20"])
+    ts(T.fo[:, :], T.t20[:, :], float(ZERO + NZ - 1), None, MIN, None, ["t20"], ["fo"])
 
     cnt["dat"] = data_in
     wr["dx"] = [("dat", data_in)]
     got = ["dx", "ownq", "owns", "zq", "fo"]
-    cut = 192
+    cut = 128
     for i, (a, b) in enumerate(((0, cut), (cut, ROOM))):
         pick(T.fq, T.fs, b - a, T.land, T.lsc, ZERO + NZ, T.fo[:, a // 16:b // 16], a, got, "f%d" % i)
     low, top = ["f0q", "f0s"], ["f1q", "f1s"]
@@ -396,14 +412,13 @@ def rank_program(g, core, T, topo):
     for i, (o, a, b, keys) in enumerate(pieces):
         op("t", g.tensor.matmul_mx, (T.acc[:, 512 * i:512 * i + b - a], T.wq[:, 128 * o:128 * o + 128], T.wsc[:, 128 * o:128 * o + 128],
                                      T.fq[:, a:b], T.fs[:, a:b], True, True), ["wq"] + keys, ["acc%d" % i])
-    for i in [0, 2, 1, 3] + list(range(4, len(pieces))):
-        o, a, b, keys = pieces[i]
+    for i, (o, a, b, keys) in enumerate(pieces):
         src, dst = T.acc[:, 512 * i:512 * i + b - a], T.yo[:, ROOM * o + a:ROOM * o + b]
-        if a == 0:
-            cp(dst, src, ["acc%d" % i], ["yo%d" % i])
-        else:
-            act(dst, src, ["acc%d" % i], ["yo%d" % i])
-            dma("y", "dy", T.y[:, ROOM * o:ROOM * o + ROOM], T.yo[:, ROOM * o:ROOM * o + ROOM],
-                ["yo%d" % j for j in range(len(pieces)) if pieces[j][0] == o], ["yout"], more=True)
+        (cp if i in (0, 1, 3, 4, 6) else act)(dst, src, ["acc%d" % i], ["yo%d" % i])
+        if o < 2:
+            dma("y", "dy", T.y[:, ROOM * o + a:ROOM * o + b], dst, ["yo%d" % i], ["yout"], more=True)
+        elif a > 0:
+            dma("y", "dy", T.y[:, ROOM * o:ROOM * o + ROOM], T.yo[:, ROOM * o:ROOM * o + ROOM], ["yo%d" % (i - 1), "yo%d" % i],
+                ["yout"], more=True)
     for sem in sorted(cnt):
         need("y", (sem, None))

from concourse.bass import DstId, RemoteDMATransfer
from concourse.mybir import dt, AluOpType, AxisListType, ActivationFunctionType

N, TOK, O, CAP, ROOM, BOTH = 8, 256, 4, 288, 320, 60
SLOT = 64
FIRST = 48
ZERO = N * SLOT
NZ = 128
WSLOT = 80
WIN = N * WSLOT
BACK = 9
LATE = 400


def _sb(n, d):
    return ("sbuf", [128, n], d)


F32, I32, U16, B16, MX, U8 = "float32", "int32", "uint16", "bfloat16", "float8_e4m3fn_x4", "uint8"
SCRATCH = {
    "lists": ("dram", [N, 128, 2], I32),
    "ct": _sb(32, I32), "xin": _sb(4 * TOK, B16), "win": _sb(512 * O, B16), "zin": _sb(4 * NZ, B16),
    "xq": _sb(TOK, MX), "xs": _sb(TOK, U8), "wq": _sb(128 * O, MX), "wsc": _sb(128 * O, U8),
    "ra": _sb(128, F32), "ca": _sb(128, F32), "rb": _sb(64, F32), "cb": _sb(64, F32), "e64": _sb(64, I32), "ec": _sb(64, I32),
    "gr": _sb(64, F32), "gt": _sb(64, F32), "gl": _sb(4, U16), "zpos": _sb(8, F32), "zfix": _sb(8, F32),
    "l4": _sb(4, I32), "l64": _sb(4, U16), "meq": _sb(32, F32), "meqn": _sb(32, F32), "mgt": _sb(32, F32), "mlt": _sb(32, F32),
    "v128": _sb(128, B16), "vals": _sb(128, B16), "j0": _sb(20, I32), "ones": _sb(32, F32), "z64": _sb(64, F32),
    "pre": _sb(256, B16), "mt": _sb(256, B16), "tcol": _sb(8, F32), "bm": _sb(128, F32), "tb": _sb(168, F32), "bcol": _sb(8, F32),
    "sc1": _sb(64, F32), "d1": _sb(64, F32), "sca": _sb(64, F32), "scb": _sb(64, F32), "wa": _sb(64, F32), "wb": _sb(64, F32),
    "qa": _sb(64, B16), "qb": _sb(64, B16), "td1": _sb(64, F32), "cs1": _sb(72, F32), "s1": _sb(8, F32),
    "al": _sb(64, I32), "eqs": _sb(192, B16), "eqj": _sb(64, B16), "gcol": _sb(8, F32), "gme": _sb(8, F32), "bg": _sb(64, F32),
    "tg": _sb(64, F32), "gs": _sb(8, F32), "b3": _sb(32, F32), "t3": _sb(32, F32), "n16": _sb(16, F32), "n8": _sb(8, F32),
    "fa": _sb(64, B16), "fb": _sb(64, B16), "r2": _sb(64, B16), "cum": _sb(64, F32), "bm2": _sb(64, F32), "p2": _sb(96, F32),
    "m16": _sb(16, F32), "m8": _sb(8, F32), "d2c": _sb(64, F32), "d2b": _sb(64, F32), "tdc": _sb(64, F32), "tdb": _sb(64, F32),
    "cs2": _sb(72, F32), "s2": _sb(8, F32), "s8": _sb(8, F32), "off": _sb(8, U16),
    "scat": _sb(WIN + 32, B16), "tw": _sb(2 * WIN, B16), "hh": _sb(WIN // 16, F32), "so": _sb(4 * N, U16),
    "sq1": _sb(2 * SLOT, MX), "sp1": _sb(2 * SLOT, U8), "sq2": _sb(4 * SLOT, MX), "sp2": _sb(4 * SLOT, U8),
    "sq3": _sb(SLOT, MX), "sp3": _sb(SLOT, U8),
    "land": _sb(ZERO + NZ, MX), "lsc": _sb(ZERO + NZ, U8),
    "n8s": _sb(8, F32), "pp": _sb(24, F32), "bb": _sb(24, F32), "de": _sb(24, F32), "dd": _sb(24, F32), "ml": _sb(8, F32),
    "ta": _sb(180, F32), "tz": _sb(180, F32), "cs3": _sb(192, F32), "t20": _sb(20, F32),
    "fo": _sb(20, U16), "fq": _sb(ROOM, MX), "fs": _sb(ROOM, U8),
    "acc": ("psum", [128, 512 * 2 * O], F32), "yo": _sb(ROOM * O, F32),
}
SEMAPHORES = ["cv", "cs", "cg", "ct", "dl0", "dc1", "dc2", "dx", "dw", "dal", "dy",
              "lst", "lsts", "mar", "mars", "dat", "dats"]

ADD, SUB, MUL, MIN, MAX = AluOpType.add, AluOpType.subtract, AluOpType.mult, AluOpType.min, AluOpType.max
GE, GT, EQ = AluOpType.is_ge, AluOpType.is_gt, AluOpType.is_equal
AND = AluOpType.bitwise_and
COPY, IDENT = ActivationFunctionType.Copy, ActivationFunctionType.Identity


def plan(me, cores, topo):
    core = cores[me]
    mate = [r for r in range(N) if r != me and topo.chip(cores[r]) == topo.chip(core)][0]
    near = (mate - me - 1) % N
    far = [z for z in range(N - 1) if z != near]
    out = topo.engines(core, cores[(me + 1 + far[0]) % N])
    inn = [e for e in topo.engines(core, cores[mate]) if e not in out]

    def deal(zs):
        k = len(out) // len(zs)
        return {z: out[k * i:k * i + k] for i, z in enumerate(zs)}

    calls = []
    for zs, e in ((far[:2], deal(far[:2])), (far[2:], deal(far[2:])), ([near], {near: inn})):
        n = SLOT if min(zs) < 2 else BOTH
        calls += [("q", zs, n, e), ("s", zs, n, e)]
    return near, calls, out[::4]


def rank_program(g, core, T, topo):
    me = T.rank_of(core)
    if me is None:
        return
    cores = [int(c) for c in T.cores]
    near, calls, few = plan(me, cores, topo)
    own = N - 1
    queue = {"v": g.vector, "s": g.scalar, "t": g.tensor, "g": g, "y": g.sync}
    cnt, seen, wr, rd = {}, {}, {}, {}

    def need(q, tok):
        sem, val = tok
        if val is None:
            val = cnt[sem]
        if seen.get((q, sem), 0) < val:
            queue[q].wait_ge(T.sem[sem], val)
            seen[(q, sem)] = val

    def before(q, reads, writes):
        toks = {}
        for k in reads:
            for t in wr.get(k, []):
                toks.setdefault(t[0], []).append(t)
        for k in writes:
            for t in wr.get(k, []) + rd.get(k, []):
                toks.setdefault(t[0], []).append(t)
        for sem in toks:
            v = [t[1] for t in toks[sem]]
            need(q, (sem, None if None in v else max(v)))

    def after(tok, reads, writes, more):
        for k in writes:
            wr[k] = (wr.get(k, []) if more else []) + [tok]
            if not more:
                rd[k] = []
        for k in reads:
            rd.setdefault(k, []).append(tok)

    def op(q, call, args, reads, writes, **kw):
        before(q, reads, writes)
        sem = "c" + q
        call(*args, **kw).then_inc(T.sem[sem], 1)
        cnt[sem] = cnt.get(sem, 0) + 1
        after((sem, cnt[sem]), reads, writes, False)

    def dma(q, sem, out, in_, reads, writes, more=False):
        if not more:
            before(q, reads, writes)
        else:
            before(q, reads, [])
        queue[q].dma_start(out, in_).then_inc(T.sem[sem], 16)
        cnt[sem] = cnt.get(sem, 0) + 16
        after((sem, None), reads, writes, more)

    V = g.vector

    def ts(out, in0, s1, s2, op0, op1, reads, writes):
        a = (out, in0, s1, s2, op0) if op1 is None else (out, in0, s1, s2, op0, op1)
        op("v", V.tensor_scalar, a, reads, writes)

    def tt(out, a, b, o, reads, writes):
        op("v", V.tensor_tensor, (out, a, b, o), reads, writes)

    def cp(out, a, reads, writes):
        op("v", V.tensor_copy, (out, a), reads, writes)

    def red(out, a, reads, writes):
        op("v", V.tensor_reduce, (out, a, AxisListType.X, ADD), reads, writes)

    def tr(out, a, reads, writes):
        op("v", V.transpose, (out, a), reads, writes)

    def quant(oq, os_, tile, reads, writes):
        op("v", V.quantize_mx, (oq, os_, tile), reads, writes)

    def scan2(out, a, b, init, reads, writes):
        op("v", V.tensor_tensor_scan, (out, a, b, init, ADD, ADD), reads, writes)

    def scan(out, a, n, init, reads, writes):
        scan2(out, a, T.z64[:, 0:n], init, reads + ["z64"], writes)

    def fill(ap, val, key):
        op("v", V.memset, (ap, val), [], [key])

    def iota(ap, key, pattern, base, flag=False):
        kw = {"allow_small_or_imprecise_dtypes": True} if flag else {}
        op("g", g.iota, (ap, pattern, base, 0), [], [key], **kw)

    def act(out, a, reads, writes, **kw):
        op("s", g.scalar.activation, (out, a, COPY), reads, writes, **kw)

    def at(z):
        rid, pid, _ = topo.addr(cores[(me + 1 + z) % N])
        return DstId(rid=rid, pnc=pid)

    def place(z):
        return N - 1 - z

    def mask(engines):
        m = 0
        for e in engines:
            m |= 1 << e
        return m

    def send(zs, src, dst, engines, sem, lsem, reads):
        before("g", reads, [])
        g.remote_dma_fused([RemoteDMATransfer(dst_ids=[at(z)], dma_engine_mask=mask(engines[z]),
                                              remote_sem=T.sem[sem], src=src(z), dst=dst(z)) for z in zs], local_sem=T.sem[lsem])
        cnt[lsem] = cnt.get(lsem, 0) + sum(len(engines[z]) for z in zs)

    data_in = list_in = count_in = 0
    for k in range(1, N):
        _, c2, f2 = plan((me + k) % N, cores, topo)
        z = N - 1 - k
        data_in += sum(len(e[z]) for _, zs, _, e in c2 if z in zs)
        count_in += sum(len(e[z]) for kind, zs, _, e in c2 if z in zs and kind == "q")
        list_in += len(f2)

    dma("y", "dl0", T.lists[0], T.c1[:, :], [], ["l0"])
    for b in range(8):
        dma("ys"[b % 2], "dc1", T.ct[16 * b:16 * b + 16, 0:16], T.c1[:, :], [], ["c1"], more=True)
    for b in range(8):
        dma("sy"[b % 2], "dc2", T.ct[16 * b:16 * b + 16, 16:32], T.c2[:, :], [], ["c2"], more=True)
    dma("y", "dx", T.xin[:, :], T.x[:, :], [], ["xin"])

    ra, rb = T.ra, T.rb
    iota(T.l4[:, :], "l4", [[2, 2], [8, 2]], 0)
    iota(ra[:, 64:96], "ra2", [[1, 2], [4, 2], [0, 8]], 0, flag=True)
    iota(ra[:, 0:32], "ra0", [[0, 4], [1, 8]], 0, flag=True)
    iota(ra[:, 32:64], "ra1", [[1, 4], [0, 8]], 0, flag=True)
    iota(ra[:, 96:128], "ra3", [[0, 4], [WSLOT, 8]], -1, flag=True)
    iota(T.e64[:, :], "e64", [[1, 64]], me + 1)
    others = [z for z in range(N) if z != own]
    before("g", ["l0"], [])
    g.remote_dma_fused([RemoteDMATransfer(dst_ids=[at(z) for z in others], dma_engine_mask=mask(few), remote_sem=T.sem["lst"],
                                          srcs=[T.lists[0]], dsts=[T.lists[place(z)] for z in others])], local_sem=T.sem["lsts"])
    cnt["lsts"] = len(few)
    cnt["lst"] = list_in
    wr["lx"] = [("lst", list_in)]
    iota(rb[:, 32:64], "rb1", [[16, 2], [0, 16]], 0, flag=True)
    iota(rb[:, 0:32], "rb0", [[0, 2], [1, 16]], 0, flag=True)
    iota(T.v128[:, :], "v128", [[32, 2], [64, 4], [1, 16]], 0, flag=True)
    iota(T.gr[:, 0:32], "gr0", [[-1, 2], [WSLOT // 16, 4], [1, 4]], 1, flag=True)
    iota(T.gr[:, 32:64], "gr1", [[-1, 2], [WSLOT // 16, 4], [1, 4]], 1 + WSLOT // 4, flag=True)
    iota(T.gr[:, 3:32:16], "gr0", [[-1, 2]], 1 + BACK, flag=True)
    iota(T.j0[:, :], "j0", [[16, 20]], 0)
    iota(T.bb[:, 0:8], "bb0", [[SLOT, 8]], 0, flag=True)

    fill(T.ones[:, :], 1.0, "ones")
    fill(T.z64[:, :], 0.0, "z64")
    fill(T.cs1[:, 0:8], 0.0, "cs1z")
    fill(T.cs2[:, 0:8], 0.0, "cs2z")
    fill(T.pp[:, 0:1], 0.0, "pp0")
    fill(T.zin[:, :], 0.0, "zin")
    fill(T.tz[:, :], 0.0, "tzz")
    fill(T.cs3[:, 0:12], 0.0, "cs3z")
    fill(T.bb[:, 15:16], float(SLOT * (N - 1) + FIRST), "bb15")
    fill(T.bb[:, 16:17], float(ZERO), "bb16")
    tr(T.ca[:, :], ra[:, :], ["ra0", "ra1", "ra2", "ra3"], ["ca"])
    zc, hc, pc, sc = [T.ca[:, 32 * j:32 * j + 1] for j in range(4)]
    ts(T.ec[:, :], T.e64[:, :], 7, None, AND, None, ["e64"], ["ec"])
    ts(T.l64[:, :], T.l4[:, :], pc, None, ADD, None, ["l4", "ca"], ["l64"])
    ts(T.meq[:, :], ra[:, 0:32], zc, None, EQ, None, ["ra0", "ca"], ["meq"])
    ts(T.mgt[:, :], ra[:, 32:64], hc, None, GT, None, ["ra1", "ca"], ["mgt"])
    ts(T.zpos[:, 0:1], zc, 0.0, None, GT, None, ["ca"], ["zpos"])
    ts(T.zfix[:, 0:1], zc, 0.0, 16.0 * BACK, EQ, MUL, ["ca"], ["zfix"])
    tt(T.mlt[:, :], T.meq[:, :], T.mgt[:, :], MUL, ["meq", "mgt"], ["mlt"])
    ts(T.meqn[:, :], ra[:, 0:32], zc, T.zpos[:, 0:1], EQ, MUL, ["ra0", "ca", "zpos"], ["meqn"])
    act(T.tb[:, 31:32], sc, ["ca"], ["tb0"])
    op("s", g.scalar.activation, (T.tb[:, 160:161], T.zfix[:, 0:1], IDENT, sc), ["zfix", "ca"], ["tb1"])

    l64 = T.l64[:, 0:4]
    c1w, c2w = T.ct[:, 0:16].indirect(l64), T.ct[:, 16:32].indirect(l64)
    m1, ma, mb, mc = [T.mt[:, 64 * i:64 * i + 64] for i in range(4)]
    tt(T.pre[:, 0:64], c1w, T.ec[:, :], EQ, ["c1", "l64", "ec"], ["pre0"])
    ts(T.pre[:, 64:128], c1w, float((me + 1) % N), None, EQ, None, ["c1", "l64"], ["pre1"])
    ts(T.pre[:, 128:192], c1w, float((me + 2) % N), None, EQ, None, ["c1", "l64"], ["pre2"])
    tt(T.pre[:, 192:256], c2w, T.ec[:, :], EQ, ["c2", "l64", "ec"], ["pre3"])
    tr(T.mt[:, :], T.pre[:, :], ["pre0", "pre1", "pre2", "pre3"], ["mt"])
    for i, m in enumerate((m1, ma, mb)):
        red(T.tcol[:, i:i + 1], m, ["mt"], ["tcol%d" % i])
    ts(T.bm[:, 0:32], T.mlt[:, :], T.tcol[:, 0:1], None, MUL, None, ["mlt", "tcol0"], ["bm0"])
    ts(T.bm[:, 32:64], T.mlt[:, :], T.tcol[:, 1:2], LATE / 32, MUL, ADD, ["mlt", "tcol1"], ["bm1"])
    ts(T.bm[:, 64:96], T.mlt[:, :], T.tcol[:, 2:3], LATE / 32, MUL, ADD, ["mlt", "tcol2"], ["bm2"])
    ts(T.bm[:, 96:128], T.meqn[:, :], T.tcol[:, 0:1], None, MUL, None, ["meqn", "tcol0"], ["bm3"])
    tr(T.tb[:, 32:160], T.bm[:, :], ["bm0", "bm1", "bm2", "bm3"], ["tb"])
    tr(T.cb[:, :], rb[:, :], ["rb0", "rb1"], ["cb"])
    tt(T.qa[:, :], ma, mc, MUL, ["mt"], ["qa"])
    bcol = T.bcol
    red(bcol[:, 1:2], T.tb[:, 64:96], ["tb"], ["ba"])
    red(bcol[:, 2:3], T.tb[:, 96:128], ["tb"], ["bq"])
    red(bcol[:, 0:1], T.tb[:, 31:64], ["tb", "tb0"], ["b1"])
    red(T.p2[:, 31:32], T.tb[:, 128:161], ["tb", "tb1"], ["p2k"])
    scan(T.sca[:, :], ma, 64, bcol[:, 1:2], ["mt", "ba"], ["sca"])
    scan(T.scb[:, :], mb, 64, bcol[:, 2:3], ["mt", "bq"], ["scb"])
    scan(T.sc1[:, :], m1, 64, bcol[:, 0:1], ["mt", "b1"], ["sc1"])
    tt(T.qb[:, :], mb, mc, MUL, ["mt"], ["qb"])
    tt(T.wa[:, :], T.qa[:, :], T.sca[:, :], MUL, ["qa", "sca"], ["wa"])
    tt(T.d1[:, :], m1, T.sc1[:, :], MUL, ["mt", "sc1"], ["d1"])
    tt(T.wb[:, :], T.qb[:, :], T.scb[:, :], MUL, ["qb", "scb"], ["wb"])
    tr(T.td1[:, :], T.d1[:, :], ["d1"], ["td1"])
    quant(T.xq[:, :], T.xs[:, :], T.xin[:, :], ["xin"], ["xq"])
    scan(T.cs1[:, 8:72], T.td1[:, :], 64, 0.0, ["td1"], ["cs1"])
    tr(T.gt[:, :], T.gr[:, :], ["gr0", "gr1"], ["gt"])
    tt(T.s1[:, :], T.cs1[:, 15:72:8], T.cs1[:, 7:64:8], SUB, ["cs1", "cs1z"], ["s1"])
    cp(T.gl[:, 0:4:2], T.gt[:, 0:64:32], ["gt"], ["gl"])

    for b in range(4):
        dma("ys"[b % 2], "dal", T.al[32 * b:32 * b + 32, 0:64], T.lists[:, :, :], ["lx", "l0"], ["al"], more=True)
    dma("y", "dw", T["win"][:, :], T.w[:, :], ["lx"], ["win"])
    op("s", g.scalar.activation, (T.vals[:, :], T.v128[:, :], IDENT, T.cb[:, 32:33]), ["v128", "cb"], ["vals"])
    half = (WIN + 32) // 2
    for i in range(2):
        act(T.scat[:, half * i:half * i + half], T.zin[:, 0:half], ["zin"], ["sz%d" % i])
    eqs, gcol = T.eqs, T.gcol
    for i in range(2):
        ts(eqs[:, 64 * i:64 * i + 64], T.al[:, :], float((me + 1 + i) % N), None, EQ, None, ["al"], ["eq%d" % i])
    for i in range(2):
        red(gcol[:, i:i + 1], eqs[:, 64 * i:64 * i + 64], ["eq%d" % i], ["gc%d" % i])
    for i in range(2):
        ts(T.bg[:, 32 * i:32 * i + 32], T.ones[:, :], gcol[:, i:i + 1], None, MUL, None, ["ones", "gc%d" % i], ["bg%d" % i])
    ts(eqs[:, 128:192], T.al[:, :], float(me), None, EQ, None, ["al"], ["eq2"])
    tr(T.tg[:, :], T.bg[:, :], ["bg0", "bg1"], ["tg"])
    for i in range(2):
        red(T.gs[:, i:i + 1], T.tg[:, 36 * i + 4:32 * i + 32], ["tg"], ["gs%d" % i])
    act(T.eqj[:, :], eqs[:, 128:192], ["eq2"], ["eqj", "gme"], accum_out=T.gme[:, 0:1])
    act(T.b3[:, :], T.ones[:, :], ["ones", "gme"], ["b3"], scale=T.gme[:, 0:1])

    lim = float(LATE + CAP + 1)
    ts(T.fa[:, :], T.wa[:, :], T.gs[:, 0:1], lim, ADD, GE, ["wa", "gs0"], ["fa"])
    ts(T.fb[:, :], T.wb[:, :], T.gs[:, 1:2], lim, ADD, GE, ["wb", "gs1"], ["fb"])
    scan2(T.cum[:, :], T.fa[:, :], T.fb[:, :], 0.0, ["fa", "fb"], ["cum"])
    act(T.bm2[:, 32:64], T.ones[:, :], ["ones", "cum"], ["bm5"], scale=T.cum[:, 63:64])
    tt(T.r2[:, :], T.fa[:, :], T.fb[:, :], ADD, ["fa", "fb"], ["r2"])
    ts(T.bm2[:, 0:32], T.mlt[:, :], T.cum[:, 63:64], None, MUL, None, ["mlt", "cum"], ["bm4"])
    tt(T.d2c[:, :], T.r2[:, :], T.cum[:, :], MUL, ["r2", "cum"], ["d2c"])
    tr(T.p2[:, 32:96], T.bm2[:, :], ["bm4", "bm5"], ["p2"])
    tr(T.tdc[:, :], T.d2c[:, :], ["d2c"], ["tdc"])
    red(bcol[:, 4:5], T.p2[:, 31:64], ["p2", "p2k"], ["b2c"])
    tt(T.m16[:, :], T.p2[:, 64:80], T.p2[:, 80:96], ADD, ["p2"], ["m16"])
    ts(T.d2b[:, :], T.r2[:, :], bcol[:, 4:5], None, MUL, None, ["r2", "b2c"], ["d2b"])
    tt(T.m8[:, :], T.m16[:, 0:8], T.m16[:, 8:16], ADD, ["m16"], ["m8"])
    for c in (0, 2, 4):
        send(calls[c][1], lambda z: T.m8[:, z:z + 1], lambda z: T.ml[:, place(z):place(z) + 1], calls[c][3], "mar", "mars", ["m8"])
    cnt["mar"] = count_in
    wr["mx"] = [("mar", count_in)]
    tr(T.tdb[:, :], T.d2b[:, :], ["d2b"], ["tdb"])
    tr(T.t3[:, :], T.b3[:, :], ["b3"], ["t3"])
    scan2(T.cs2[:, 8:72], T.tdc[:, :], T.tdb[:, :], 0.0, ["tdc", "tdb"], ["cs2"])
    tt(T.n16[:, :], T.t3[:, 0:32:2], T.t3[:, 1:32:2], ADD, ["t3"], ["n16"])
    tt(T.s2[:, :], T.cs2[:, 15:72:8], T.cs2[:, 7:64:8], SUB, ["cs2", "cs2z"], ["s2"])
    tt(T.n8[:, :], T.n16[:, 0:16:2], T.n16[:, 1:16:2], ADD, ["n16"], ["n8"])
    tt(T.s8[:, :], T.s1[:, :], T.s2[:, :], MAX, ["s1", "s2"], ["s8"])
    scan(T.n8s[:, :], T.n8[:, :], 8, 0.0, ["n8"], ["n8s"])
    cp(T.off[:, :], T.s8[:, :], ["s8"], ["off"])
    ts(T.ta[:, 0:180:9], T.j0[:, :], T.cb[:, 0:1], None, ADD, None, ["j0", "cb"], ["jj"])
    cp(T.scat[:, 32:32 + WIN].indirect(T.off[:, 0:8]), T.vals[:, :], ["off", "vals", "sz0", "sz1"], ["scat"])

    pp, bb, dd = T.pp, T.bb, T.dd
    tw, hh, so = T.tw, T.hh, T.so
    H = WIN // 2

    def turn(i, late):
        tr(tw[:, late * WIN + H * i:late * WIN + H * i + H], T.scat[:, 32 - 16 * late + H * i:32 - 16 * late + H * i + H],
           ["scat"], ["tw%d%d" % (late, i)])

    def join(i, late):
        a = late * WIN + H * i
        tt(hh[:, 20 * i + 1 - late:20 * i + 20:2], tw[:, a:a + H:32], tw[:, a + 16:a + H:32], ADD, ["tw%d%d" % (late, i)],
           ["hh%d%d" % (late, i)])

    def entries(i):
        cp(so[:, 16 * i:16 * i + 16], hh[:, 0:20 * i + 20].indirect(T.gl[:, 2 * i:2 * i + 1]),
           ["gl"] + ["hh%d%d" % (a, b) for a in range(2) for b in range(i + 1)], ["so%d" % i])

    def pick(oq, os_, n, iq, is_, m, off, n0, reads, writes):
        op("v", V.tensor_copy, (oq[:, n0:n0 + n].bitcast(dt.uint32), iq[:, 0:m].bitcast(dt.uint32).indirect(off)), reads, [writes + "q"])
        act(os_[:, n0:n0 + n], is_[:, 0:m].indirect(off), reads, [writes + "s"])

    def columns(call, sq, sp, key):
        kind, zs, n, engines = call

        def src(z):
            c = SLOT * (z - zs[0])
            return sq[:, c:c + n].bitcast(dt.uint8) if kind == "q" else sp[:, c:c + n]

        def dst(z):
            c = SLOT * place(z)
            return T.land[:, c:c + n].bitcast(dt.uint8) if kind == "q" else T.lsc[:, c:c + n]
        send(zs, src, dst, engines, "dat", "dats", [key + kind])

    def wave(i, lists):
        (sq, sp), zs, key = ((T.sq1, T.sp1), (T.sq2, T.sp2), (T.sq3, T.sp3))[i], calls[2 * i][1], "w%d" % i
        za, zb = zs[0], zs[-1] + 1
        pick(sq, sp, SLOT * (zb - za), T.xq, T.xs, TOK, so[:, 4 * za:4 * zb], 0, lists + ["xq"], key)
        columns(calls[2 * i], sq, sp, key)
        columns(calls[2 * i + 1], sq, sp, key)

    turn(0, 0)
    turn(0, 1)
    join(0, 0)
    join(0, 1)
    turn(1, 0)
    entries(0)
    turn(1, 1)
    wave(0, ["so0"])
    join(1, 0)
    join(1, 1)
    tt(bb[:, 8:15], bb[:, 0:7], T.n8[:, 0:7], ADD, ["bb0", "n8"], ["bb8"])
    entries(1)
    ts(pp[:, 1:9], T.n8s[:, :], float(CAP), None, MIN, None, ["n8s"], ["pp1"])
    wave(1, ["so0", "so1"])
    wave(2, ["so0", "so1"])
    pick(T.land, T.lsc, SLOT, T.xq, T.xs, TOK, so[:, 4 * own:4 * own + 4], 0, ["so1", "xq"], "own")

    tt(pp[:, 9:10], pp[:, 8:9], T.m8[:, own:own + 1], ADD, ["pp1", "m8"], ["pp9"])
    quant(T.land[:, ZERO:ZERO + NZ], T.lsc[:, ZERO:ZERO + NZ], T.zin[:, :], ["zin"], ["zq"])
    scan2(pp[:, 10:17], T.ml[:, 1:8], T.z64[:, 0:7], pp[:, 9:10], ["mx", "z64", "pp9"], ["pp10"])
    quant(T.wq[:, :], T.wsc[:, :], T["win"][:, :], ["win"], ["wq"])
    places = ["pp0", "pp1", "pp9", "pp10"]
    tt(T.de[:, 0:17], bb[:, 0:17], pp[:, 0:17], SUB, ["bb0", "bb8", "bb15", "bb16"] + places, ["de"])
    tt(dd[:, 1:17], T.de[:, 1:17], T.de[:, 0:16], SUB, ["de"], ["dd"])
    for q in range(1, 17):
        t, i = (T.ta, q) if q < 9 else (T.tz, q - 8)
        ts(t[:, i:180:9], T.ta[:, 0:180:9], pp[:, q:q + 1], dd[:, q:q + 1], GE, MUL, ["jj", "dd", "tzz"] + places, ["tm%d" % q])
    scan2(T.cs3[:, 12:192], T.ta[:, :], T.tz[:, :], 0.0, ["jj", "tzz"] + ["tm%d" % q for q in range(1, 17)], ["cs3"])
    tt(T.t20[:, :], T.cs3[:, 20:192:9], T.cs3[:, 11:183:9], SUB, ["cs3", "cs3z"], ["t20"])
    ts(T.fo[:, :], T.t20[:, :], float(ZERO + NZ - 1), None, MIN, None, ["t20"], ["fo"])

    cnt["dat"] = data_in
    wr["dx"] = [("dat", data_in)]
    got = ["dx", "ownq", "owns", "zq", "fo"]
    cut = 128
    for i, (a, b) in enumerate(((0, cut), (cut, ROOM))):
        pick(T.fq, T.fs, b - a, T.land, T.lsc, ZERO + NZ, T.fo[:, a // 16:b // 16], a, got, "f%d" % i)
    low, top = ["f0q", "f0s"], ["f1q", "f1s"]
    pieces = [(0, 0, cut, low), (1, 0, cut, low), (0, cut, ROOM, top), (1, cut, ROOM, top)]
    for o in range(2, O):
        pieces += [(o, 0, ROOM // 2, low + top), (o, ROOM // 2, ROOM, low + top)]
    for i, (o, a, b, keys) in enumerate(pieces):
        op("t", g.tensor.matmul_mx, (T.acc[:, 512 * i:512 * i + b - a], T.wq[:, 128 * o:128 * o + 128], T.wsc[:, 128 * o:128 * o + 128],
                                     T.fq[:, a:b], T.fs[:, a:b], True, True), ["wq"] + keys, ["acc%d" % i])
    for i, (o, a, b, keys) in enumerate(pieces):
        src, dst = T.acc[:, 512 * i:512 * i + b - a], T.yo[:, ROOM * o + a:ROOM * o + b]
        (cp if i in (0, 1, 3, 4, 6) else act)(dst, src, ["acc%d" % i], ["yo%d" % i])
        if o < 2:
            dma("y", "dy", T.y[:, ROOM * o + a:ROOM * o + b], dst, ["yo%d" % i], ["yout"], more=True)
        elif a > 0:
            dma("y", "dy", T.y[:, ROOM * o:ROOM * o + ROOM], T.yo[:, ROOM * o:ROOM * o + ROOM], ["yo%d" % (i - 1), "yo%d" % i],
                ["yout"], more=True)
    for sem in sorted(cnt):
        need("y", (sem, None))
